import numpy as np
import ml_dtypes


def mxq(x, axis, fmt="e4m3"):
    dtype, down = {"e4m3": (ml_dtypes.float8_e4m3fn, 7), "e5m2": (ml_dtypes.float8_e5m2, 14)}[fmt]
    v = np.moveaxis(np.asarray(x, np.float32).astype(ml_dtypes.bfloat16).astype(np.float64), axis, -1)
    blocks = v.reshape(v.shape[:-1] + (-1, 32))
    amax = np.abs(blocks).max(-1, keepdims=True)
    byte = np.maximum(np.where(amax > 0, np.frexp(amax)[1] - 1 + 127, 0) - down, 1)
    scale = np.exp2(byte - 127.0)
    codes = (blocks / scale).astype(np.float32).astype(dtype).astype(np.float64)
    return np.moveaxis((codes * scale).reshape(v.shape), -1, axis)


WIDE = False


def mx_kscale(k):
    if not WIDE:
        return np.ones(k)
    levels = np.array([10, -10, 5, -5, 0])
    if k % 512:
        return np.exp2(np.random.permutation(np.resize(levels, k // 32))).repeat(32)
    a = np.empty((k // 512, 16))
    for p in range(k // 512):
        a[p, :8] = np.random.permutation(np.resize(levels, 8))
        for g in range(8):
            far = levels[np.abs(levels - a[p, g]) >= 10]
            a[p, g + 8] = far[np.random.randint(len(far))]
    return np.exp2(a.ravel()).repeat(32)


def f64(x):
    return np.asarray(x).astype(np.float64)


def striped(idx):
    return np.tile(idx.reshape(-1, 16).T, (8, 1)).astype(np.uint16)


def unstriped(offs):
    return offs[:16].T.reshape(-1).astype(np.int64)


E2M1 = np.array([0.0, 0.5, 1.0, 1.5, 2.0, 3.0, 4.0, 6.0, -0.0, -0.5, -1.0, -1.5, -2.0, -3.0, -4.0, -6.0])


def pack_weight(w, fmt):
    k, n = w.shape
    w = f64(np.asarray(w, np.float32).astype(ml_dtypes.bfloat16)).reshape(k // 32, 32, n)
    amax = np.abs(w).max(1)
    if fmt == "e4m3":
        byte = np.frexp(amax)[1] - 1 + 127 - 7
    else:
        mant, ex = np.frexp(amax / 6.0)
        byte = np.where(mant > 0.5, ex, ex - 1) + 127
    byte = np.clip(np.where(amax > 0, byte, 1), 1, 254)
    scaled = (w * np.exp2(127.0 - byte)[:, None, :]).reshape(k, n).astype(np.float32)
    by_word = np.ascontiguousarray(scaled.reshape(k // 512, 128, 4, n).transpose(0, 1, 3, 2))
    if fmt == "e4m3":
        words = by_word.astype(ml_dtypes.float8_e4m3fn).view(np.uint8)
    else:
        c = by_word.astype(ml_dtypes.float4_e2m1fn).view(np.uint8) & 0xF
        words = (c[..., 0::2] | (c[..., 1::2] << 4)).reshape(k // 512, 128, 2 * n)
    return np.ascontiguousarray(words), np.ascontiguousarray(byte.astype(np.uint8).reshape(k // 512, 16, n))


def unpack_weight(words, scales, fmt):
    g, _, n = scales.shape
    words = np.ascontiguousarray(words).reshape(g, 128, n, -1)
    if fmt == "e4m3":
        vals = words.view(ml_dtypes.float8_e4m3fn).astype(np.float64)
    else:
        nib = np.empty((g, 128, n, 4), np.uint8)
        nib[..., 0::2] = words & 0xF
        nib[..., 1::2] = words >> 4
        vals = E2M1[nib]
    vals = vals * np.repeat(np.exp2(scales.astype(np.float64) - 127.0), 8, axis=1)[..., None]
    return vals.transpose(0, 1, 3, 2).reshape(g * 512, n)


def split(x):
    m, e = np.frexp(f64(x))
    hi = np.ldexp(np.trunc(16.0 * m) / 16.0, e)
    return hi, f64(x) - hi


def silu(v):
    return v / (1.0 + np.exp(-np.maximum(v, -700.0)))


K, M, T, S = 1536, 512, 2048, 1024


def setup_inputs():
    n = np.random.standard_normal
    s = mx_kscale(K)[:, None]
    v = pack_weight(n((K, T)) * s, "e4m3")
    return {
        "tab_words": v[0],
        "tab_scales": v[1],
        "w": (n((K, M)) / np.sqrt(K) / s).astype(np.float32),
        "rT": n((M, T)).astype(np.float32),
        "b": (0.3 * n(512)).astype(np.float32),
        "offs": striped(np.random.permutation(T)[:S]),
    }


def reference(tab_words, tab_scales, w, rT, b, offs):
    tab_ = unpack_weight(tab_words, tab_scales, "e4m3")[:, unstriped(offs)]
    w_hi, w_lo = split(w)
    w_hi_, w_lo_ = mxq(w_hi, 0, "e4m3"), mxq(w_lo, 0, "e4m3")
    y = w_hi_.T @ tab_ + w_lo_.T @ tab_
    return (silu(y + f64(b)[:, None])) + f64(rT)[:, unstriped(offs)]

@@ -1,0 +1,104 @@
+from contextlib import ExitStack
+
+import concourse.mybir as mybir
+
+K, M, T, S = 1536, 512, 2048, 1024
+FLOPS = 2 * 2 * K * M * S
+
+F32 = mybir.dt.float32
+BF16 = mybir.dt.bfloat16
+I32 = mybir.dt.int32
+U32 = mybir.dt.uint32
+U16 = mybir.dt.uint16
+U8 = mybir.dt.uint8
+FP8X4 = mybir.dt.float8_e4m3fn_x4
+ALU = mybir.AluOpType
+SILU = mybir.ActivationFunctionType.Silu
+
+P = 128
+PACK = 4
+PASSES = K // (P * PACK)
+TILES = M // P
+BANK = 512
+HALVES = S // BANK
+HI_MASK = 0xFFF0FFF0 - (1 << 32)
+
+
+def tile_list_tabres_silu_kernel(tc, tab_words, tab_scales, w, rT, b, offs, out):
+    nc = tc.nc
+    with ExitStack() as ctx:
+        keep = ctx.enter_context(tc.tile_pool(name="keep", bufs=1))
+        psum = ctx.enter_context(tc.psum_pool(name="psum", bufs=1))
+
+        offsets = keep.tile([P, S // 16], U16, name="offsets")
+        nc.sync.dma_start(offsets[:], offs)
+
+        planes = keep.tile([P, T // 4], I32, name="planes", align_bytes=64)
+        nc.vector.memset(planes[:], 0)
+        for q in range(4):
+            nc.scalar.dma_start(planes[32 * q : 32 * q + 4 * PASSES, :], tab_scales[:, 4 * q : 4 * q + 4, :].bitcast(I32))
+        bias = keep.tile([P, TILES], F32, name="bias")
+        with nc.allow_non_contiguous_dma(reason="one bias value for each partition"):
+            nc.scalar.dma_start(bias[:], b.rearrange("(c p) -> p c", p=P))
+
+        table, weight, resid = [], [], []
+        for a in range(PASSES):
+            tab = keep.tile([P, T], I32, name="table%d" % a, align_bytes=64)
+            nc.sync.dma_start(tab[:], tab_words[a].rearrange("p t i -> p (t i)").bitcast(I32))
+            table.append(tab)
+            wt = keep.tile([P, PACK * M], F32, name="weight%d" % a, align_bytes=64)
+            nc.sync.dma_start(wt[:], w[a * P * PACK : (a + 1) * P * PACK, :].rearrange("(p t) n -> p (t n)", t=PACK))
+            weight.append(wt)
+        for c in range(TILES):
+            rt = keep.tile([P, T], F32, name="resid%d" % c, align_bytes=64)
+            nc.sync.dma_start(rt[:], rT[c * P : (c + 1) * P, :])
+            resid.append(rt)
+
+        v_scales = keep.tile([P, S], U8, name="v_scales", align_bytes=64)
+        acc = [[psum.tile([P, BANK], F32, name="acc%d_%d" % (c, h)) for h in range(HALVES)] for c in range(TILES)]
+
+        for a in range(PASSES):
+            v_words = keep.tile([P, S], U32, name="v_words%d" % a, align_bytes=64)
+            nc.vector.tensor_copy(v_words[:], table[a][:].bitcast(U32).indirect(offsets[:]))
+            if a == 0:
+                nc.vector.tensor_copy(v_scales[:], planes[:].bitcast(U8).indirect(offsets[:]))
+
+            upper = keep.tile([P, PACK * M], BF16, name="upper%d" % a, align_bytes=64)
+            hi = keep.tile([P, PACK * M], BF16, name="hi%d" % a, align_bytes=64)
+            lo = keep.tile([P, PACK * M], BF16, name="lo%d" % a, align_bytes=64)
+            halves16 = weight[a][:].bitcast(BF16).rearrange("p (t c i h) -> p c t i h", t=PACK, i=2, h=2)
+            nc.scalar.copy(upper[:].rearrange("p (c i t) -> p c t i", i=2, t=PACK), halves16[:, :, :, :, 1])
+            nc.vector.tensor_scalar(hi[:].bitcast(I32), upper[:].bitcast(I32), HI_MASK, None, ALU.bitwise_and)
+            nc.vector.tensor_tensor(
+                lo[:].rearrange("p (c i t) -> p c t i", i=2, t=PACK),
+                weight[a][:].rearrange("p (t c i) -> p c t i", t=PACK, i=2),
+                hi[:].rearrange("p (c i t) -> p c t i", i=2, t=PACK),
+                ALU.subtract,
+            )
+            for part, src in enumerate((hi, lo)):
+                codes = keep.tile([P, M], U32, name="codes%d_%d" % (a, part), align_bytes=64)
+                scales = keep.tile([P, M], U8, name="scales%d_%d" % (a, part), align_bytes=64)
+                nc.vector.quantize_mx(out=codes[:].bitcast(FP8X4), scales=scales[:], in_=src[:])
+                for c in range(TILES):
+                    for h in range(HALVES):
+                        nc.tensor.matmul_mx(
+                            out=acc[c][h][:],
+                            lhsT=codes[:, c * P : (c + 1) * P].bitcast(FP8X4),
+                            lhsT_scale=scales[:, c * P : (c + 1) * P],
+                            rhs=v_words[:, h * BANK : (h + 1) * BANK].bitcast(FP8X4),
+                            rhs_scale=v_scales[4 * a : P, h * BANK : (h + 1) * BANK],
+                            start=(a == 0 and part == 0),
+                            stop=(a == PASSES - 1 and part == 1),
+                        )
+
+        for c in range(TILES):
+            act = keep.tile([P, S], F32, name="act%d" % c, align_bytes=64)
+            picked = keep.tile([P, S], F32, name="picked%d" % c, align_bytes=64)
+            res = keep.tile([P, S], F32, name="res%d" % c, align_bytes=64)
+            for h in range(HALVES):
+                nc.scalar.activation(act[:, h * BANK : (h + 1) * BANK], acc[c][h][:], SILU, bias=bias[:, c : c + 1])
+            nc.vector.tensor_copy(picked[:], resid[c][:].indirect(offsets[:]))
+            for h in range(HALVES):
+                cols = slice(h * BANK, (h + 1) * BANK)
+                nc.vector.tensor_tensor(res[:, cols], picked[:, cols], act[:, cols], ALU.add)
+                nc.sync.dma_start(out[c * P : (c + 1) * P, cols], res[:, cols])

@@ -1,6 +1,7 @@
 from contextlib import ExitStack
 
 import concourse.mybir as mybir
+from concourse.masks import make_identity
 
 K, M, T, S = 1536, 512, 2048, 1024
 FLOPS = 2 * 2 * K * M * S
@@ -35,70 +36,171 @@ def tile_list_tabres_silu_kernel(tc, tab_words, tab_scales, w, rT, b, offs, out)
 
         planes = keep.tile([P, T // 4], I32, name="planes", align_bytes=64)
         nc.vector.memset(planes[:], 0)
-        for q in range(4):
-            nc.scalar.dma_start(planes[32 * q : 32 * q + 4 * PASSES, :], tab_scales[:, 4 * q : 4 * q + 4, :].bitcast(I32))
         bias = keep.tile([P, TILES], F32, name="bias")
         with nc.allow_non_contiguous_dma(reason="one bias value for each partition"):
             nc.scalar.dma_start(bias[:], b.rearrange("(c p) -> p c", p=P))
 
-        table, weight, resid = [], [], []
-        for a in range(PASSES):
-            tab = keep.tile([P, T], I32, name="table%d" % a, align_bytes=64)
-            nc.sync.dma_start(tab[:], tab_words[a].rearrange("p t i -> p (t i)").bitcast(I32))
-            table.append(tab)
-            wt = keep.tile([P, PACK * M], F32, name="weight%d" % a, align_bytes=64)
-            nc.sync.dma_start(wt[:], w[a * P * PACK : (a + 1) * P * PACK, :].rearrange("(p t) n -> p (t n)", t=PACK))
-            weight.append(wt)
+        identity = keep.tile([P, P], F32, name="identity", align_bytes=64)
+        make_identity(nc, identity[:])
+
+        table, weight, resid = {}, {}, {}
+        WIDE = PACK * P
+
+        def load_table(a):
+            table[a] = keep.tile([P, T], I32, name="table%d" % a, align_bytes=64)
+            nc.sync.dma_start(table[a][:], tab_words[a].rearrange("p t i -> p (t i)").bitcast(I32))
+
+        def load_weight(a):
+            weight[a] = keep.tile([P, PACK, M], F32, name="weight%d" % a, align_bytes=64)
+            rows = w[a * P * PACK : (a + 1) * P * PACK, :]
+            nc.sync.dma_start(weight[a][:], rows.rearrange("(p t) n -> p t n", t=PACK))
+
+        def load_resid(c):
+            resid[c] = keep.tile([P, T], F32, name="resid%d" % c, align_bytes=64)
+            nc.sync.dma_start(resid[c][:], rT[c * P : (c + 1) * P, :])
+
+        load_table(0)
+        load_weight(0)
+        for q in range(4):
+            nc.sync.dma_start(planes[32 * q : 32 * q + 4 * PASSES, :], tab_scales[:, 4 * q : 4 * q + 4, :].bitcast(I32))
+        for a in range(1, PASSES):
+            load_table(a)
+            load_weight(a)
         for c in range(TILES):
-            rt = keep.tile([P, T], F32, name="resid%d" % c, align_bytes=64)
-            nc.sync.dma_start(rt[:], rT[c * P : (c + 1) * P, :])
-            resid.append(rt)
+            load_resid(c)
 
         v_scales = keep.tile([P, S], U8, name="v_scales", align_bytes=64)
         acc = [[psum.tile([P, BANK], F32, name="acc%d_%d" % (c, h)) for h in range(HALVES)] for c in range(TILES)]
+        v_words, parts, picked, act = {}, {}, {}, {}
 
-        for a in range(PASSES):
-            v_words = keep.tile([P, S], U32, name="v_words%d" % a, align_bytes=64)
-            nc.vector.tensor_copy(v_words[:], table[a][:].bitcast(U32).indirect(offsets[:]))
-            if a == 0:
-                nc.vector.tensor_copy(v_scales[:], planes[:].bitcast(U8).indirect(offsets[:]))
+        def gather_words(a):
+            v_words[a] = keep.tile([P, S], U32, name="v_words%d" % a, align_bytes=64)
+            nc.vector.tensor_copy(v_words[a][:], table[a][:].bitcast(U32).indirect(offsets[:]))
 
-            upper = keep.tile([P, PACK * M], BF16, name="upper%d" % a, align_bytes=64)
-            hi = keep.tile([P, PACK * M], BF16, name="hi%d" % a, align_bytes=64)
-            lo = keep.tile([P, PACK * M], BF16, name="lo%d" % a, align_bytes=64)
-            halves16 = weight[a][:].bitcast(BF16).rearrange("p (t c i h) -> p c t i h", t=PACK, i=2, h=2)
-            nc.scalar.copy(upper[:].rearrange("p (c i t) -> p c t i", i=2, t=PACK), halves16[:, :, :, :, 1])
-            nc.vector.tensor_scalar(hi[:].bitcast(I32), upper[:].bitcast(I32), HI_MASK, None, ALU.bitwise_and)
+        def gather_scales():
+            nc.vector.tensor_copy(v_scales[:], planes[:].bitcast(U8).indirect(offsets[:]))
+
+        def gather_resid(c):
+            tag = "shared%d" % c
+            picked[c] = keep.tile([P, S], F32, name="picked%d" % c, tag=tag, align_bytes=64)
+            nc.vector.tensor_copy(picked[c][:], resid[c][:].indirect(offsets[:]))
+
+        SHARED = {("parts", 2, 0): "shared0", ("parts", 1, 2): "shared1", ("upper", 2, 2): "shared2", ("parts", 2, 3): "shared3"}
+
+        def make_hi(a, tiles):
+            first, count = tiles[0], len(tiles)
+            names = {kind: "%s%d_%d" % (kind, a, first) for kind in ("upper", "parts")}
+            upper = keep.tile([P, count, WIDE], BF16, name=names["upper"], tag=SHARED.get(("upper", a, first), names["upper"]), align_bytes=64)
+            both = keep.tile([P, 2, count, WIDE], BF16, name=names["parts"], tag=SHARED.get(("parts", a, first), names["parts"]), align_bytes=64)
+            parts[a, first] = both
+            halves16 = weight[a][:].rearrange("p t n -> p (t n)").bitcast(BF16)
+            halves16 = halves16.rearrange("p (t c i h) -> p c t i h", t=PACK, i=2, h=2)
+            pairs = slice(first * P // 2, (first + count) * P // 2)
+            nc.scalar.copy(upper[:].rearrange("p m (c i t) -> p (m c) t i", i=2, t=PACK), halves16[:, pairs, :, :, 1])
+            nc.vector.tensor_scalar(both[:, 0, :, :].bitcast(I32), upper[:].bitcast(I32), HI_MASK, None, ALU.bitwise_and)
+
+        def make_lo(a, tiles):
+            both = parts[a, tiles[0]]
             nc.vector.tensor_tensor(
-                lo[:].rearrange("p (c i t) -> p c t i", i=2, t=PACK),
-                weight[a][:].rearrange("p (t c i) -> p c t i", t=PACK, i=2),
-                hi[:].rearrange("p (c i t) -> p c t i", i=2, t=PACK),
+                both[:, 1, :, :].rearrange("p m (c i t) -> p (m c) t i", i=2, t=PACK),
+                weight[a][:, :, tiles[0] * P : (tiles[-1] + 1) * P].rearrange("p t (c i) -> p c t i", i=2),
+                both[:, 0, :, :].rearrange("p m (c i t) -> p (m c) t i", i=2, t=PACK),
                 ALU.subtract,
             )
-            for part, src in enumerate((hi, lo)):
-                codes = keep.tile([P, M], U32, name="codes%d_%d" % (a, part), align_bytes=64)
-                scales = keep.tile([P, M], U8, name="scales%d_%d" % (a, part), align_bytes=64)
-                nc.vector.quantize_mx(out=codes[:].bitcast(FP8X4), scales=scales[:], in_=src[:])
-                for c in range(TILES):
-                    for h in range(HALVES):
+
+        def multiply(a, tiles, calls):
+            span = 2 * P * len(tiles)
+            codes = keep.tile([P, span], U32, name="codes%d_%d" % (a, tiles[0]), align_bytes=64)
+            scales = keep.tile([P, span], U8, name="scales%d_%d" % (a, tiles[0]), align_bytes=64)
+            source = parts[a, tiles[0]][:].rearrange("p s m x -> p (s m x)")
+            width = span // calls
+            for n in range(calls):
+                cols = slice(n * width, (n + 1) * width)
+                nc.vector.quantize_mx(
+                    out=codes[:, cols].bitcast(FP8X4),
+                    scales=scales[:, cols],
+                    in_=source[:, n * PACK * width : (n + 1) * PACK * width],
+                )
+            for m, c in enumerate(tiles):
+                for h in range(HALVES):
+                    for part in range(2):
+                        cols = slice((part * len(tiles) + m) * P, (part * len(tiles) + m + 1) * P)
                         nc.tensor.matmul_mx(
                             out=acc[c][h][:],
-                            lhsT=codes[:, c * P : (c + 1) * P].bitcast(FP8X4),
-                            lhsT_scale=scales[:, c * P : (c + 1) * P],
-                            rhs=v_words[:, h * BANK : (h + 1) * BANK].bitcast(FP8X4),
+                            lhsT=codes[:, cols].bitcast(FP8X4),
+                            lhsT_scale=scales[:, cols],
+                            rhs=v_words[a][:, h * BANK : (h + 1) * BANK].bitcast(FP8X4),
                             rhs_scale=v_scales[4 * a : P, h * BANK : (h + 1) * BANK],
                             start=(a == 0 and part == 0),
                             stop=(a == PASSES - 1 and part == 1),
                         )
 
-        for c in range(TILES):
-            act = keep.tile([P, S], F32, name="act%d" % c, align_bytes=64)
-            picked = keep.tile([P, S], F32, name="picked%d" % c, align_bytes=64)
-            res = keep.tile([P, S], F32, name="res%d" % c, align_bytes=64)
+        def activate(c):
+            act[c] = keep.tile([P, S], F32, name="act%d" % c, align_bytes=64)
             for h in range(HALVES):
-                nc.scalar.activation(act[:, h * BANK : (h + 1) * BANK], acc[c][h][:], SILU, bias=bias[:, c : c + 1])
-            nc.vector.tensor_copy(picked[:], resid[c][:].indirect(offsets[:]))
-            for h in range(HALVES):
-                cols = slice(h * BANK, (h + 1) * BANK)
-                nc.vector.tensor_tensor(res[:, cols], picked[:, cols], act[:, cols], ALU.add)
-                nc.sync.dma_start(out[c * P : (c + 1) * P, cols], res[:, cols])
+                nc.scalar.activation(act[c][:, h * BANK : (h + 1) * BANK], acc[c][h][:], SILU, bias=bias[:, c : c + 1])
+
+        def finish_vector(c, first, widths):
+            res = keep.tile([P, sum(widths)], F32, name="res%d_%d" % (c, first), align_bytes=64)
+            done = 0
+            for width in widths:
+                cols = slice(first + done, first + done + width)
+                nc.vector.tensor_tensor(res[:, done : done + width], picked[c][:, cols], act[c][:, cols], ALU.add)
+                nc.sync.dma_start(out[c * P : (c + 1) * P, cols], res[:, done : done + width])
+                done += width
+
+        def finish_tensor(c, halves):
+            flipped = keep.tile([P, halves * BANK], F32, name="flipped%d" % c, align_bytes=64)
+            res = keep.tile([P, halves * BANK], F32, name="res%d" % c, align_bytes=64)
+            for h in range(halves):
+                for g in range(BANK // P):
+                    cols = slice(h * BANK + g * P, h * BANK + (g + 1) * P)
+                    block = acc[c][h][:, g * P : (g + 1) * P]
+                    nc.tensor.matmul(block, act[c][:, cols], identity[:], start=True, stop=False, is_transpose=True)
+                    nc.tensor.matmul(block, picked[c][:, cols], identity[:], start=False, stop=True, is_transpose=True)
+                nc.scalar.copy(flipped[:, h * BANK : (h + 1) * BANK], acc[c][h][:])
+            for h in range(halves):
+                for g in range(BANK // P):
+                    cols = slice(h * BANK + g * P, h * BANK + (g + 1) * P)
+                    nc.tensor.transpose(acc[c][h][:, g * P : (g + 1) * P], flipped[:, cols], identity[:])
+                nc.scalar.copy(res[:, h * BANK : (h + 1) * BANK], acc[c][h][:])
+            nc.sync.dma_start(out[c * P : (c + 1) * P, : halves * BANK], res[:])
+
+        gather_words(0)
+        gather_scales()
+        make_hi(0, (0, 1))
+        make_hi(0, (2, 3))
+        make_lo(0, (0, 1))
+        make_lo(0, (2, 3))
+        multiply(0, (0, 1), 1)
+        gather_words(1)
+        multiply(0, (2, 3), 1)
+        make_hi(1, (0, 1))
+        gather_words(2)
+        make_lo(1, (0, 1))
+        make_hi(2, (0, 1))
+        multiply(1, (0, 1), 1)
+        make_lo(2, (0, 1))
+        make_hi(1, (2, 3))
+        multiply(2, (0, 1), 1)
+        activate(0)
+        activate(1)
+        make_lo(1, (2, 3))
+        gather_resid(0)
+        finish_tensor(0, 2)
+        multiply(1, (2, 3), 1)
+        make_hi(2, (2,))
+        gather_resid(1)
+        make_lo(2, (2,))
+        make_hi(2, (3,))
+        multiply(2, (2,), 1)
+        activate(2)
+        finish_tensor(1, 2)
+        gather_resid(2)
+        make_lo(2, (3,))
+        finish_vector(2, BANK, (BANK,))
+        multiply(2, (3,), 1)
+        activate(3)
+        finish_tensor(2, 1)
+        gather_resid(3)
+        finish_vector(3, 0, (512, 256, 256))

@@ -23,6 +23,9 @@ TILES = M // P
 BANK = 512
 HALVES = S // BANK
 HI_MASK = 0xFFF0FFF0 - (1 << 32)
+TOP_MASK = 0xFFF00000 - (1 << 32)
+SIGN_BIT = -(1 << 31)
+COPY = mybir.ActivationFunctionType.Copy
 
 
 def tile_list_tabres_silu_kernel(tc, tab_words, tab_scales, w, rT, b, offs, out):
@@ -50,22 +53,30 @@ def tile_list_tabres_silu_kernel(tc, tab_words, tab_scales, w, rT, b, offs, out)
             table[a] = keep.tile([P, T], I32, name="table%d" % a, align_bytes=64)
             nc.sync.dma_start(table[a][:], tab_words[a].rearrange("p t i -> p (t i)").bitcast(I32))
 
-        def load_weight(a):
-            weight[a] = keep.tile([P, PACK, M], F32, name="weight%d" % a, align_bytes=64)
-            rows = w[a * P * PACK : (a + 1) * P * PACK, :]
-            nc.sync.dma_start(weight[a][:], rows.rearrange("(p t) n -> p t n", t=PACK))
+        SHARED = {("parts", 2, 0): "shared0", ("parts", 2, 2): "shared1", ("parts", 1, 2): "shared2", ("weight", 2, 0): "shared3"}
+
+        def load_weight(a, tiles):
+            name = "weight%d_%d" % (a, tiles[0])
+            tag = SHARED.get(("weight", a, tiles[0]), name)
+            weight[a, tiles[0]] = keep.tile([P, PACK, len(tiles) * P], F32, name=name, tag=tag, align_bytes=64)
+            rows = w[a * P * PACK : (a + 1) * P * PACK, tiles[0] * P : (tiles[-1] + 1) * P]
+            nc.sync.dma_start(weight[a, tiles[0]][:], rows.rearrange("(p t) n -> p t n", t=PACK))
 
         def load_resid(c):
             resid[c] = keep.tile([P, T], F32, name="resid%d" % c, align_bytes=64)
             nc.sync.dma_start(resid[c][:], rT[c * P : (c + 1) * P, :])
 
         load_table(0)
-        load_weight(0)
+        load_weight(0, (0, 1))
         for q in range(4):
             nc.sync.dma_start(planes[32 * q : 32 * q + 4 * PASSES, :], tab_scales[:, 4 * q : 4 * q + 4, :].bitcast(I32))
-        for a in range(1, PASSES):
-            load_table(a)
-            load_weight(a)
+        load_weight(0, (2, 3))
+        load_weight(1, (0, 1))
+        load_table(1)
+        load_weight(1, (2, 3))
+        load_weight(2, (2, 3))
+        load_weight(2, (0, 1))
+        load_table(2)
         for c in range(TILES):
             load_resid(c)
 
@@ -85,25 +96,22 @@ def tile_list_tabres_silu_kernel(tc, tab_words, tab_scales, w, rT, b, offs, out)
             picked[c] = keep.tile([P, S], F32, name="picked%d" % c, tag=tag, align_bytes=64)
             nc.vector.tensor_copy(picked[c][:], resid[c][:].indirect(offsets[:]))
 
-        SHARED = {("parts", 2, 0): "shared0", ("parts", 1, 2): "shared1", ("upper", 2, 2): "shared2", ("parts", 2, 3): "shared3"}
-
         def make_hi(a, tiles):
             first, count = tiles[0], len(tiles)
             names = {kind: "%s%d_%d" % (kind, a, first) for kind in ("upper", "parts")}
             upper = keep.tile([P, count, WIDE], BF16, name=names["upper"], tag=SHARED.get(("upper", a, first), names["upper"]), align_bytes=64)
             both = keep.tile([P, 2, count, WIDE], BF16, name=names["parts"], tag=SHARED.get(("parts", a, first), names["parts"]), align_bytes=64)
             parts[a, first] = both
-            halves16 = weight[a][:].rearrange("p t n -> p (t n)").bitcast(BF16)
+            halves16 = weight[a, first][:].rearrange("p t n -> p (t n)").bitcast(BF16)
             halves16 = halves16.rearrange("p (t c i h) -> p c t i h", t=PACK, i=2, h=2)
-            pairs = slice(first * P // 2, (first + count) * P // 2)
-            nc.scalar.copy(upper[:].rearrange("p m (c i t) -> p (m c) t i", i=2, t=PACK), halves16[:, pairs, :, :, 1])
+            nc.scalar.copy(upper[:].rearrange("p m (c i t) -> p (m c) t i", i=2, t=PACK), halves16[:, :, :, :, 1])
             nc.vector.tensor_scalar(both[:, 0, :, :].bitcast(I32), upper[:].bitcast(I32), HI_MASK, None, ALU.bitwise_and)
 
         def make_lo(a, tiles):
             both = parts[a, tiles[0]]
             nc.vector.tensor_tensor(
                 both[:, 1, :, :].rearrange("p m (c i t) -> p (m c) t i", i=2, t=PACK),
-                weight[a][:, :, tiles[0] * P : (tiles[-1] + 1) * P].rearrange("p t (c i) -> p c t i", i=2),
+                weight[a, tiles[0]][:].rearrange("p t (c i) -> p c t i", i=2),
                 both[:, 0, :, :].rearrange("p m (c i t) -> p (m c) t i", i=2, t=PACK),
                 ALU.subtract,
             )
@@ -149,58 +157,70 @@ def tile_list_tabres_silu_kernel(tc, tab_words, tab_scales, w, rT, b, offs, out)
                 nc.sync.dma_start(out[c * P : (c + 1) * P, cols], res[:, done : done + width])
                 done += width
 
-        def finish_tensor(c, halves):
-            flipped = keep.tile([P, halves * BANK], F32, name="flipped%d" % c, align_bytes=64)
-            res = keep.tile([P, halves * BANK], F32, name="res%d" % c, align_bytes=64)
-            for h in range(halves):
-                for g in range(BANK // P):
-                    cols = slice(h * BANK + g * P, h * BANK + (g + 1) * P)
-                    block = acc[c][h][:, g * P : (g + 1) * P]
-                    nc.tensor.matmul(block, act[c][:, cols], identity[:], start=True, stop=False, is_transpose=True)
-                    nc.tensor.matmul(block, picked[c][:, cols], identity[:], start=False, stop=True, is_transpose=True)
-                nc.scalar.copy(flipped[:, h * BANK : (h + 1) * BANK], acc[c][h][:])
-            for h in range(halves):
-                for g in range(BANK // P):
-                    cols = slice(h * BANK + g * P, h * BANK + (g + 1) * P)
-                    nc.tensor.transpose(acc[c][h][:, g * P : (g + 1) * P], flipped[:, cols], identity[:])
-                nc.scalar.copy(res[:, h * BANK : (h + 1) * BANK], acc[c][h][:])
-            nc.sync.dma_start(out[c * P : (c + 1) * P, : halves * BANK], res[:])
+        def split_on_tensor(a, tiles):
+            first, count = tiles[0], len(tiles)
+            name = "parts%d_%d" % (a, first)
+            both = keep.tile([P, 2, count, WIDE], BF16, name=name, tag=SHARED.get(("parts", a, first), name), align_bytes=64)
+            parts[a, first] = both
+            src = weight[a, first]
+            minus_hi = keep.tile([P, PACK, count * P], F32, name="minus_hi%d" % a, align_bytes=64)
+            nc.vector.tensor_scalar(minus_hi[:].bitcast(I32), src[:].bitcast(I32), TOP_MASK, SIGN_BIT, ALU.bitwise_and, ALU.bitwise_xor)
+            nc.scalar.activation(
+                both[:, 0, :, :].rearrange("p m (c i t) -> p (m c) t i", i=2, t=PACK),
+                minus_hi[:].rearrange("p t (c i) -> p c t i", i=2),
+                COPY,
+                scale=-1.0,
+            )
+            turned = keep.tile([P, count, WIDE], BF16, name="turned%d" % a, align_bytes=64)
+            back = acc[3][a % 2]
+            for m in range(count):
+                cols = slice(m * P, (m + 1) * P)
+                for t in range(PACK):
+                    block = acc[2][m][:, t * P : (t + 1) * P]
+                    nc.tensor.matmul(block, src[:, t, cols], identity[:], start=True, stop=False, is_transpose=True)
+                    nc.tensor.matmul(block, minus_hi[:, t, cols], identity[:], start=False, stop=True, is_transpose=True)
+                nc.scalar.copy(
+                    turned[:, m, :].rearrange("n (u p e) -> n u p e", u=2, e=2),
+                    acc[2][m][:].rearrange("n (u e p) -> n u p e", u=2, e=2),
+                )
+            for m in range(count):
+                words = turned[:, m, :].bitcast(F32)
+                for u in range(2):
+                    nc.tensor.transpose(back[:, (2 * m + u) * P : (2 * m + u + 1) * P], words[:, u * P : (u + 1) * P], identity[:])
+            nc.scalar.copy(
+                both[:, 1, :, :].bitcast(F32).rearrange("p m (n u) -> p m n u", u=2),
+                back[:].rearrange("p (m u n) -> p m n u", m=count, u=2),
+            )
 
+        A, B = (0, 1), (2, 3)
         gather_words(0)
+        make_hi(0, A)
+        split_on_tensor(0, B)
+        make_lo(0, A)
         gather_scales()
-        make_hi(0, (0, 1))
-        make_hi(0, (2, 3))
-        make_lo(0, (0, 1))
-        make_lo(0, (2, 3))
-        multiply(0, (0, 1), 1)
+        multiply(0, A, 1)
+        make_hi(1, A)
+        split_on_tensor(1, B)
+        make_lo(1, A)
+        split_on_tensor(2, B)
         gather_words(1)
-        multiply(0, (2, 3), 1)
-        make_hi(1, (0, 1))
+        multiply(1, A, 1)
+        make_hi(2, A)
         gather_words(2)
-        make_lo(1, (0, 1))
-        make_hi(2, (0, 1))
-        multiply(1, (0, 1), 1)
-        make_lo(2, (0, 1))
-        make_hi(1, (2, 3))
-        multiply(2, (0, 1), 1)
+        make_lo(2, A)
+        multiply(0, B, 1)
+        multiply(2, A, 1)
         activate(0)
         activate(1)
-        make_lo(1, (2, 3))
+        multiply(1, B, 1)
         gather_resid(0)
-        finish_tensor(0, 2)
-        multiply(1, (2, 3), 1)
-        make_hi(2, (2,))
-        gather_resid(1)
-        make_lo(2, (2,))
-        make_hi(2, (3,))
-        multiply(2, (2,), 1)
+        multiply(2, B, 1)
         activate(2)
-        finish_tensor(1, 2)
-        gather_resid(2)
-        make_lo(2, (3,))
-        finish_vector(2, BANK, (BANK,))
-        multiply(2, (3,), 1)
         activate(3)
-        finish_tensor(2, 1)
+        gather_resid(1)
+        finish_vector(0, 0, (1024,))
+        gather_resid(2)
+        finish_vector(1, 0, (1024,))
         gather_resid(3)
+        finish_vector(2, 0, (512, 512))
         finish_vector(3, 0, (512, 256, 256))

@@ -39,12 +39,12 @@ def tile_list_tabres_silu_kernel(tc, tab_words, tab_scales, w, rT, b, offs, out)
 
         planes = keep.tile([P, T // 4], I32, name="planes", align_bytes=64)
         nc.vector.memset(planes[:], 0)
-        bias = keep.tile([P, TILES], F32, name="bias")
-        with nc.allow_non_contiguous_dma(reason="one bias value for each partition"):
-            nc.scalar.dma_start(bias[:], b.rearrange("(c p) -> p c", p=P))
 
         identity = keep.tile([P, P], F32, name="identity", align_bytes=64)
         make_identity(nc, identity[:])
+        bias_rows = keep.tile([P, P], F32, name="bias_rows", align_bytes=64)
+        nc.vector.memset(bias_rows[:], 0.0)
+        nc.scalar.dma_start(bias_rows[:TILES, :], b.rearrange("(c p) -> c p", p=P))
 
         table, weight, resid = {}, {}, {}
         WIDE = PACK * P
@@ -68,9 +68,9 @@ def tile_list_tabres_silu_kernel(tc, tab_words, tab_scales, w, rT, b, offs, out)
 
         load_table(0)
         load_weight(0, (0, 1))
+        load_weight(0, (2, 3))
         for q in range(4):
             nc.sync.dma_start(planes[32 * q : 32 * q + 4 * PASSES, :], tab_scales[:, 4 * q : 4 * q + 4, :].bitcast(I32))
-        load_weight(0, (2, 3))
         load_weight(1, (0, 1))
         load_table(1)
         load_weight(1, (2, 3))
@@ -82,6 +82,9 @@ def tile_list_tabres_silu_kernel(tc, tab_words, tab_scales, w, rT, b, offs, out)
 
         v_scales = keep.tile([P, S], U8, name="v_scales", align_bytes=64)
         acc = [[psum.tile([P, BANK], F32, name="acc%d_%d" % (c, h)) for h in range(HALVES)] for c in range(TILES)]
+        bias = keep.tile([P, TILES], F32, name="bias")
+        nc.tensor.transpose(acc[3][1][:, :P], bias_rows[:], identity[:])
+        nc.scalar.copy(bias[:], acc[3][1][:, :TILES])
         v_words, parts, picked, act = {}, {}, {}, {}
 
         def gather_words(a):

@@ -53,7 +53,7 @@ def tile_list_tabres_silu_kernel(tc, tab_words, tab_scales, w, rT, b, offs, out)
             table[a] = keep.tile([P, T], I32, name="table%d" % a, align_bytes=64)
             nc.sync.dma_start(table[a][:], tab_words[a].rearrange("p t i -> p (t i)").bitcast(I32))
 
-        SHARED = {("parts", 2, 0): "shared0", ("parts", 2, 2): "shared1", ("parts", 1, 2): "shared2", ("weight", 2, 0): "shared3"}
+        SHARED = {}
 
         def load_weight(a, tiles):
             name = "weight%d_%d" % (a, tiles[0])
@@ -156,7 +156,8 @@ def tile_list_tabres_silu_kernel(tc, tab_words, tab_scales, w, rT, b, offs, out)
             done = 0
             for width in widths:
                 cols = slice(first + done, first + done + width)
-                nc.vector.tensor_tensor(res[:, done : done + width], picked[c][:, cols], act[c][:, cols], ALU.add)
+                picks = offsets[:, (first + done) // 16 : (first + done + width) // 16]
+                nc.vector.tensor_tensor(res[:, done : done + width], resid[c][:].indirect(picks), act[c][:, cols], ALU.add)
                 nc.sync.dma_start(out[c * P : (c + 1) * P, cols], res[:, done : done + width])
                 done += width
 
@@ -216,14 +217,10 @@ def tile_list_tabres_silu_kernel(tc, tab_words, tab_scales, w, rT, b, offs, out)
         activate(0)
         activate(1)
         multiply(1, B, 1)
-        gather_resid(0)
         multiply(2, B, 1)
         activate(2)
         activate(3)
-        gather_resid(1)
         finish_vector(0, 0, (1024,))
-        gather_resid(2)
         finish_vector(1, 0, (1024,))
-        gather_resid(3)
         finish_vector(2, 0, (512, 512))
-        finish_vector(3, 0, (512, 256, 256))
+        finish_vector(3, 0, (512, 512))

@@ -15,6 +15,7 @@ U8 = mybir.dt.uint8
 FP8X4 = mybir.dt.float8_e4m3fn_x4
 ALU = mybir.AluOpType
 SILU = mybir.ActivationFunctionType.Silu
+COPY = mybir.ActivationFunctionType.Copy
 
 P = 128
 PACK = 4
@@ -25,7 +26,7 @@ HALVES = S // BANK
 HI_MASK = 0xFFF0FFF0 - (1 << 32)
 TOP_MASK = 0xFFF00000 - (1 << 32)
 SIGN_BIT = -(1 << 31)
-COPY = mybir.ActivationFunctionType.Copy
+RUN = 2
 
 
 def tile_list_tabres_silu_kernel(tc, tab_words, tab_scales, w, rT, b, offs, out):
@@ -47,18 +48,14 @@ def tile_list_tabres_silu_kernel(tc, tab_words, tab_scales, w, rT, b, offs, out)
         nc.scalar.dma_start(bias_rows[:TILES, :], b.rearrange("(c p) -> c p", p=P))
 
         table, weight, resid = {}, {}, {}
-        WIDE = PACK * P
 
         def load_table(a):
             table[a] = keep.tile([P, T], I32, name="table%d" % a, align_bytes=64)
             nc.sync.dma_start(table[a][:], tab_words[a].rearrange("p t i -> p (t i)").bitcast(I32))
 
-        SHARED = {}
-
         def load_weight(a, tiles):
             name = "weight%d_%d" % (a, tiles[0])
-            tag = SHARED.get(("weight", a, tiles[0]), name)
-            weight[a, tiles[0]] = keep.tile([P, PACK, len(tiles) * P], F32, name=name, tag=tag, align_bytes=64)
+            weight[a, tiles[0]] = keep.tile([P, PACK, len(tiles) * P], F32, name=name, align_bytes=64)
             rows = w[a * P * PACK : (a + 1) * P * PACK, tiles[0] * P : (tiles[-1] + 1) * P]
             nc.sync.dma_start(weight[a, tiles[0]][:], rows.rearrange("(p t) n -> p t n", t=PACK))
 
@@ -66,16 +63,18 @@ def tile_list_tabres_silu_kernel(tc, tab_words, tab_scales, w, rT, b, offs, out)
             resid[c] = keep.tile([P, T], F32, name="resid%d" % c, align_bytes=64)
             nc.sync.dma_start(resid[c][:], rT[c * P : (c + 1) * P, :])
 
+        def load_scales():
+            for q in range(4):
+                nc.sync.dma_start(planes[32 * q : 32 * q + 4 * PASSES, :], tab_scales[:, 4 * q : 4 * q + 4, :].bitcast(I32))
+
+        A, B, ALL = (0, 1), (2, 3), (0, 1, 2, 3)
+        load_weight(0, A)
         load_table(0)
-        load_weight(0, (0, 1))
-        load_weight(0, (2, 3))
-        for q in range(4):
-            nc.sync.dma_start(planes[32 * q : 32 * q + 4 * PASSES, :], tab_scales[:, 4 * q : 4 * q + 4, :].bitcast(I32))
-        load_weight(1, (0, 1))
+        load_weight(0, B)
+        load_scales()
+        load_weight(1, ALL)
         load_table(1)
-        load_weight(1, (2, 3))
-        load_weight(2, (2, 3))
-        load_weight(2, (0, 1))
+        load_weight(2, ALL)
         load_table(2)
         for c in range(TILES):
             load_resid(c)
@@ -85,7 +84,7 @@ def tile_list_tabres_silu_kernel(tc, tab_words, tab_scales, w, rT, b, offs, out)
         bias = keep.tile([P, TILES], F32, name="bias")
         nc.tensor.transpose(acc[3][1][:, :P], bias_rows[:], identity[:])
         nc.scalar.copy(bias[:], acc[3][1][:, :TILES])
-        v_words, parts, picked, act = {}, {}, {}, {}
+        v_words, parts, act, codes, scales = {}, {}, {}, {}, {}
 
         def gather_words(a):
             v_words[a] = keep.tile([P, S], U32, name="v_words%d" % a, align_bytes=64)
@@ -94,52 +93,47 @@ def tile_list_tabres_silu_kernel(tc, tab_words, tab_scales, w, rT, b, offs, out)
         def gather_scales():
             nc.vector.tensor_copy(v_scales[:], planes[:].bitcast(U8).indirect(offsets[:]))
 
-        def gather_resid(c):
-            tag = "shared%d" % c
-            picked[c] = keep.tile([P, S], F32, name="picked%d" % c, tag=tag, align_bytes=64)
-            nc.vector.tensor_copy(picked[c][:], resid[c][:].indirect(offsets[:]))
+        def source(a, tiles):
+            first = tiles[0] if (a, tiles[0]) in weight else 0
+            return weight[a, first][:, :, (tiles[0] - first) * P : (tiles[-1] + 1 - first) * P]
 
         def make_hi(a, tiles):
-            first, count = tiles[0], len(tiles)
-            names = {kind: "%s%d_%d" % (kind, a, first) for kind in ("upper", "parts")}
-            upper = keep.tile([P, count, WIDE], BF16, name=names["upper"], tag=SHARED.get(("upper", a, first), names["upper"]), align_bytes=64)
-            both = keep.tile([P, 2, count, WIDE], BF16, name=names["parts"], tag=SHARED.get(("parts", a, first), names["parts"]), align_bytes=64)
+            first, width = tiles[0], len(tiles) * P * PACK
+            upper = keep.tile([P, width], BF16, name="upper%d_%d" % (a, first), align_bytes=64)
+            both = keep.tile([P, 2, width], BF16, name="parts%d_%d" % (a, first), align_bytes=64)
             parts[a, first] = both
-            halves16 = weight[a, first][:].rearrange("p t n -> p (t n)").bitcast(BF16)
-            halves16 = halves16.rearrange("p (t c i h) -> p c t i h", t=PACK, i=2, h=2)
-            nc.scalar.copy(upper[:].rearrange("p m (c i t) -> p (m c) t i", i=2, t=PACK), halves16[:, :, :, :, 1])
-            nc.vector.tensor_scalar(both[:, 0, :, :].bitcast(I32), upper[:].bitcast(I32), HI_MASK, None, ALU.bitwise_and)
+            halves16 = source(a, tiles).bitcast(BF16).rearrange("p t (c i h) -> p c t i h", i=RUN, h=2)
+            nc.scalar.copy(upper[:].rearrange("p (c i t) -> p c t i", i=RUN, t=PACK), halves16[:, :, :, :, 1])
+            nc.vector.tensor_scalar(both[:, 0, :].bitcast(I32), upper[:].bitcast(I32), HI_MASK, None, ALU.bitwise_and)
 
         def make_lo(a, tiles):
             both = parts[a, tiles[0]]
             nc.vector.tensor_tensor(
-                both[:, 1, :, :].rearrange("p m (c i t) -> p (m c) t i", i=2, t=PACK),
-                weight[a, tiles[0]][:].rearrange("p t (c i) -> p c t i", i=2),
-                both[:, 0, :, :].rearrange("p m (c i t) -> p (m c) t i", i=2, t=PACK),
+                both[:, 1, :].rearrange("p (c i t) -> p c t i", i=RUN, t=PACK),
+                source(a, tiles).rearrange("p t (c i) -> p c t i", i=RUN),
+                both[:, 0, :].rearrange("p (c i t) -> p c t i", i=RUN, t=PACK),
                 ALU.subtract,
             )
 
-        def multiply(a, tiles, calls):
+        def quantise(a, tiles):
             span = 2 * P * len(tiles)
-            codes = keep.tile([P, span], U32, name="codes%d_%d" % (a, tiles[0]), align_bytes=64)
-            scales = keep.tile([P, span], U8, name="scales%d_%d" % (a, tiles[0]), align_bytes=64)
-            source = parts[a, tiles[0]][:].rearrange("p s m x -> p (s m x)")
-            width = span // calls
-            for n in range(calls):
-                cols = slice(n * width, (n + 1) * width)
-                nc.vector.quantize_mx(
-                    out=codes[:, cols].bitcast(FP8X4),
-                    scales=scales[:, cols],
-                    in_=source[:, n * PACK * width : (n + 1) * PACK * width],
-                )
+            codes[a, tiles[0]] = keep.tile([P, span], U32, name="codes%d_%d" % (a, tiles[0]), align_bytes=64)
+            scales[a, tiles[0]] = keep.tile([P, span], U8, name="scales%d_%d" % (a, tiles[0]), align_bytes=64)
+            nc.vector.quantize_mx(
+                out=codes[a, tiles[0]][:].bitcast(FP8X4),
+                scales=scales[a, tiles[0]][:],
+                in_=parts[a, tiles[0]][:].rearrange("p s x -> p (s x)"),
+            )
+
+        def multiply(a, tiles):
             for m, c in enumerate(tiles):
                 for h in range(HALVES):
                     for part in range(2):
                         cols = slice((part * len(tiles) + m) * P, (part * len(tiles) + m + 1) * P)
                         nc.tensor.matmul_mx(
                             out=acc[c][h][:],
-                            lhsT=codes[:, cols].bitcast(FP8X4),
-                            lhsT_scale=scales[:, cols],
+                            lhsT=codes[a, tiles[0]][:, cols].bitcast(FP8X4),
+                            lhsT_scale=scales[a, tiles[0]][:, cols],
                             rhs=v_words[a][:, h * BANK : (h + 1) * BANK].bitcast(FP8X4),
                             rhs_scale=v_scales[4 * a : P, h * BANK : (h + 1) * BANK],
                             start=(a == 0 and part == 0),
@@ -151,76 +145,45 @@ def tile_list_tabres_silu_kernel(tc, tab_words, tab_scales, w, rT, b, offs, out)
             for h in range(HALVES):
                 nc.scalar.activation(act[c][:, h * BANK : (h + 1) * BANK], acc[c][h][:], SILU, bias=bias[:, c : c + 1])
 
-        def finish_vector(c, first, widths):
-            res = keep.tile([P, sum(widths)], F32, name="res%d_%d" % (c, first), align_bytes=64)
+        def finish(c, widths):
+            res = keep.tile([P, S], F32, name="res%d" % c, align_bytes=64)
             done = 0
             for width in widths:
-                cols = slice(first + done, first + done + width)
-                picks = offsets[:, (first + done) // 16 : (first + done + width) // 16]
-                nc.vector.tensor_tensor(res[:, done : done + width], resid[c][:].indirect(picks), act[c][:, cols], ALU.add)
-                nc.sync.dma_start(out[c * P : (c + 1) * P, cols], res[:, done : done + width])
+                cols = slice(done, done + width)
+                picks = offsets[:, done // 16 : (done + width) // 16]
+                nc.vector.tensor_tensor(res[:, cols], resid[c][:].indirect(picks), act[c][:, cols], ALU.add)
+                nc.sync.dma_start(out[c * P : (c + 1) * P, cols], res[:, cols])
                 done += width
 
-        def split_on_tensor(a, tiles):
-            first, count = tiles[0], len(tiles)
-            name = "parts%d_%d" % (a, first)
-            both = keep.tile([P, 2, count, WIDE], BF16, name=name, tag=SHARED.get(("parts", a, first), name), align_bytes=64)
-            parts[a, first] = both
-            src = weight[a, first]
-            minus_hi = keep.tile([P, PACK, count * P], F32, name="minus_hi%d" % a, align_bytes=64)
-            nc.vector.tensor_scalar(minus_hi[:].bitcast(I32), src[:].bitcast(I32), TOP_MASK, SIGN_BIT, ALU.bitwise_and, ALU.bitwise_xor)
-            nc.scalar.activation(
-                both[:, 0, :, :].rearrange("p m (c i t) -> p (m c) t i", i=2, t=PACK),
-                minus_hi[:].rearrange("p t (c i) -> p c t i", i=2),
-                COPY,
-                scale=-1.0,
-            )
-            turned = keep.tile([P, count, WIDE], BF16, name="turned%d" % a, align_bytes=64)
-            back = acc[3][a % 2]
-            for m in range(count):
-                cols = slice(m * P, (m + 1) * P)
-                for t in range(PACK):
-                    block = acc[2][m][:, t * P : (t + 1) * P]
-                    nc.tensor.matmul(block, src[:, t, cols], identity[:], start=True, stop=False, is_transpose=True)
-                    nc.tensor.matmul(block, minus_hi[:, t, cols], identity[:], start=False, stop=True, is_transpose=True)
-                nc.scalar.copy(
-                    turned[:, m, :].rearrange("n (u p e) -> n u p e", u=2, e=2),
-                    acc[2][m][:].rearrange("n (u e p) -> n u p e", u=2, e=2),
-                )
-            for m in range(count):
-                words = turned[:, m, :].bitcast(F32)
-                for u in range(2):
-                    nc.tensor.transpose(back[:, (2 * m + u) * P : (2 * m + u + 1) * P], words[:, u * P : (u + 1) * P], identity[:])
-            nc.scalar.copy(
-                both[:, 1, :, :].bitcast(F32).rearrange("p m (n u) -> p m n u", u=2),
-                back[:].rearrange("p (m u n) -> p m n u", m=count, u=2),
-            )
-
-        A, B = (0, 1), (2, 3)
-        gather_words(0)
         make_hi(0, A)
-        split_on_tensor(0, B)
         make_lo(0, A)
+        gather_words(0)
+        make_hi(0, B)
+        quantise(0, A)
+        make_lo(0, B)
         gather_scales()
-        multiply(0, A, 1)
-        make_hi(1, A)
-        split_on_tensor(1, B)
-        make_lo(1, A)
-        split_on_tensor(2, B)
+        quantise(0, B)
+        multiply(0, A)
+        multiply(0, B)
+        make_hi(1, ALL)
         gather_words(1)
-        multiply(1, A, 1)
+        make_lo(1, ALL)
         make_hi(2, A)
-        gather_words(2)
+        quantise(1, ALL)
+        multiply(1, ALL)
         make_lo(2, A)
-        multiply(0, B, 1)
-        multiply(2, A, 1)
+        gather_words(2)
+        quantise(2, A)
+        multiply(2, A)
+        make_hi(2, B)
+        make_lo(2, B)
         activate(0)
         activate(1)
-        multiply(1, B, 1)
-        multiply(2, B, 1)
+        quantise(2, B)
+        multiply(2, B)
         activate(2)
         activate(3)
-        finish_vector(0, 0, (1024,))
-        finish_vector(1, 0, (1024,))
-        finish_vector(2, 0, (512, 512))
-        finish_vector(3, 0, (512, 512))
+        finish(0, (1024,))
+        finish(1, (1024,))
+        finish(2, (1024,))
+        finish(3, (512, 256, 256))

@@ -47,6 +47,9 @@ def tile_list_tabres_silu_kernel(tc, tab_words, tab_scales, w, rT, b, offs, out)
         nc.vector.memset(bias_rows[:], 0.0)
         nc.scalar.dma_start(bias_rows[:TILES, :], b.rearrange("(c p) -> c p", p=P))
 
+        warm = keep.tile([P, 1], F32, name="warm")
+        nc.scalar.activation(warm[:], identity[:, :1], SILU)
+
         table, weight, resid = {}, {}, {}
 
         def load_table(a):
@@ -68,7 +71,8 @@ def tile_list_tabres_silu_kernel(tc, tab_words, tab_scales, w, rT, b, offs, out)
                 nc.sync.dma_start(planes[32 * q : 32 * q + 4 * PASSES, :], tab_scales[:, 4 * q : 4 * q + 4, :].bitcast(I32))
 
         A, B, ALL = (0, 1), (2, 3), (0, 1, 2, 3)
-        load_weight(0, A)
+        load_weight(0, (0,))
+        load_weight(0, (1,))
         load_table(0)
         load_weight(0, B)
         load_scales()
@@ -155,19 +159,23 @@ def tile_list_tabres_silu_kernel(tc, tab_words, tab_scales, w, rT, b, offs, out)
                 nc.sync.dma_start(out[c * P : (c + 1) * P, cols], res[:, cols])
                 done += width
 
-        make_hi(0, A)
-        make_lo(0, A)
+        make_hi(0, (0,))
+        make_hi(0, (1,))
+        make_lo(0, (0,))
+        make_lo(0, (1,))
+        quantise(0, (0,))
+        quantise(0, (1,))
         gather_words(0)
         make_hi(0, B)
-        quantise(0, A)
-        make_lo(0, B)
         gather_scales()
-        quantise(0, B)
-        multiply(0, A)
-        multiply(0, B)
+        make_lo(0, B)
+        multiply(0, (0,))
+        multiply(0, (1,))
         make_hi(1, ALL)
-        gather_words(1)
+        quantise(0, B)
+        multiply(0, B)
         make_lo(1, ALL)
+        gather_words(1)
         make_hi(2, A)
         quantise(1, ALL)
         multiply(1, ALL)

@@ -26,7 +26,7 @@ HALVES = S // BANK
 HI_MASK = 0xFFF0FFF0 - (1 << 32)
 TOP_MASK = 0xFFF00000 - (1 << 32)
 SIGN_BIT = -(1 << 31)
-RUN = 2
+RUN = 4
 
 
 def tile_list_tabres_silu_kernel(tc, tab_words, tab_scales, w, rT, b, offs, out):

@@ -83,7 +83,6 @@ def tile_list_tabres_silu_kernel(tc, tab_words, tab_scales, w, rT, b, offs, out)
         for c in range(TILES):
             load_resid(c)
 
-        v_scales = keep.tile([P, S], U8, name="v_scales", align_bytes=64)
         acc = [[psum.tile([P, BANK], F32, name="acc%d_%d" % (c, h)) for h in range(HALVES)] for c in range(TILES)]
         bias = keep.tile([P, TILES], F32, name="bias")
         nc.tensor.transpose(acc[3][1][:, :P], bias_rows[:], identity[:])
@@ -91,10 +90,16 @@ def tile_list_tabres_silu_kernel(tc, tab_words, tab_scales, w, rT, b, offs, out)
         v_words, parts, act, codes, scales = {}, {}, {}, {}, {}
 
         def gather_words(a):
-            v_words[a] = keep.tile([P, S], U32, name="v_words%d" % a, align_bytes=64)
+            name = "v_words%d" % a
+            v_words[a] = keep.tile([P, S], U32, name=name, tag=SLOT.get(name, name), align_bytes=64)
             nc.vector.tensor_copy(v_words[a][:], table[a][:].bitcast(U32).indirect(offsets[:]))
 
+        SLOT = {"v_words2": "upper2_0", "v_scales": "upper0_2", "codes0_2": "planes", "codes2_0": "table2"}
+        held = {}
+
         def gather_scales():
+            v_scales = keep.tile([P, S], U8, name="v_scales", tag=SLOT["v_scales"], align_bytes=64)
+            held["scales"] = v_scales
             nc.vector.tensor_copy(v_scales[:], planes[:].bitcast(U8).indirect(offsets[:]))
 
         def source(a, tiles):
@@ -119,9 +124,19 @@ def tile_list_tabres_silu_kernel(tc, tab_words, tab_scales, w, rT, b, offs, out)
                 ALU.subtract,
             )
 
+        def make_lo_on_gpsimd(a, tiles):
+            both = parts[a, tiles[0]]
+            nc.gpsimd.tensor_tensor(
+                both[:, 1, :].rearrange("p (n t) -> p n t", t=PACK),
+                source(a, tiles).rearrange("p t n -> p n t"),
+                both[:, 0, :].rearrange("p (n t) -> p n t", t=PACK),
+                ALU.subtract,
+            )
+
         def quantise(a, tiles):
             span = 2 * P * len(tiles)
-            codes[a, tiles[0]] = keep.tile([P, span], U32, name="codes%d_%d" % (a, tiles[0]), align_bytes=64)
+            name = "codes%d_%d" % (a, tiles[0])
+            codes[a, tiles[0]] = keep.tile([P, span], U32, name=name, tag=SLOT.get(name, name), align_bytes=64)
             scales[a, tiles[0]] = keep.tile([P, span], U8, name="scales%d_%d" % (a, tiles[0]), align_bytes=64)
             nc.vector.quantize_mx(
                 out=codes[a, tiles[0]][:].bitcast(FP8X4),
@@ -139,7 +154,7 @@ def tile_list_tabres_silu_kernel(tc, tab_words, tab_scales, w, rT, b, offs, out)
                             lhsT=codes[a, tiles[0]][:, cols].bitcast(FP8X4),
                             lhsT_scale=scales[a, tiles[0]][:, cols],
                             rhs=v_words[a][:, h * BANK : (h + 1) * BANK].bitcast(FP8X4),
-                            rhs_scale=v_scales[4 * a : P, h * BANK : (h + 1) * BANK],
+                            rhs_scale=held["scales"][4 * a : P, h * BANK : (h + 1) * BANK],
                             start=(a == 0 and part == 0),
                             stop=(a == PASSES - 1 and part == 1),
                         )
@@ -168,7 +183,7 @@ def tile_list_tabres_silu_kernel(tc, tab_words, tab_scales, w, rT, b, offs, out)
         gather_words(0)
         make_hi(0, B)
         gather_scales()
-        make_lo(0, B)
+        make_lo_on_gpsimd(0, B)
         multiply(0, (0,))
         multiply(0, (1,))
         make_hi(1, ALL)
@@ -179,7 +194,7 @@ def tile_list_tabres_silu_kernel(tc, tab_words, tab_scales, w, rT, b, offs, out)
         make_hi(2, A)
         quantise(1, ALL)
         multiply(1, ALL)
-        make_lo(2, A)
+        make_lo_on_gpsimd(2, A)
         gather_words(2)
         quantise(2, A)
         multiply(2, A)

@@ -35,6 +35,31 @@ def tile_list_tabres_silu_kernel(tc, tab_words, tab_scales, w, rT, b, offs, out)
         keep = ctx.enter_context(tc.tile_pool(name="keep", bufs=1))
         psum = ctx.enter_context(tc.psum_pool(name="psum", bufs=1))
 
+        reuse = ctx.enter_context(tc.tile_pool(name="reuse", bufs=1))
+        TABLE_BYTES = 4 * T
+        PLACE = {
+            "table0": 0,
+            "codes0_1": 0,
+            "table1": TABLE_BYTES,
+            "parts1_2": TABLE_BYTES,
+            "table2": 2 * TABLE_BYTES,
+            "parts2_0": 2 * TABLE_BYTES,
+            "codes1_2": 2 * TABLE_BYTES + 4096,
+        }
+        SLOT = {
+            "v_words0": "upper0_1",
+            "v_scales": "upper0_2",
+            "parts1_0": "planes",
+            "v_words1": "upper1_0",
+            "v_words2": "upper1_2",
+            "parts2_2": "upper2_0",
+        }
+
+        def new_tile(shape, dtype, name):
+            if name in PLACE:
+                return reuse.tile(shape, dtype, name=name, align_bytes=64, offset=PLACE[name])
+            return keep.tile(shape, dtype, name=name, tag=SLOT.get(name, name), align_bytes=64)
+
         offsets = keep.tile([P, S // 16], U16, name="offsets")
         nc.sync.dma_start(offsets[:], offs)
 
@@ -45,7 +70,6 @@ def tile_list_tabres_silu_kernel(tc, tab_words, tab_scales, w, rT, b, offs, out)
         make_identity(nc, identity[:])
         bias_rows = keep.tile([P, P], F32, name="bias_rows", align_bytes=64)
         nc.vector.memset(bias_rows[:], 0.0)
-        nc.scalar.dma_start(bias_rows[:TILES, :], b.rearrange("(c p) -> c p", p=P))
 
         warm = keep.tile([P, 1], F32, name="warm")
         nc.scalar.activation(warm[:], identity[:, :1], SILU)
@@ -53,7 +77,7 @@ def tile_list_tabres_silu_kernel(tc, tab_words, tab_scales, w, rT, b, offs, out)
         table, weight, resid = {}, {}, {}
 
         def load_table(a):
-            table[a] = keep.tile([P, T], I32, name="table%d" % a, align_bytes=64)
+            table[a] = new_tile([P, T], I32, "table%d" % a)
             nc.sync.dma_start(table[a][:], tab_words[a].rearrange("p t i -> p (t i)").bitcast(I32))
 
         def load_weight(a, tiles):
@@ -76,6 +100,7 @@ def tile_list_tabres_silu_kernel(tc, tab_words, tab_scales, w, rT, b, offs, out)
         load_table(0)
         load_weight(0, B)
         load_scales()
+        nc.sync.dma_start(bias_rows[:TILES, :], b.rearrange("(c p) -> c p", p=P))
         load_weight(1, ALL)
         load_table(1)
         load_weight(2, ALL)
@@ -90,15 +115,13 @@ def tile_list_tabres_silu_kernel(tc, tab_words, tab_scales, w, rT, b, offs, out)
         v_words, parts, act, codes, scales = {}, {}, {}, {}, {}
 
         def gather_words(a):
-            name = "v_words%d" % a
-            v_words[a] = keep.tile([P, S], U32, name=name, tag=SLOT.get(name, name), align_bytes=64)
+            v_words[a] = new_tile([P, S], U32, "v_words%d" % a)
             nc.vector.tensor_copy(v_words[a][:], table[a][:].bitcast(U32).indirect(offsets[:]))
 
-        SLOT = {"v_words2": "upper2_0", "v_scales": "upper0_2", "codes0_2": "planes", "codes2_0": "table2"}
         held = {}
 
         def gather_scales():
-            v_scales = keep.tile([P, S], U8, name="v_scales", tag=SLOT["v_scales"], align_bytes=64)
+            v_scales = new_tile([P, S], U8, "v_scales")
             held["scales"] = v_scales
             nc.vector.tensor_copy(v_scales[:], planes[:].bitcast(U8).indirect(offsets[:]))
 
@@ -109,7 +132,7 @@ def tile_list_tabres_silu_kernel(tc, tab_words, tab_scales, w, rT, b, offs, out)
         def make_hi(a, tiles):
             first, width = tiles[0], len(tiles) * P * PACK
             upper = keep.tile([P, width], BF16, name="upper%d_%d" % (a, first), align_bytes=64)
-            both = keep.tile([P, 2, width], BF16, name="parts%d_%d" % (a, first), align_bytes=64)
+            both = new_tile([P, 2, width], BF16, "parts%d_%d" % (a, first))
             parts[a, first] = both
             halves16 = source(a, tiles).bitcast(BF16).rearrange("p t (c i h) -> p c t i h", i=RUN, h=2)
             nc.scalar.copy(upper[:].rearrange("p (c i t) -> p c t i", i=RUN, t=PACK), halves16[:, :, :, :, 1])
@@ -135,8 +158,7 @@ def tile_list_tabres_silu_kernel(tc, tab_words, tab_scales, w, rT, b, offs, out)
 
         def quantise(a, tiles):
             span = 2 * P * len(tiles)
-            name = "codes%d_%d" % (a, tiles[0])
-            codes[a, tiles[0]] = keep.tile([P, span], U32, name=name, tag=SLOT.get(name, name), align_bytes=64)
+            codes[a, tiles[0]] = new_tile([P, span], U32, "codes%d_%d" % (a, tiles[0]))
             scales[a, tiles[0]] = keep.tile([P, span], U8, name="scales%d_%d" % (a, tiles[0]), align_bytes=64)
             nc.vector.quantize_mx(
                 out=codes[a, tiles[0]][:].bitcast(FP8X4),
@@ -175,38 +197,42 @@ def tile_list_tabres_silu_kernel(tc, tab_words, tab_scales, w, rT, b, offs, out)
                 done += width
 
         make_hi(0, (0,))
-        make_hi(0, (1,))
         make_lo(0, (0,))
-        make_lo(0, (1,))
+        make_hi(0, (1,))
+        make_lo_on_gpsimd(0, (1,))
         quantise(0, (0,))
-        quantise(0, (1,))
         gather_words(0)
+        quantise(0, (1,))
         make_hi(0, B)
-        gather_scales()
         make_lo_on_gpsimd(0, B)
+        gather_scales()
         multiply(0, (0,))
         multiply(0, (1,))
-        make_hi(1, ALL)
+        make_hi(1, A)
+        make_lo_on_gpsimd(1, A)
         quantise(0, B)
         multiply(0, B)
-        make_lo(1, ALL)
         gather_words(1)
-        make_hi(2, A)
-        quantise(1, ALL)
-        multiply(1, ALL)
-        make_lo_on_gpsimd(2, A)
+        make_hi(1, B)
+        make_lo_on_gpsimd(1, B)
+        quantise(1, A)
+        multiply(1, A)
         gather_words(2)
+        make_hi(2, A)
+        quantise(1, B)
+        multiply(1, B)
+        make_lo(2, A)
+        make_hi(2, B)
         quantise(2, A)
         multiply(2, A)
-        make_hi(2, B)
-        make_lo(2, B)
         activate(0)
         activate(1)
+        make_lo(2, B)
         quantise(2, B)
         multiply(2, B)
         activate(2)
         activate(3)
-        finish(0, (1024,))
+        finish(0, (512, 512))
         finish(1, (1024,))
         finish(2, (1024,))
         finish(3, (512, 256, 256))

@@ -47,11 +47,8 @@ def tile_list_tabres_silu_kernel(tc, tab_words, tab_scales, w, rT, b, offs, out)
             "codes1_2": 2 * TABLE_BYTES + 4096,
         }
         SLOT = {
-            "v_words0": "upper0_1",
             "v_scales": "upper0_2",
             "parts1_0": "planes",
-            "v_words1": "upper1_0",
-            "v_words2": "upper1_2",
             "parts2_2": "upper2_0",
         }
 
@@ -156,6 +153,15 @@ def tile_list_tabres_silu_kernel(tc, tab_words, tab_scales, w, rT, b, offs, out)
                 ALU.subtract,
             )
 
+        def make_lo_woven(a, tiles):
+            both = parts[a, tiles[0]]
+            woven = keep.tile([P, len(tiles) * P * PACK], F32, name="woven%d_%d" % (a, tiles[0]), align_bytes=64)
+            nc.scalar.copy(
+                woven[:].rearrange("p (c i t) -> p c t i", i=RUN, t=PACK),
+                source(a, tiles).rearrange("p t (c i) -> p c t i", i=RUN),
+            )
+            nc.gpsimd.tensor_tensor(both[:, 1, :], woven[:], both[:, 0, :], ALU.subtract)
+
         def quantise(a, tiles):
             span = 2 * P * len(tiles)
             codes[a, tiles[0]] = new_tile([P, span], U32, "codes%d_%d" % (a, tiles[0]))
@@ -209,12 +215,12 @@ def tile_list_tabres_silu_kernel(tc, tab_words, tab_scales, w, rT, b, offs, out)
         multiply(0, (0,))
         multiply(0, (1,))
         make_hi(1, A)
-        make_lo_on_gpsimd(1, A)
+        make_lo_woven(1, A)
         quantise(0, B)
         multiply(0, B)
         gather_words(1)
         make_hi(1, B)
-        make_lo_on_gpsimd(1, B)
+        make_lo_woven(1, B)
         quantise(1, A)
         multiply(1, A)
         gather_words(2)

@@ -105,10 +105,11 @@ def tile_list_tabres_silu_kernel(tc, tab_words, tab_scales, w, rT, b, offs, out)
         for c in range(TILES):
             load_resid(c)
 
-        acc = [[psum.tile([P, BANK], F32, name="acc%d_%d" % (c, h)) for h in range(HALVES)] for c in range(TILES)]
+        acc = {}
         bias = keep.tile([P, TILES], F32, name="bias")
-        nc.tensor.transpose(acc[3][1][:, :P], bias_rows[:], identity[:])
-        nc.scalar.copy(bias[:], acc[3][1][:, :TILES])
+        turned_bias = psum.tile([P, BANK], F32, name="turned_bias")
+        nc.tensor.transpose(turned_bias[:, :P], bias_rows[:], identity[:])
+        nc.scalar.copy(bias[:], turned_bias[:, :TILES])
         v_words, parts, act, codes, scales = {}, {}, {}, {}, {}
 
         def gather_words(a):
@@ -172,13 +173,17 @@ def tile_list_tabres_silu_kernel(tc, tab_words, tab_scales, w, rT, b, offs, out)
                 in_=parts[a, tiles[0]][:].rearrange("p s x -> p (s x)"),
             )
 
-        def multiply(a, tiles):
+        def multiply(a, tiles, wanted):
             for m, c in enumerate(tiles):
+                if c not in wanted:
+                    continue
                 for h in range(HALVES):
+                    if a == 0:
+                        acc[c, h] = psum.tile([P, BANK], F32, name="acc%d_%d" % (c, h), tag="bank%d_%d" % (c % 3, h))
                     for part in range(2):
                         cols = slice((part * len(tiles) + m) * P, (part * len(tiles) + m + 1) * P)
                         nc.tensor.matmul_mx(
-                            out=acc[c][h][:],
+                            out=acc[c, h][:],
                             lhsT=codes[a, tiles[0]][:, cols].bitcast(FP8X4),
                             lhsT_scale=scales[a, tiles[0]][:, cols],
                             rhs=v_words[a][:, h * BANK : (h + 1) * BANK].bitcast(FP8X4),
@@ -190,7 +195,7 @@ def tile_list_tabres_silu_kernel(tc, tab_words, tab_scales, w, rT, b, offs, out)
         def activate(c):
             act[c] = keep.tile([P, S], F32, name="act%d" % c, align_bytes=64)
             for h in range(HALVES):
-                nc.scalar.activation(act[c][:, h * BANK : (h + 1) * BANK], acc[c][h][:], SILU, bias=bias[:, c : c + 1])
+                nc.scalar.activation(act[c][:, h * BANK : (h + 1) * BANK], acc[c, h][:], SILU, bias=bias[:, c : c + 1])
 
         def finish(c, widths):
             res = keep.tile([P, S], F32, name="res%d" % c, align_bytes=64)
@@ -212,31 +217,33 @@ def tile_list_tabres_silu_kernel(tc, tab_words, tab_scales, w, rT, b, offs, out)
         make_hi(0, B)
         make_lo_on_gpsimd(0, B)
         gather_scales()
-        multiply(0, (0,))
-        multiply(0, (1,))
+        multiply(0, (0,), ALL)
+        multiply(0, (1,), ALL)
         make_hi(1, A)
         make_lo_woven(1, A)
         quantise(0, B)
-        multiply(0, B)
+        multiply(0, B, (2,))
         gather_words(1)
         make_hi(1, B)
         make_lo_woven(1, B)
         quantise(1, A)
-        multiply(1, A)
+        multiply(1, A, ALL)
         gather_words(2)
         make_hi(2, A)
         quantise(1, B)
-        multiply(1, B)
+        multiply(1, B, (2,))
         make_lo(2, A)
         make_hi(2, B)
         quantise(2, A)
-        multiply(2, A)
+        multiply(2, A, ALL)
         activate(0)
         activate(1)
         make_lo(2, B)
         quantise(2, B)
-        multiply(2, B)
+        multiply(2, B, (2,))
         activate(2)
+        for a in range(PASSES):
+            multiply(a, B, (3,))
         activate(3)
         finish(0, (512, 512))
         finish(1, (1024,))

@@ -37,19 +37,22 @@ def tile_list_tabres_silu_kernel(tc, tab_words, tab_scales, w, rT, b, offs, out)
 
         reuse = ctx.enter_context(tc.tile_pool(name="reuse", bufs=1))
         TABLE_BYTES = 4 * T
+        PLANES = 3 * TABLE_BYTES + 3072
         PLACE = {
             "table0": 0,
-            "codes0_1": 0,
+            "parts1_2": 0,
+            "codes1_0": 4096,
             "table1": TABLE_BYTES,
-            "parts1_2": TABLE_BYTES,
+            "codes1_2": TABLE_BYTES,
             "table2": 2 * TABLE_BYTES,
-            "parts2_0": 2 * TABLE_BYTES,
-            "codes1_2": 2 * TABLE_BYTES + 4096,
+            "parts2_2": 2 * TABLE_BYTES,
+            "codes2_0": 2 * TABLE_BYTES + 4096,
+            "planes": PLANES,
+            "parts1_0": PLANES - 3072,
+            "codes0_2": PLANES + 1024,
         }
         SLOT = {
             "v_scales": "upper0_2",
-            "parts1_0": "planes",
-            "parts2_2": "upper2_0",
         }
 
         def new_tile(shape, dtype, name):
@@ -60,7 +63,7 @@ def tile_list_tabres_silu_kernel(tc, tab_words, tab_scales, w, rT, b, offs, out)
         offsets = keep.tile([P, S // 16], U16, name="offsets")
         nc.sync.dma_start(offsets[:], offs)
 
-        planes = keep.tile([P, T // 4], I32, name="planes", align_bytes=64)
+        planes = new_tile([P, T // 4], I32, "planes")
         nc.vector.memset(planes[:], 0)
 
         identity = keep.tile([P, P], F32, name="identity", align_bytes=64)
@@ -92,13 +95,12 @@ def tile_list_tabres_silu_kernel(tc, tab_words, tab_scales, w, rT, b, offs, out)
                 nc.sync.dma_start(planes[32 * q : 32 * q + 4 * PASSES, :], tab_scales[:, 4 * q : 4 * q + 4, :].bitcast(I32))
 
         A, B, ALL = (0, 1), (2, 3), (0, 1, 2, 3)
-        load_weight(0, (0,))
-        load_weight(0, (1,))
-        load_table(0)
+        load_weight(0, A)
         load_weight(0, B)
-        load_scales()
-        nc.sync.dma_start(bias_rows[:TILES, :], b.rearrange("(c p) -> c p", p=P))
         load_weight(1, ALL)
+        load_scales()
+        load_table(0)
+        nc.sync.dma_start(bias_rows[:TILES, :], b.rearrange("(c p) -> c p", p=P))
         load_table(1)
         load_weight(2, ALL)
         load_table(2)
@@ -124,7 +126,7 @@ def tile_list_tabres_silu_kernel(tc, tab_words, tab_scales, w, rT, b, offs, out)
             nc.vector.tensor_copy(v_scales[:], planes[:].bitcast(U8).indirect(offsets[:]))
 
         def source(a, tiles):
-            first = tiles[0] if (a, tiles[0]) in weight else 0
+            first = max(f for (n, f) in weight if n == a and f <= tiles[0])
             return weight[a, first][:, :, (tiles[0] - first) * P : (tiles[-1] + 1 - first) * P]
 
         def make_hi(a, tiles):
@@ -210,29 +212,29 @@ def tile_list_tabres_silu_kernel(tc, tab_words, tab_scales, w, rT, b, offs, out)
         make_hi(0, (0,))
         make_lo(0, (0,))
         make_hi(0, (1,))
-        make_lo_on_gpsimd(0, (1,))
         quantise(0, (0,))
-        gather_words(0)
-        quantise(0, (1,))
+        make_lo(0, (1,))
         make_hi(0, B)
         make_lo_on_gpsimd(0, B)
+        quantise(0, (1,))
         gather_scales()
-        multiply(0, (0,), ALL)
-        multiply(0, (1,), ALL)
         make_hi(1, A)
         make_lo_woven(1, A)
         quantise(0, B)
+        gather_words(0)
+        multiply(0, (0,), ALL)
+        multiply(0, (1,), ALL)
         multiply(0, B, (2,))
-        gather_words(1)
         make_hi(1, B)
         make_lo_woven(1, B)
         quantise(1, A)
+        gather_words(1)
         multiply(1, A, ALL)
-        gather_words(2)
         make_hi(2, A)
+        make_lo_woven(2, A)
         quantise(1, B)
         multiply(1, B, (2,))
-        make_lo(2, A)
+        gather_words(2)
         make_hi(2, B)
         quantise(2, A)
         multiply(2, A, ALL)

@@ -97,8 +97,8 @@ def tile_list_tabres_silu_kernel(tc, tab_words, tab_scales, w, rT, b, offs, out)
         A, B, ALL = (0, 1), (2, 3), (0, 1, 2, 3)
         load_weight(0, A)
         load_weight(0, B)
-        load_weight(1, ALL)
         load_scales()
+        load_weight(1, ALL)
         load_table(0)
         nc.sync.dma_start(bias_rows[:TILES, :], b.rearrange("(c p) -> c p", p=P))
         load_table(1)

@@ -27,6 +27,7 @@ HI_MASK = 0xFFF0FFF0 - (1 << 32)
 TOP_MASK = 0xFFF00000 - (1 << 32)
 SIGN_BIT = -(1 << 31)
 RUN = 4
+WIDE = PACK * P
 
 
 def tile_list_tabres_silu_kernel(tc, tab_words, tab_scales, w, rT, b, offs, out):
@@ -40,19 +41,22 @@ def tile_list_tabres_silu_kernel(tc, tab_words, tab_scales, w, rT, b, offs, out)
         PLANES = 3 * TABLE_BYTES + 3072
         PLACE = {
             "table0": 0,
-            "parts1_2": 0,
+            "parts2_0": 0,
             "codes1_0": 4096,
             "table1": TABLE_BYTES,
-            "codes1_2": TABLE_BYTES,
+            "parts2_2": TABLE_BYTES,
+            "codes2_0": TABLE_BYTES + 4096,
             "table2": 2 * TABLE_BYTES,
-            "parts2_2": 2 * TABLE_BYTES,
-            "codes2_0": 2 * TABLE_BYTES + 4096,
+            "codes2_2": 2 * TABLE_BYTES,
+            "codes1_2": 2 * TABLE_BYTES + 4096,
             "planes": PLANES,
-            "parts1_0": PLANES - 3072,
+            "minus_hi1": PLANES - 3072,
             "codes0_2": PLANES + 1024,
         }
         SLOT = {
             "v_scales": "upper0_2",
+            "parts1_0": "parts0_2",
+            "turned1_0": "upper2_0",
         }
 
         def new_tile(shape, dtype, name):
@@ -99,17 +103,17 @@ def tile_list_tabres_silu_kernel(tc, tab_words, tab_scales, w, rT, b, offs, out)
         load_weight(0, B)
         load_scales()
         load_weight(1, ALL)
-        load_table(0)
         nc.sync.dma_start(bias_rows[:TILES, :], b.rearrange("(c p) -> c p", p=P))
-        load_table(1)
+        load_table(0)
         load_weight(2, ALL)
+        load_table(1)
         load_table(2)
         for c in range(TILES):
             load_resid(c)
 
         acc = {}
         bias = keep.tile([P, TILES], F32, name="bias")
-        turned_bias = psum.tile([P, BANK], F32, name="turned_bias")
+        turned_bias = psum.tile([P, BANK], F32, name="turned_bias", tag="spare1")
         nc.tensor.transpose(turned_bias[:, :P], bias_rows[:], identity[:])
         nc.scalar.copy(bias[:], turned_bias[:, :TILES])
         v_words, parts, act, codes, scales = {}, {}, {}, {}, {}
@@ -165,6 +169,50 @@ def tile_list_tabres_silu_kernel(tc, tab_words, tab_scales, w, rT, b, offs, out)
             )
             nc.gpsimd.tensor_tensor(both[:, 1, :], woven[:], both[:, 0, :], ALU.subtract)
 
+        there = {}
+
+        def split_on_tensor(a, tiles):
+            first, count = tiles[0], len(tiles)
+            both = new_tile([P, 2, count * WIDE], BF16, "parts%d_%d" % (a, first))
+            parts[a, first] = both
+            src = source(a, tiles)
+            minus_hi = new_tile([P, PACK, count * P], F32, "minus_hi%d" % a)
+            nc.vector.tensor_scalar(minus_hi[:].bitcast(I32), src.bitcast(I32), TOP_MASK, SIGN_BIT, ALU.bitwise_and, ALU.bitwise_xor)
+            nc.scalar.activation(
+                both[:, 0, :].rearrange("p (c i t) -> p c t i", i=RUN, t=PACK),
+                minus_hi[:].rearrange("p t (c i) -> p c t i", i=RUN),
+                COPY,
+                scale=-1.0,
+            )
+            for m in range(count):
+                cols = slice(m * P, (m + 1) * P)
+                bank = psum.tile([P, BANK], F32, name="there%d_%d" % (a, m), tag="spare%d" % m)
+                there[m] = bank
+                for t in range(PACK):
+                    block = bank[:, t * P : (t + 1) * P]
+                    nc.tensor.matmul(block, src[:, t, cols], identity[:], start=True, stop=False, is_transpose=True)
+                    nc.tensor.matmul(block, minus_hi[:, t, cols], identity[:], start=False, stop=True, is_transpose=True)
+
+        def turn_back(a, tiles):
+            first, count = tiles[0], len(tiles)
+            both = parts[a, first]
+            turned = new_tile([P, count * WIDE], BF16, "turned%d_0" % a)
+            for m in range(count):
+                bank = there[m]
+                nc.scalar.copy(
+                    turned[:, m * WIDE : (m + 1) * WIDE].rearrange("n (u p e) -> n u p e", u=2, e=2),
+                    bank[:].rearrange("n (u e p) -> n u p e", u=2, e=2),
+                )
+            for m in range(count):
+                back = there[m]
+                words = turned[:, m * WIDE : (m + 1) * WIDE].bitcast(F32)
+                for u in range(2):
+                    nc.tensor.transpose(back[:, u * P : (u + 1) * P], words[:, u * P : (u + 1) * P], identity[:])
+                nc.scalar.copy(
+                    both[:, 1, m * WIDE : (m + 1) * WIDE].bitcast(F32).rearrange("p (n u) -> p n u", u=2),
+                    back[:, : 2 * P].rearrange("p (u n) -> p n u", u=2),
+                )
+
         def quantise(a, tiles):
             span = 2 * P * len(tiles)
             codes[a, tiles[0]] = new_tile([P, span], U32, "codes%d_%d" % (a, tiles[0]))
@@ -218,29 +266,29 @@ def tile_list_tabres_silu_kernel(tc, tab_words, tab_scales, w, rT, b, offs, out)
         make_lo_on_gpsimd(0, B)
         quantise(0, (1,))
         gather_scales()
-        make_hi(1, A)
-        make_lo_woven(1, A)
+        split_on_tensor(1, B)
         quantise(0, B)
+        make_hi(1, A)
+        make_lo_on_gpsimd(1, A)
         gather_words(0)
         multiply(0, (0,), ALL)
         multiply(0, (1,), ALL)
         multiply(0, B, (2,))
-        make_hi(1, B)
-        make_lo_woven(1, B)
+        make_hi(2, A)
+        make_lo_on_gpsimd(2, A)
+        turn_back(1, B)
         quantise(1, A)
         gather_words(1)
         multiply(1, A, ALL)
-        make_hi(2, A)
-        make_lo_woven(2, A)
-        quantise(1, B)
-        multiply(1, B, (2,))
-        gather_words(2)
         make_hi(2, B)
+        make_lo_on_gpsimd(2, B)
         quantise(2, A)
+        gather_words(2)
         multiply(2, A, ALL)
         activate(0)
         activate(1)
-        make_lo(2, B)
+        quantise(1, B)
+        multiply(1, B, (2,))
         quantise(2, B)
         multiply(2, B, (2,))
         activate(2)

@@ -269,19 +269,19 @@ def tile_list_tabres_silu_kernel(tc, tab_words, tab_scales, w, rT, b, offs, out)
         split_on_tensor(1, B)
         quantise(0, B)
         make_hi(1, A)
-        make_lo_on_gpsimd(1, A)
+        make_lo_woven(1, A)
         gather_words(0)
         multiply(0, (0,), ALL)
         multiply(0, (1,), ALL)
         multiply(0, B, (2,))
         make_hi(2, A)
-        make_lo_on_gpsimd(2, A)
+        make_lo_woven(2, A)
         turn_back(1, B)
         quantise(1, A)
         gather_words(1)
         multiply(1, A, ALL)
         make_hi(2, B)
-        make_lo_on_gpsimd(2, B)
+        make_lo_woven(2, B)
         quantise(2, A)
         gather_words(2)
         multiply(2, A, ALL)

@@ -56,7 +56,8 @@ def tile_list_tabres_silu_kernel(tc, tab_words, tab_scales, w, rT, b, offs, out)
         SLOT = {
             "v_scales": "upper0_2",
             "parts1_0": "parts0_2",
-            "turned1_0": "upper2_0",
+            "turned1": "upper2_0",
+            "parts1_2": "upper2_2",
         }
 
         def new_tile(shape, dtype, name):
@@ -118,9 +119,12 @@ def tile_list_tabres_silu_kernel(tc, tab_words, tab_scales, w, rT, b, offs, out)
         nc.scalar.copy(bias[:], turned_bias[:, :TILES])
         v_words, parts, act, codes, scales = {}, {}, {}, {}, {}
 
-        def gather_words(a):
+        def gather_words(a, pieces):
             v_words[a] = new_tile([P, S], U32, "v_words%d" % a)
-            nc.vector.tensor_copy(v_words[a][:], table[a][:].bitcast(U32).indirect(offsets[:]))
+            width = S // pieces
+            for n in range(pieces):
+                picks = offsets[:, n * width // 16 : (n + 1) * width // 16]
+                nc.vector.tensor_copy(v_words[a][:, n * width : (n + 1) * width], table[a][:].bitcast(U32).indirect(picks))
 
         held = {}
 
@@ -169,48 +173,48 @@ def tile_list_tabres_silu_kernel(tc, tab_words, tab_scales, w, rT, b, offs, out)
             )
             nc.gpsimd.tensor_tensor(both[:, 1, :], woven[:], both[:, 0, :], ALU.subtract)
 
-        there = {}
+        there, minus_hi = {}, {}
 
-        def split_on_tensor(a, tiles):
+        def subtract_on_tensor(a, tiles):
+            count = len(tiles)
+            src = source(a, tiles)
+            minus_hi[a] = new_tile([P, PACK, count * P], F32, "minus_hi%d" % a)
+            nc.vector.tensor_scalar(minus_hi[a][:].bitcast(I32), src.bitcast(I32), TOP_MASK, SIGN_BIT, ALU.bitwise_and, ALU.bitwise_xor)
+            for m in range(count):
+                cols = slice(m * P, (m + 1) * P)
+                there[m] = psum.tile([P, BANK], F32, name="there%d_%d" % (a, m), tag="spare%d" % m)
+                for t in range(PACK):
+                    block = there[m][:, t * P : (t + 1) * P]
+                    nc.tensor.matmul(block, src[:, t, cols], identity[:], start=True, stop=False, is_transpose=True)
+                    nc.tensor.matmul(block, minus_hi[a][:, t, cols], identity[:], start=False, stop=True, is_transpose=True)
+
+        def turn_back(a, tiles):
+            count = len(tiles)
+            turned = new_tile([P, count * WIDE], BF16, "turned%d" % a)
+            for m in range(count):
+                nc.scalar.copy(
+                    turned[:, m * WIDE : (m + 1) * WIDE].rearrange("n (u p e) -> n u p e", u=2, e=2),
+                    there[m][:].rearrange("n (u e p) -> n u p e", u=2, e=2),
+                )
+            for m in range(count):
+                words = turned[:, m * WIDE : (m + 1) * WIDE].bitcast(F32)
+                for u in range(2):
+                    nc.tensor.transpose(there[m][:, u * P : (u + 1) * P], words[:, u * P : (u + 1) * P], identity[:])
+
+        def collect_parts(a, tiles):
             first, count = tiles[0], len(tiles)
             both = new_tile([P, 2, count * WIDE], BF16, "parts%d_%d" % (a, first))
             parts[a, first] = both
-            src = source(a, tiles)
-            minus_hi = new_tile([P, PACK, count * P], F32, "minus_hi%d" % a)
-            nc.vector.tensor_scalar(minus_hi[:].bitcast(I32), src.bitcast(I32), TOP_MASK, SIGN_BIT, ALU.bitwise_and, ALU.bitwise_xor)
             nc.scalar.activation(
                 both[:, 0, :].rearrange("p (c i t) -> p c t i", i=RUN, t=PACK),
-                minus_hi[:].rearrange("p t (c i) -> p c t i", i=RUN),
+                minus_hi[a][:].rearrange("p t (c i) -> p c t i", i=RUN),
                 COPY,
                 scale=-1.0,
             )
             for m in range(count):
-                cols = slice(m * P, (m + 1) * P)
-                bank = psum.tile([P, BANK], F32, name="there%d_%d" % (a, m), tag="spare%d" % m)
-                there[m] = bank
-                for t in range(PACK):
-                    block = bank[:, t * P : (t + 1) * P]
-                    nc.tensor.matmul(block, src[:, t, cols], identity[:], start=True, stop=False, is_transpose=True)
-                    nc.tensor.matmul(block, minus_hi[:, t, cols], identity[:], start=False, stop=True, is_transpose=True)
-
-        def turn_back(a, tiles):
-            first, count = tiles[0], len(tiles)
-            both = parts[a, first]
-            turned = new_tile([P, count * WIDE], BF16, "turned%d_0" % a)
-            for m in range(count):
-                bank = there[m]
-                nc.scalar.copy(
-                    turned[:, m * WIDE : (m + 1) * WIDE].rearrange("n (u p e) -> n u p e", u=2, e=2),
-                    bank[:].rearrange("n (u e p) -> n u p e", u=2, e=2),
-                )
-            for m in range(count):
-                back = there[m]
-                words = turned[:, m * WIDE : (m + 1) * WIDE].bitcast(F32)
-                for u in range(2):
-                    nc.tensor.transpose(back[:, u * P : (u + 1) * P], words[:, u * P : (u + 1) * P], identity[:])
                 nc.scalar.copy(
                     both[:, 1, m * WIDE : (m + 1) * WIDE].bitcast(F32).rearrange("p (n u) -> p n u", u=2),
-                    back[:, : 2 * P].rearrange("p (u n) -> p n u", u=2),
+                    there[m][:, : 2 * P].rearrange("p (u n) -> p n u", u=2),
                 )
 
         def quantise(a, tiles):
@@ -223,11 +227,11 @@ def tile_list_tabres_silu_kernel(tc, tab_words, tab_scales, w, rT, b, offs, out)
                 in_=parts[a, tiles[0]][:].rearrange("p s x -> p (s x)"),
             )
 
-        def multiply(a, tiles, wanted):
-            for m, c in enumerate(tiles):
-                if c not in wanted:
-                    continue
-                for h in range(HALVES):
+        def multiply(a, tiles, wanted, halves=(0, 1)):
+            for h in halves:
+                for m, c in enumerate(tiles):
+                    if c not in wanted:
+                        continue
                     if a == 0:
                         acc[c, h] = psum.tile([P, BANK], F32, name="acc%d_%d" % (c, h), tag="bank%d_%d" % (c % 3, h))
                     for part in range(2):
@@ -266,30 +270,32 @@ def tile_list_tabres_silu_kernel(tc, tab_words, tab_scales, w, rT, b, offs, out)
         make_lo_on_gpsimd(0, B)
         quantise(0, (1,))
         gather_scales()
-        split_on_tensor(1, B)
+        subtract_on_tensor(1, B)
         quantise(0, B)
         make_hi(1, A)
         make_lo_woven(1, A)
-        gather_words(0)
-        multiply(0, (0,), ALL)
-        multiply(0, (1,), ALL)
-        multiply(0, B, (2,))
+        gather_words(0, 2)
+        for h in range(HALVES):
+            multiply(0, (0,), ALL, (h,))
+            multiply(0, (1,), ALL, (h,))
+            multiply(0, B, (2,), (h,))
         make_hi(2, A)
         make_lo_woven(2, A)
         turn_back(1, B)
         quantise(1, A)
-        gather_words(1)
+        gather_words(1, 1)
         multiply(1, A, ALL)
         make_hi(2, B)
         make_lo_woven(2, B)
+        collect_parts(1, B)
         quantise(2, A)
-        gather_words(2)
+        gather_words(2, 2)
         multiply(2, A, ALL)
         activate(0)
         activate(1)
+        quantise(2, B)
         quantise(1, B)
         multiply(1, B, (2,))
-        quantise(2, B)
         multiply(2, B, (2,))
         activate(2)
         for a in range(PASSES):

@@ -26,7 +26,7 @@ HALVES = S // BANK
 HI_MASK = 0xFFF0FFF0 - (1 << 32)
 TOP_MASK = 0xFFF00000 - (1 << 32)
 SIGN_BIT = -(1 << 31)
-RUN = 4
+RUN = 2
 WIDE = PACK * P
 
 
@@ -168,8 +168,8 @@ def tile_list_tabres_silu_kernel(tc, tab_words, tab_scales, w, rT, b, offs, out)
             both = parts[a, tiles[0]]
             woven = keep.tile([P, len(tiles) * P * PACK], F32, name="woven%d_%d" % (a, tiles[0]), align_bytes=64)
             nc.scalar.copy(
-                woven[:].rearrange("p (c i t) -> p c t i", i=RUN, t=PACK),
-                source(a, tiles).rearrange("p t (c i) -> p c t i", i=RUN),
+                woven[:].rearrange("p (n t) -> p n t", t=PACK),
+                source(a, tiles).rearrange("p t n -> p n t"),
             )
             nc.gpsimd.tensor_tensor(both[:, 1, :], woven[:], both[:, 0, :], ALU.subtract)
 

@@ -233,7 +233,7 @@ def tile_list_tabres_silu_kernel(tc, tab_words, tab_scales, w, rT, b, offs, out)
                     if c not in wanted:
                         continue
                     if a == 0:
-                        acc[c, h] = psum.tile([P, BANK], F32, name="acc%d_%d" % (c, h), tag="bank%d_%d" % (c % 3, h))
+                        acc[c, h] = psum.tile([P, BANK], F32, name="acc%d_%d" % (c, h), tag="bank%d_%d" % (c % 2, h))
                     for part in range(2):
                         cols = slice((part * len(tiles) + m) * P, (part * len(tiles) + m + 1) * P)
                         nc.tensor.matmul_mx(
@@ -278,9 +278,8 @@ def tile_list_tabres_silu_kernel(tc, tab_words, tab_scales, w, rT, b, offs, out)
         for h in range(HALVES):
             multiply(0, (0,), ALL, (h,))
             multiply(0, (1,), ALL, (h,))
-            multiply(0, B, (2,), (h,))
         make_hi(2, A)
-        make_lo_woven(2, A)
+        make_lo_on_gpsimd(2, A)
         turn_back(1, B)
         quantise(1, A)
         gather_words(1, 1)
@@ -295,12 +294,11 @@ def tile_list_tabres_silu_kernel(tc, tab_words, tab_scales, w, rT, b, offs, out)
         activate(1)
         quantise(2, B)
         quantise(1, B)
-        multiply(1, B, (2,))
-        multiply(2, B, (2,))
-        activate(2)
-        for a in range(PASSES):
-            multiply(a, B, (3,))
-        activate(3)
+        for c in B:
+            for h in range(HALVES):
+                for a in range(PASSES):
+                    multiply(a, B, (c,), (h,))
+            activate(c)
         finish(0, (512, 512))
         finish(1, (1024,))
         finish(2, (1024,))

@@ -66,7 +66,6 @@ def tile_list_tabres_silu_kernel(tc, tab_words, tab_scales, w, rT, b, offs, out)
             return keep.tile(shape, dtype, name=name, tag=SLOT.get(name, name), align_bytes=64)
 
         offsets = keep.tile([P, S // 16], U16, name="offsets")
-        nc.sync.dma_start(offsets[:], offs)
 
         planes = new_tile([P, T // 4], I32, "planes")
         nc.vector.memset(planes[:], 0)
@@ -102,6 +101,7 @@ def tile_list_tabres_silu_kernel(tc, tab_words, tab_scales, w, rT, b, offs, out)
         A, B, ALL = (0, 1), (2, 3), (0, 1, 2, 3)
         load_weight(0, A)
         load_weight(0, B)
+        nc.sync.dma_start(offsets[:], offs)
         load_scales()
         load_weight(1, ALL)
         nc.sync.dma_start(bias_rows[:TILES, :], b.rearrange("(c p) -> c p", p=P))
@@ -145,6 +145,23 @@ def tile_list_tabres_silu_kernel(tc, tab_words, tab_scales, w, rT, b, offs, out)
             halves16 = source(a, tiles).bitcast(BF16).rearrange("p t (c i h) -> p c t i h", i=RUN, h=2)
             nc.scalar.copy(upper[:].rearrange("p (c i t) -> p c t i", i=RUN, t=PACK), halves16[:, :, :, :, 1])
             nc.vector.tensor_scalar(both[:, 0, :].bitcast(I32), upper[:].bitcast(I32), HI_MASK, None, ALU.bitwise_and)
+
+        def split_on_vector(a, tiles):
+            first, width = tiles[0], len(tiles) * WIDE
+            both = new_tile([P, 2, width], BF16, "parts%d_%d" % (a, first))
+            parts[a, first] = both
+            top = keep.tile([P, PACK, len(tiles) * P], F32, name="top%d_%d" % (a, first), align_bytes=64)
+            nc.vector.tensor_scalar(top[:].bitcast(I32), source(a, tiles).bitcast(I32), TOP_MASK, None, ALU.bitwise_and)
+            nc.vector.tensor_tensor(
+                both[:, 1, :].rearrange("p (c i t) -> p c t i", i=RUN, t=PACK),
+                source(a, tiles).rearrange("p t (c i) -> p c t i", i=RUN),
+                top[:].rearrange("p t (c i) -> p c t i", i=RUN),
+                ALU.subtract,
+            )
+            nc.vector.tensor_copy(
+                both[:, 0, :].rearrange("p (c i t) -> p c t i", i=RUN, t=PACK),
+                top[:].rearrange("p t (c i) -> p c t i", i=RUN),
+            )
 
         def make_lo(a, tiles):
             both = parts[a, tiles[0]]
@@ -261,20 +278,19 @@ def tile_list_tabres_silu_kernel(tc, tab_words, tab_scales, w, rT, b, offs, out)
                 nc.sync.dma_start(out[c * P : (c + 1) * P, cols], res[:, cols])
                 done += width
 
-        make_hi(0, (0,))
-        make_lo(0, (0,))
+        split_on_vector(0, (0,))
         make_hi(0, (1,))
-        quantise(0, (0,))
         make_lo(0, (1,))
+        quantise(0, (0,))
+        quantise(0, (1,))
         make_hi(0, B)
         make_lo_on_gpsimd(0, B)
-        quantise(0, (1,))
         gather_scales()
         subtract_on_tensor(1, B)
         quantise(0, B)
         make_hi(1, A)
         make_lo_woven(1, A)
-        gather_words(0, 2)
+        gather_words(0, 1)
         for h in range(HALVES):
             multiply(0, (0,), ALL, (h,))
             multiply(0, (1,), ALL, (h,))

@@ -38,7 +38,7 @@ def tile_list_tabres_silu_kernel(tc, tab_words, tab_scales, w, rT, b, offs, out)
 
         reuse = ctx.enter_context(tc.tile_pool(name="reuse", bufs=1))
         TABLE_BYTES = 4 * T
-        PLANES = 3 * TABLE_BYTES + 3072
+        PLANES = 3 * TABLE_BYTES + 3584
         PLACE = {
             "table0": 0,
             "parts2_0": 0,
@@ -50,12 +50,12 @@ def tile_list_tabres_silu_kernel(tc, tab_words, tab_scales, w, rT, b, offs, out)
             "codes2_2": 2 * TABLE_BYTES,
             "codes1_2": 2 * TABLE_BYTES + 4096,
             "planes": PLANES,
-            "minus_hi1": PLANES - 3072,
-            "codes0_2": PLANES + 1024,
+            "minus_hi1": PLANES - 3584,
+            "scales0_2": PLANES + 512,
+            "parts1_0": PLANES + 1024,
         }
         SLOT = {
             "v_scales": "upper0_2",
-            "parts1_0": "parts0_2",
             "turned1": "upper2_0",
             "parts1_2": "upper2_2",
         }
@@ -74,9 +74,6 @@ def tile_list_tabres_silu_kernel(tc, tab_words, tab_scales, w, rT, b, offs, out)
         make_identity(nc, identity[:])
         bias_rows = keep.tile([P, P], F32, name="bias_rows", align_bytes=64)
         nc.vector.memset(bias_rows[:], 0.0)
-
-        warm = keep.tile([P, 1], F32, name="warm")
-        nc.scalar.activation(warm[:], identity[:, :1], SILU)
 
         table, weight, resid = {}, {}, {}
 
@@ -237,7 +234,7 @@ def tile_list_tabres_silu_kernel(tc, tab_words, tab_scales, w, rT, b, offs, out)
         def quantise(a, tiles):
             span = 2 * P * len(tiles)
             codes[a, tiles[0]] = new_tile([P, span], U32, "codes%d_%d" % (a, tiles[0]))
-            scales[a, tiles[0]] = keep.tile([P, span], U8, name="scales%d_%d" % (a, tiles[0]), align_bytes=64)
+            scales[a, tiles[0]] = new_tile([P, span], U8, "scales%d_%d" % (a, tiles[0]))
             nc.vector.quantize_mx(
                 out=codes[a, tiles[0]][:].bitcast(FP8X4),
                 scales=scales[a, tiles[0]][:],

@@ -39,21 +39,7 @@ def tile_list_tabres_silu_kernel(tc, tab_words, tab_scales, w, rT, b, offs, out)
         reuse = ctx.enter_context(tc.tile_pool(name="reuse", bufs=1))
         TABLE_BYTES = 4 * T
         PLANES = 3 * TABLE_BYTES + 3584
-        PLACE = {
-            "table0": 0,
-            "parts2_0": 0,
-            "codes1_0": 4096,
-            "table1": TABLE_BYTES,
-            "parts2_2": TABLE_BYTES,
-            "codes2_0": TABLE_BYTES + 4096,
-            "table2": 2 * TABLE_BYTES,
-            "codes2_2": 2 * TABLE_BYTES,
-            "codes1_2": 2 * TABLE_BYTES + 4096,
-            "planes": PLANES,
-            "minus_hi1": PLANES - 3584,
-            "scales0_2": PLANES + 512,
-            "parts1_0": PLANES + 1024,
-        }
+        PLACE = {}
         SLOT = {
             "v_scales": "upper0_2",
             "turned1": "upper2_0",

@@ -39,7 +39,7 @@ def tile_list_tabres_silu_kernel(tc, tab_words, tab_scales, w, rT, b, offs, out)
         reuse = ctx.enter_context(tc.tile_pool(name="reuse", bufs=1))
         TABLE_BYTES = 4 * T
         PLANES = 3 * TABLE_BYTES + 3584
-        PLACE = {}
+        PLACE = {"table1": 0, "parts2_2": 0}
         SLOT = {
             "v_scales": "upper0_2",
             "turned1": "upper2_0",

@@ -39,7 +39,7 @@ def tile_list_tabres_silu_kernel(tc, tab_words, tab_scales, w, rT, b, offs, out)
         reuse = ctx.enter_context(tc.tile_pool(name="reuse", bufs=1))
         TABLE_BYTES = 4 * T
         PLANES = 3 * TABLE_BYTES + 3584
-        PLACE = {"table1": 0, "parts2_2": 0}
+        PLACE = {"table1": 0, "parts2_2": 0, "codes2_0": 4096}
         SLOT = {
             "v_scales": "upper0_2",
             "turned1": "upper2_0",

@@ -37,19 +37,24 @@ def tile_list_tabres_silu_kernel(tc, tab_words, tab_scales, w, rT, b, offs, out)
         psum = ctx.enter_context(tc.psum_pool(name="psum", bufs=1))
 
         reuse = ctx.enter_context(tc.tile_pool(name="reuse", bufs=1))
-        TABLE_BYTES = 4 * T
-        PLANES = 3 * TABLE_BYTES + 3584
-        PLACE = {"table1": 0, "parts2_2": 0, "codes2_0": 4096}
-        SLOT = {
-            "v_scales": "upper0_2",
-            "turned1": "upper2_0",
-            "parts1_2": "upper2_2",
+        POOL_START = 18
+        PLACE = {
+            "resid1": 18, "top0_0": 26, "parts0_0": 28, "parts0_1": 30,
+            "table0": 32, "res2": 40, "act0": 44, "weight0_0": 48, "weight0_2": 52, "upper0_1": 56,
+            "table1": 64, "parts2_2": 64, "codes2_0": 68, "res0": 72, "act1": 76, "parts0_2": 80,
+            "resid2": 96, "weight1_0": 104, "woven1_0": 112, "parts1_0": 116, "upper1_0": 120, "minus_hi1": 122,
+            "table2": 128, "res1": 136, "act2": 140,
+            "resid3": 160, "weight2_0": 168, "upper2_0": 176, "turned1": 176, "parts2_0": 178,
+            "resid0": 192, "planes": 200, "woven2_2": 202, "upper2_2": 206, "parts1_2": 206, "res3": 210, "act3": 214,
+            "v_words0": 224, "v_words1": 228, "v_words2": 232, "upper0_2": 236, "v_scales": 236,
+            "codes0_0": 238, "codes0_1": 239, "codes0_2": 240, "codes1_0": 242, "codes1_2": 244, "codes2_2": 246,
+            "scales0_0": 248, "scales0_1": 248.5, "scales0_2": 249, "scales1_0": 249.5, "scales1_2": 250,
+            "scales2_0": 250.5, "scales2_2": 251,
         }
 
         def new_tile(shape, dtype, name):
-            if name in PLACE:
-                return reuse.tile(shape, dtype, name=name, align_bytes=64, offset=PLACE[name])
-            return keep.tile(shape, dtype, name=name, tag=SLOT.get(name, name), align_bytes=64)
+            align = 2048 if name == "table0" else 64
+            return reuse.tile(shape, dtype, name=name, align_bytes=align, offset=int((PLACE[name] - POOL_START) * 1024))
 
         offsets = keep.tile([P, S // 16], U16, name="offsets")
 
@@ -69,12 +74,12 @@ def tile_list_tabres_silu_kernel(tc, tab_words, tab_scales, w, rT, b, offs, out)
 
         def load_weight(a, tiles):
             name = "weight%d_%d" % (a, tiles[0])
-            weight[a, tiles[0]] = keep.tile([P, PACK, len(tiles) * P], F32, name=name, align_bytes=64)
+            weight[a, tiles[0]] = new_tile([P, PACK, len(tiles) * P], F32, name)
             rows = w[a * P * PACK : (a + 1) * P * PACK, tiles[0] * P : (tiles[-1] + 1) * P]
             nc.sync.dma_start(weight[a, tiles[0]][:], rows.rearrange("(p t) n -> p t n", t=PACK))
 
         def load_resid(c):
-            resid[c] = keep.tile([P, T], F32, name="resid%d" % c, align_bytes=64)
+            resid[c] = new_tile([P, T], F32, "resid%d" % c)
             nc.sync.dma_start(resid[c][:], rT[c * P : (c + 1) * P, :])
 
         def load_scales():
@@ -122,7 +127,7 @@ def tile_list_tabres_silu_kernel(tc, tab_words, tab_scales, w, rT, b, offs, out)
 
         def make_hi(a, tiles):
             first, width = tiles[0], len(tiles) * P * PACK
-            upper = keep.tile([P, width], BF16, name="upper%d_%d" % (a, first), align_bytes=64)
+            upper = new_tile([P, width], BF16, "upper%d_%d" % (a, first))
             both = new_tile([P, 2, width], BF16, "parts%d_%d" % (a, first))
             parts[a, first] = both
             halves16 = source(a, tiles).bitcast(BF16).rearrange("p t (c i h) -> p c t i h", i=RUN, h=2)
@@ -133,7 +138,7 @@ def tile_list_tabres_silu_kernel(tc, tab_words, tab_scales, w, rT, b, offs, out)
             first, width = tiles[0], len(tiles) * WIDE
             both = new_tile([P, 2, width], BF16, "parts%d_%d" % (a, first))
             parts[a, first] = both
-            top = keep.tile([P, PACK, len(tiles) * P], F32, name="top%d_%d" % (a, first), align_bytes=64)
+            top = new_tile([P, PACK, len(tiles) * P], F32, "top%d_%d" % (a, first))
             nc.vector.tensor_scalar(top[:].bitcast(I32), source(a, tiles).bitcast(I32), TOP_MASK, None, ALU.bitwise_and)
             nc.vector.tensor_tensor(
                 both[:, 1, :].rearrange("p (c i t) -> p c t i", i=RUN, t=PACK),
@@ -166,7 +171,7 @@ def tile_list_tabres_silu_kernel(tc, tab_words, tab_scales, w, rT, b, offs, out)
 
         def make_lo_woven(a, tiles):
             both = parts[a, tiles[0]]
-            woven = keep.tile([P, len(tiles) * P * PACK], F32, name="woven%d_%d" % (a, tiles[0]), align_bytes=64)
+            woven = new_tile([P, len(tiles) * P * PACK], F32, "woven%d_%d" % (a, tiles[0]))
             nc.scalar.copy(
                 woven[:].rearrange("p (n t) -> p n t", t=PACK),
                 source(a, tiles).rearrange("p t n -> p n t"),
@@ -247,12 +252,12 @@ def tile_list_tabres_silu_kernel(tc, tab_words, tab_scales, w, rT, b, offs, out)
                         )
 
         def activate(c):
-            act[c] = keep.tile([P, S], F32, name="act%d" % c, align_bytes=64)
+            act[c] = new_tile([P, S], F32, "act%d" % c)
             for h in range(HALVES):
                 nc.scalar.activation(act[c][:, h * BANK : (h + 1) * BANK], acc[c, h][:], SILU, bias=bias[:, c : c + 1])
 
         def finish(c, widths):
-            res = keep.tile([P, S], F32, name="res%d" % c, align_bytes=64)
+            res = new_tile([P, S], F32, "res%d" % c)
             done = 0
             for width in widths:
                 cols = slice(done, done + width)

@@ -64,7 +64,9 @@ def tile_list_tabres_silu_kernel(tc, tab_words, tab_scales, w, rT, b, offs, out)
         identity = keep.tile([P, P], F32, name="identity", align_bytes=64)
         make_identity(nc, identity[:])
         bias_rows = keep.tile([P, P], F32, name="bias_rows", align_bytes=64)
-        nc.vector.memset(bias_rows[:], 0.0)
+        zeros = keep.tile([P, P], F32, name="zeros", align_bytes=64)
+        nc.vector.memset(zeros[:], 0.0)
+        nc.scalar.activation(bias_rows[:], zeros[:], SILU)
 
         table, weight, resid = {}, {}, {}
 

@@ -41,15 +41,15 @@ def tile_list_tabres_silu_kernel(tc, tab_words, tab_scales, w, rT, b, offs, out)
         PLACE = {
             "resid1": 18, "top0_0": 26, "parts0_0": 28, "parts0_1": 30,
             "table0": 32, "res2": 40, "act0": 44, "weight0_0": 48, "weight0_2": 52, "upper0_1": 56,
-            "table1": 64, "parts2_2": 64, "codes2_0": 68, "res0": 72, "act1": 76, "parts0_2": 80,
+            "table1": 64, "parts2_2": 84, "codes2_0": 88, "res0": 72, "act1": 76, "parts0_2": 80,
             "resid2": 96, "weight1_0": 104, "woven1_0": 112, "parts1_0": 116, "upper1_0": 120, "minus_hi1": 122,
             "table2": 128, "res1": 136, "act2": 140,
-            "resid3": 160, "weight2_0": 168, "upper2_0": 176, "turned1": 176, "parts2_0": 178,
-            "resid0": 192, "planes": 200, "woven2_2": 202, "upper2_2": 206, "parts1_2": 206, "res3": 210, "act3": 214,
+            "resid3": 160, "weight2_0": 168, "weight2_2": 172, "woven2_0": 182, "upper2_0": 176, "parts2_0": 178,
+            "resid0": 192, "planes": 200, "woven2_2": 186, "turned1": 204.5, "upper2_2": 206, "parts1_2": 207, "res3": 212, "act3": 216,
             "v_words0": 224, "v_words1": 228, "v_words2": 232, "upper0_2": 236, "v_scales": 236,
             "codes0_0": 238, "codes0_1": 239, "codes0_2": 240, "codes1_0": 242, "codes1_2": 244, "codes2_2": 246,
             "scales0_0": 248, "scales0_1": 248.5, "scales0_2": 249, "scales1_0": 249.5, "scales1_2": 250,
-            "scales2_0": 250.5, "scales2_2": 251,
+            "scales2_0": 206.5, "scales2_2": 251,
         }
 
         def new_tile(shape, dtype, name):
@@ -96,8 +96,9 @@ def tile_list_tabres_silu_kernel(tc, tab_words, tab_scales, w, rT, b, offs, out)
         load_weight(1, ALL)
         nc.sync.dma_start(bias_rows[:TILES, :], b.rearrange("(c p) -> c p", p=P))
         load_table(0)
-        load_weight(2, ALL)
+        load_weight(2, A)
         load_table(1)
+        load_weight(2, B)
         load_table(2)
         for c in range(TILES):
             load_resid(c)
@@ -285,13 +286,13 @@ def tile_list_tabres_silu_kernel(tc, tab_words, tab_scales, w, rT, b, offs, out)
             multiply(0, (0,), ALL, (h,))
             multiply(0, (1,), ALL, (h,))
         make_hi(2, A)
-        make_lo_on_gpsimd(2, A)
-        turn_back(1, B)
+        make_lo_woven(2, A)
         quantise(1, A)
         gather_words(1, 1)
         multiply(1, A, ALL)
         make_hi(2, B)
         make_lo_woven(2, B)
+        turn_back(1, B)
         collect_parts(1, B)
         quantise(2, A)
         gather_words(2, 2)
@@ -308,4 +309,4 @@ def tile_list_tabres_silu_kernel(tc, tab_words, tab_scales, w, rT, b, offs, out)
         finish(0, (512, 512))
         finish(1, (1024,))
         finish(2, (1024,))
-        finish(3, (512, 256, 256))
+        finish(3, (512, 384, 128))

@@ -241,7 +241,7 @@ def tile_list_tabres_silu_kernel(tc, tab_words, tab_scales, w, rT, b, offs, out)
                     if c not in wanted:
                         continue
                     if a == 0:
-                        acc[c, h] = psum.tile([P, BANK], F32, name="acc%d_%d" % (c, h), tag="bank%d_%d" % (c % 2, h))
+                        acc[c, h] = psum.tile([P, BANK], F32, name="acc%d_%d" % (c, h), tag="bank%d_%d" % (c % 3, h))
                     for part in range(2):
                         cols = slice((part * len(tiles) + m) * P, (part * len(tiles) + m + 1) * P)
                         nc.tensor.matmul_mx(
@@ -281,10 +281,11 @@ def tile_list_tabres_silu_kernel(tc, tab_words, tab_scales, w, rT, b, offs, out)
         quantise(0, B)
         make_hi(1, A)
         make_lo_woven(1, A)
-        gather_words(0, 1)
+        gather_words(0, 2)
         for h in range(HALVES):
             multiply(0, (0,), ALL, (h,))
             multiply(0, (1,), ALL, (h,))
+        multiply(0, B, (2,))
         make_hi(2, A)
         make_lo_woven(2, A)
         quantise(1, A)
@@ -303,10 +304,10 @@ def tile_list_tabres_silu_kernel(tc, tab_words, tab_scales, w, rT, b, offs, out)
         quantise(1, B)
         for c in B:
             for h in range(HALVES):
-                for a in range(PASSES):
+                for a in range(1 if c == 2 else 0, PASSES):
                     multiply(a, B, (c,), (h,))
             activate(c)
         finish(0, (512, 512))
         finish(1, (1024,))
         finish(2, (1024,))
-        finish(3, (512, 384, 128))
+        finish(3, (512, 256, 256))

@@ -176,8 +176,8 @@ def tile_list_tabres_silu_kernel(tc, tab_words, tab_scales, w, rT, b, offs, out)
             both = parts[a, tiles[0]]
             woven = new_tile([P, len(tiles) * P * PACK], F32, "woven%d_%d" % (a, tiles[0]))
             nc.scalar.copy(
-                woven[:].rearrange("p (n t) -> p n t", t=PACK),
-                source(a, tiles).rearrange("p t n -> p n t"),
+                woven[:].rearrange("p (c i t) -> p c t i", i=RUN, t=PACK),
+                source(a, tiles).rearrange("p t (c i) -> p c t i", i=RUN),
             )
             nc.gpsimd.tensor_tensor(both[:, 1, :], woven[:], both[:, 0, :], ALU.subtract)
 

@@ -23,11 +23,27 @@ PASSES = K // (P * PACK)
 TILES = M // P
 BANK = 512
 HALVES = S // BANK
-HI_MASK = 0xFFF0FFF0 - (1 << 32)
-TOP_MASK = 0xFFF00000 - (1 << 32)
-SIGN_BIT = -(1 << 31)
-RUN = 2
+GROUP = 16
+QUADRANT = 32
+SCALE_ROWS = 4
+WORD_BYTES = 4
 WIDE = PACK * P
+RUN = 2
+ALIGN = 256
+PAIR_MASK = 0xFFF0FFF0 - (1 << 32)
+WORD_MASK = 0xFFF00000 - (1 << 32)
+SIGN_BIT = -(1 << 31)
+FIRST, SECOND, ALL = (0, 1), (2, 3), (0, 1, 2, 3)
+
+FOLLOWS = {"v_scales": "upper0_2"}
+PIECE_BYTES = len(SECOND) * WIDE * 2
+SHARE_BYTES = PIECE_BYTES // 4
+ON_LAST_MASK = {
+    "turned": 0,
+    "upper2_2": PIECE_BYTES - SHARE_BYTES,
+    "scales2_0": PIECE_BYTES,
+    "parts1_2": PIECE_BYTES + SHARE_BYTES,
+}
 
 
 def tile_list_tabres_silu_kernel(tc, tab_words, tab_scales, w, rT, b, offs, out):
@@ -35,36 +51,23 @@ def tile_list_tabres_silu_kernel(tc, tab_words, tab_scales, w, rT, b, offs, out)
     with ExitStack() as ctx:
         keep = ctx.enter_context(tc.tile_pool(name="keep", bufs=1))
         psum = ctx.enter_context(tc.psum_pool(name="psum", bufs=1))
-
-        reuse = ctx.enter_context(tc.tile_pool(name="reuse", bufs=1))
-        POOL_START = 18
-        PLACE = {
-            "resid1": 18, "top0_0": 26, "parts0_0": 28, "parts0_1": 30,
-            "table0": 32, "res2": 40, "act0": 44, "weight0_0": 48, "weight0_2": 52, "upper0_1": 56,
-            "table1": 64, "parts2_2": 84, "codes2_0": 88, "res0": 72, "act1": 76, "parts0_2": 80,
-            "resid2": 96, "weight1_0": 104, "woven1_0": 112, "parts1_0": 116, "upper1_0": 120, "minus_hi1": 122,
-            "table2": 128, "res1": 136, "act2": 140,
-            "resid3": 160, "weight2_0": 168, "weight2_2": 172, "woven2_0": 182, "upper2_0": 176, "parts2_0": 178,
-            "resid0": 192, "planes": 200, "woven2_2": 186, "turned1": 204.5, "upper2_2": 206, "parts1_2": 207, "res3": 212, "act3": 216,
-            "v_words0": 224, "v_words1": 228, "v_words2": 232, "upper0_2": 236, "v_scales": 236,
-            "codes0_0": 238, "codes0_1": 239, "codes0_2": 240, "codes1_0": 242, "codes1_2": 244, "codes2_2": 246,
-            "scales0_0": 248, "scales0_1": 248.5, "scales0_2": 249, "scales1_0": 249.5, "scales1_2": 250,
-            "scales2_0": 206.5, "scales2_2": 251,
-        }
+        overlaid = ctx.enter_context(tc.tile_pool(name="overlaid", bufs=1))
 
         def new_tile(shape, dtype, name):
-            align = 2048 if name == "table0" else 64
-            return reuse.tile(shape, dtype, name=name, align_bytes=align, offset=int((PLACE[name] - POOL_START) * 1024))
+            if name in ON_LAST_MASK:
+                return overlaid.tile(shape, dtype, name=name, align_bytes=ALIGN, offset=ON_LAST_MASK[name])
+            return keep.tile(shape, dtype, name=name, tag=FOLLOWS.get(name, name), align_bytes=ALIGN)
 
-        offsets = keep.tile([P, S // 16], U16, name="offsets")
+        offsets = keep.tile([P, S // GROUP], U16, name="offsets")
 
-        planes = new_tile([P, T // 4], I32, "planes")
-        nc.vector.memset(planes[:], 0)
+        scale_rows = new_tile([P, T // WORD_BYTES], I32, "scale_rows")
+        nc.vector.memset(scale_rows[:], 0)
 
-        identity = keep.tile([P, P], F32, name="identity", align_bytes=64)
+        identity = new_tile([P, P], F32, "identity")
         make_identity(nc, identity[:])
-        bias_rows = keep.tile([P, P], F32, name="bias_rows", align_bytes=64)
-        zeros = keep.tile([P, P], F32, name="zeros", align_bytes=64)
+
+        bias_rows = new_tile([P, P], F32, "bias_rows")
+        zeros = new_tile([P, P], F32, "zeros")
         nc.vector.memset(zeros[:], 0.0)
         nc.scalar.activation(bias_rows[:], zeros[:], SILU)
 
@@ -75,8 +78,7 @@ def tile_list_tabres_silu_kernel(tc, tab_words, tab_scales, w, rT, b, offs, out)
             nc.sync.dma_start(table[a][:], tab_words[a].rearrange("p t i -> p (t i)").bitcast(I32))
 
         def load_weight(a, tiles):
-            name = "weight%d_%d" % (a, tiles[0])
-            weight[a, tiles[0]] = new_tile([P, PACK, len(tiles) * P], F32, name)
+            weight[a, tiles[0]] = new_tile([P, PACK, len(tiles) * P], F32, "weight%d_%d" % (a, tiles[0]))
             rows = w[a * P * PACK : (a + 1) * P * PACK, tiles[0] * P : (tiles[-1] + 1) * P]
             nc.sync.dma_start(weight[a, tiles[0]][:], rows.rearrange("(p t) n -> p t n", t=PACK))
 
@@ -84,145 +86,116 @@ def tile_list_tabres_silu_kernel(tc, tab_words, tab_scales, w, rT, b, offs, out)
             resid[c] = new_tile([P, T], F32, "resid%d" % c)
             nc.sync.dma_start(resid[c][:], rT[c * P : (c + 1) * P, :])
 
-        def load_scales():
-            for q in range(4):
-                nc.sync.dma_start(planes[32 * q : 32 * q + 4 * PASSES, :], tab_scales[:, 4 * q : 4 * q + 4, :].bitcast(I32))
+        def load_scale_rows():
+            for q in range(P // QUADRANT):
+                rows = scale_rows[QUADRANT * q : QUADRANT * q + SCALE_ROWS * PASSES, :]
+                nc.sync.dma_start(rows, tab_scales[:, SCALE_ROWS * q : SCALE_ROWS * (q + 1), :].bitcast(I32))
 
-        A, B, ALL = (0, 1), (2, 3), (0, 1, 2, 3)
-        load_weight(0, A)
-        load_weight(0, B)
+        load_weight(0, FIRST)
+        load_weight(0, SECOND)
         nc.sync.dma_start(offsets[:], offs)
-        load_scales()
+        load_scale_rows()
         load_weight(1, ALL)
         nc.sync.dma_start(bias_rows[:TILES, :], b.rearrange("(c p) -> c p", p=P))
         load_table(0)
-        load_weight(2, A)
+        load_weight(2, FIRST)
         load_table(1)
-        load_weight(2, B)
+        load_weight(2, SECOND)
         load_table(2)
         for c in range(TILES):
             load_resid(c)
 
-        acc = {}
         bias = keep.tile([P, TILES], F32, name="bias")
         turned_bias = psum.tile([P, BANK], F32, name="turned_bias", tag="spare1")
         nc.tensor.transpose(turned_bias[:, :P], bias_rows[:], identity[:])
         nc.scalar.copy(bias[:], turned_bias[:, :TILES])
-        v_words, parts, act, codes, scales = {}, {}, {}, {}, {}
 
-        def gather_words(a, pieces):
+        v_words, v_scales, parts, codes, scales, acc, act = {}, {}, {}, {}, {}, {}, {}
+
+        def gather_words(a, cuts):
             v_words[a] = new_tile([P, S], U32, "v_words%d" % a)
-            width = S // pieces
-            for n in range(pieces):
-                picks = offsets[:, n * width // 16 : (n + 1) * width // 16]
+            width = S // cuts
+            for n in range(cuts):
+                picks = offsets[:, n * width // GROUP : (n + 1) * width // GROUP]
                 nc.vector.tensor_copy(v_words[a][:, n * width : (n + 1) * width], table[a][:].bitcast(U32).indirect(picks))
 
-        held = {}
-
         def gather_scales():
-            v_scales = new_tile([P, S], U8, "v_scales")
-            held["scales"] = v_scales
-            nc.vector.tensor_copy(v_scales[:], planes[:].bitcast(U8).indirect(offsets[:]))
+            gathered = new_tile([P, S], U8, "v_scales")
+            nc.vector.tensor_copy(gathered[:], scale_rows[:].bitcast(U8).indirect(offsets[:]))
+            for a in range(PASSES):
+                v_scales[a] = gathered[SCALE_ROWS * a : P, :]
 
         def source(a, tiles):
             first = max(f for (n, f) in weight if n == a and f <= tiles[0])
             return weight[a, first][:, :, (tiles[0] - first) * P : (tiles[-1] + 1 - first) * P]
 
-        def make_hi(a, tiles):
-            first, width = tiles[0], len(tiles) * P * PACK
-            upper = new_tile([P, width], BF16, "upper%d_%d" % (a, first))
-            both = new_tile([P, 2, width], BF16, "parts%d_%d" % (a, first))
-            parts[a, first] = both
-            halves16 = source(a, tiles).bitcast(BF16).rearrange("p t (c i h) -> p c t i h", i=RUN, h=2)
-            nc.scalar.copy(upper[:].rearrange("p (c i t) -> p c t i", i=RUN, t=PACK), halves16[:, :, :, :, 1])
-            nc.vector.tensor_scalar(both[:, 0, :].bitcast(I32), upper[:].bitcast(I32), HI_MASK, None, ALU.bitwise_and)
+        def by_rows(rows):
+            return rows.rearrange("p t (c i) -> p c t i", i=RUN)
+
+        def woven_by_rows(values):
+            return values.rearrange("p (c i t) -> p c t i", i=RUN, t=PACK)
+
+        def new_parts(a, tiles):
+            parts[a, tiles[0]] = new_tile([P, 2, len(tiles) * WIDE], BF16, "parts%d_%d" % (a, tiles[0]))
+            return parts[a, tiles[0]]
 
         def split_on_vector(a, tiles):
-            first, width = tiles[0], len(tiles) * WIDE
-            both = new_tile([P, 2, width], BF16, "parts%d_%d" % (a, first))
-            parts[a, first] = both
-            top = new_tile([P, PACK, len(tiles) * P], F32, "top%d_%d" % (a, first))
-            nc.vector.tensor_scalar(top[:].bitcast(I32), source(a, tiles).bitcast(I32), TOP_MASK, None, ALU.bitwise_and)
-            nc.vector.tensor_tensor(
-                both[:, 1, :].rearrange("p (c i t) -> p c t i", i=RUN, t=PACK),
-                source(a, tiles).rearrange("p t (c i) -> p c t i", i=RUN),
-                top[:].rearrange("p t (c i) -> p c t i", i=RUN),
-                ALU.subtract,
-            )
-            nc.vector.tensor_copy(
-                both[:, 0, :].rearrange("p (c i t) -> p c t i", i=RUN, t=PACK),
-                top[:].rearrange("p t (c i) -> p c t i", i=RUN),
-            )
+            both = new_parts(a, tiles)
+            masked = new_tile([P, PACK, len(tiles) * P], F32, "masked")
+            nc.vector.tensor_scalar(masked[:].bitcast(I32), source(a, tiles).bitcast(I32), WORD_MASK, None, ALU.bitwise_and)
+            nc.vector.tensor_tensor(woven_by_rows(both[:, 1, :]), by_rows(source(a, tiles)), by_rows(masked[:]), ALU.subtract)
+            nc.vector.tensor_copy(woven_by_rows(both[:, 0, :]), by_rows(masked[:]))
 
-        def make_lo(a, tiles):
+        def make_hi(a, tiles):
+            upper = new_tile([P, len(tiles) * WIDE], BF16, "upper%d_%d" % (a, tiles[0]))
+            both = new_parts(a, tiles)
+            halves16 = source(a, tiles).bitcast(BF16).rearrange("p t (c i h) -> p c t i h", i=RUN, h=2)
+            nc.scalar.copy(woven_by_rows(upper[:]), halves16[:, :, :, :, 1])
+            nc.vector.tensor_scalar(both[:, 0, :].bitcast(I32), upper[:].bitcast(I32), PAIR_MASK, None, ALU.bitwise_and)
+
+        def make_lo_on_vector(a, tiles):
             both = parts[a, tiles[0]]
-            nc.vector.tensor_tensor(
-                both[:, 1, :].rearrange("p (c i t) -> p c t i", i=RUN, t=PACK),
-                source(a, tiles).rearrange("p t (c i) -> p c t i", i=RUN),
-                both[:, 0, :].rearrange("p (c i t) -> p c t i", i=RUN, t=PACK),
-                ALU.subtract,
-            )
+            nc.vector.tensor_tensor(woven_by_rows(both[:, 1, :]), by_rows(source(a, tiles)), woven_by_rows(both[:, 0, :]), ALU.subtract)
 
         def make_lo_on_gpsimd(a, tiles):
             both = parts[a, tiles[0]]
-            nc.gpsimd.tensor_tensor(
-                both[:, 1, :].rearrange("p (n t) -> p n t", t=PACK),
-                source(a, tiles).rearrange("p t n -> p n t"),
-                both[:, 0, :].rearrange("p (n t) -> p n t", t=PACK),
-                ALU.subtract,
-            )
-
-        def make_lo_woven(a, tiles):
-            both = parts[a, tiles[0]]
-            woven = new_tile([P, len(tiles) * P * PACK], F32, "woven%d_%d" % (a, tiles[0]))
-            nc.scalar.copy(
-                woven[:].rearrange("p (c i t) -> p c t i", i=RUN, t=PACK),
-                source(a, tiles).rearrange("p t (c i) -> p c t i", i=RUN),
-            )
+            woven = new_tile([P, len(tiles) * WIDE], F32, "woven%d_%d" % (a, tiles[0]))
+            nc.scalar.copy(woven_by_rows(woven[:]), by_rows(source(a, tiles)))
             nc.gpsimd.tensor_tensor(both[:, 1, :], woven[:], both[:, 0, :], ALU.subtract)
 
-        there, minus_hi = {}, {}
+        transposed, minus_hi = {}, {}
 
         def subtract_on_tensor(a, tiles):
-            count = len(tiles)
             src = source(a, tiles)
-            minus_hi[a] = new_tile([P, PACK, count * P], F32, "minus_hi%d" % a)
-            nc.vector.tensor_scalar(minus_hi[a][:].bitcast(I32), src.bitcast(I32), TOP_MASK, SIGN_BIT, ALU.bitwise_and, ALU.bitwise_xor)
-            for m in range(count):
+            minus_hi[a] = new_tile([P, PACK, len(tiles) * P], F32, "minus_hi")
+            nc.vector.tensor_scalar(minus_hi[a][:].bitcast(I32), src.bitcast(I32), WORD_MASK, SIGN_BIT, ALU.bitwise_and, ALU.bitwise_xor)
+            for m in range(len(tiles)):
                 cols = slice(m * P, (m + 1) * P)
-                there[m] = psum.tile([P, BANK], F32, name="there%d_%d" % (a, m), tag="spare%d" % m)
+                transposed[m] = psum.tile([P, BANK], F32, name="transposed%d" % m, tag="spare%d" % m)
                 for t in range(PACK):
-                    block = there[m][:, t * P : (t + 1) * P]
+                    block = transposed[m][:, t * P : (t + 1) * P]
                     nc.tensor.matmul(block, src[:, t, cols], identity[:], start=True, stop=False, is_transpose=True)
                     nc.tensor.matmul(block, minus_hi[a][:, t, cols], identity[:], start=False, stop=True, is_transpose=True)
 
-        def turn_back(a, tiles):
-            count = len(tiles)
-            turned = new_tile([P, count * WIDE], BF16, "turned%d" % a)
-            for m in range(count):
+        def turn_back(tiles):
+            turned = new_tile([P, len(tiles) * WIDE], BF16, "turned")
+            for m in range(len(tiles)):
                 nc.scalar.copy(
                     turned[:, m * WIDE : (m + 1) * WIDE].rearrange("n (u p e) -> n u p e", u=2, e=2),
-                    there[m][:].rearrange("n (u e p) -> n u p e", u=2, e=2),
+                    transposed[m][:].rearrange("n (u e p) -> n u p e", u=2, e=2),
                 )
-            for m in range(count):
-                words = turned[:, m * WIDE : (m + 1) * WIDE].bitcast(F32)
+            for m in range(len(tiles)):
+                pairs = turned[:, m * WIDE : (m + 1) * WIDE].bitcast(F32)
                 for u in range(2):
-                    nc.tensor.transpose(there[m][:, u * P : (u + 1) * P], words[:, u * P : (u + 1) * P], identity[:])
+                    nc.tensor.transpose(transposed[m][:, u * P : (u + 1) * P], pairs[:, u * P : (u + 1) * P], identity[:])
 
         def collect_parts(a, tiles):
-            first, count = tiles[0], len(tiles)
-            both = new_tile([P, 2, count * WIDE], BF16, "parts%d_%d" % (a, first))
-            parts[a, first] = both
-            nc.scalar.activation(
-                both[:, 0, :].rearrange("p (c i t) -> p c t i", i=RUN, t=PACK),
-                minus_hi[a][:].rearrange("p t (c i) -> p c t i", i=RUN),
-                COPY,
-                scale=-1.0,
-            )
-            for m in range(count):
+            both = new_parts(a, tiles)
+            nc.scalar.activation(woven_by_rows(both[:, 0, :]), by_rows(minus_hi[a][:]), COPY, scale=-1.0)
+            for m in range(len(tiles)):
                 nc.scalar.copy(
                     both[:, 1, m * WIDE : (m + 1) * WIDE].bitcast(F32).rearrange("p (n u) -> p n u", u=2),
-                    there[m][:, : 2 * P].rearrange("p (u n) -> p n u", u=2),
+                    transposed[m][:, : 2 * P].rearrange("p (u n) -> p n u", u=2),
                 )
 
         def quantise(a, tiles):
@@ -235,24 +208,20 @@ def tile_list_tabres_silu_kernel(tc, tab_words, tab_scales, w, rT, b, offs, out)
                 in_=parts[a, tiles[0]][:].rearrange("p s x -> p (s x)"),
             )
 
-        def multiply(a, tiles, wanted, halves=(0, 1)):
-            for h in halves:
-                for m, c in enumerate(tiles):
-                    if c not in wanted:
-                        continue
-                    if a == 0:
-                        acc[c, h] = psum.tile([P, BANK], F32, name="acc%d_%d" % (c, h), tag="bank%d_%d" % (c % 3, h))
-                    for part in range(2):
-                        cols = slice((part * len(tiles) + m) * P, (part * len(tiles) + m + 1) * P)
-                        nc.tensor.matmul_mx(
-                            out=acc[c, h][:],
-                            lhsT=codes[a, tiles[0]][:, cols].bitcast(FP8X4),
-                            lhsT_scale=scales[a, tiles[0]][:, cols],
-                            rhs=v_words[a][:, h * BANK : (h + 1) * BANK].bitcast(FP8X4),
-                            rhs_scale=held["scales"][4 * a : P, h * BANK : (h + 1) * BANK],
-                            start=(a == 0 and part == 0),
-                            stop=(a == PASSES - 1 and part == 1),
-                        )
+        def multiply(a, tiles, c, h):
+            if a == 0:
+                acc[c, h] = psum.tile([P, BANK], F32, name="acc%d_%d" % (c, h), tag="bank%d_%d" % (c % (TILES - 1), h))
+            for part in range(2):
+                at = (part * len(tiles) + tiles.index(c)) * P
+                nc.tensor.matmul_mx(
+                    out=acc[c, h][:],
+                    lhsT=codes[a, tiles[0]][:, at : at + P].bitcast(FP8X4),
+                    lhsT_scale=scales[a, tiles[0]][:, at : at + P],
+                    rhs=v_words[a][:, h * BANK : (h + 1) * BANK].bitcast(FP8X4),
+                    rhs_scale=v_scales[a][:, h * BANK : (h + 1) * BANK],
+                    start=(a == 0 and part == 0),
+                    stop=(a == PASSES - 1 and part == 1),
+                )
 
         def activate(c):
             act[c] = new_tile([P, S], F32, "act%d" % c)
@@ -264,50 +233,58 @@ def tile_list_tabres_silu_kernel(tc, tab_words, tab_scales, w, rT, b, offs, out)
             done = 0
             for width in widths:
                 cols = slice(done, done + width)
-                picks = offsets[:, done // 16 : (done + width) // 16]
+                picks = offsets[:, done // GROUP : (done + width) // GROUP]
                 nc.vector.tensor_tensor(res[:, cols], resid[c][:].indirect(picks), act[c][:, cols], ALU.add)
                 nc.sync.dma_start(out[c * P : (c + 1) * P, cols], res[:, cols])
                 done += width
 
         split_on_vector(0, (0,))
         make_hi(0, (1,))
-        make_lo(0, (1,))
+        make_lo_on_vector(0, (1,))
         quantise(0, (0,))
         quantise(0, (1,))
-        make_hi(0, B)
-        make_lo_on_gpsimd(0, B)
+        make_hi(0, SECOND)
+        make_lo_on_gpsimd(0, SECOND)
         gather_scales()
-        subtract_on_tensor(1, B)
-        quantise(0, B)
-        make_hi(1, A)
-        make_lo_woven(1, A)
-        gather_words(0, 2)
+
+        subtract_on_tensor(1, SECOND)
+        quantise(0, SECOND)
+        make_hi(1, FIRST)
+        make_lo_on_gpsimd(1, FIRST)
+        gather_words(0, HALVES)
         for h in range(HALVES):
-            multiply(0, (0,), ALL, (h,))
-            multiply(0, (1,), ALL, (h,))
-        multiply(0, B, (2,))
-        make_hi(2, A)
-        make_lo_woven(2, A)
-        quantise(1, A)
+            for c in FIRST:
+                multiply(0, (c,), c, h)
+        for h in range(HALVES):
+            multiply(0, SECOND, SECOND[0], h)
+
+        make_hi(2, FIRST)
+        make_lo_on_gpsimd(2, FIRST)
+        quantise(1, FIRST)
         gather_words(1, 1)
-        multiply(1, A, ALL)
-        make_hi(2, B)
-        make_lo_woven(2, B)
-        turn_back(1, B)
-        collect_parts(1, B)
-        quantise(2, A)
-        gather_words(2, 2)
-        multiply(2, A, ALL)
-        activate(0)
-        activate(1)
-        quantise(2, B)
-        quantise(1, B)
-        for c in B:
-            for h in range(HALVES):
-                for a in range(1 if c == 2 else 0, PASSES):
-                    multiply(a, B, (c,), (h,))
+        for h in range(HALVES):
+            for c in FIRST:
+                multiply(1, FIRST, c, h)
+        make_hi(2, SECOND)
+        make_lo_on_gpsimd(2, SECOND)
+        turn_back(SECOND)
+        collect_parts(1, SECOND)
+        quantise(2, FIRST)
+        gather_words(2, HALVES)
+        for h in range(HALVES):
+            for c in FIRST:
+                multiply(2, FIRST, c, h)
+        for c in FIRST:
             activate(c)
-        finish(0, (512, 512))
-        finish(1, (1024,))
-        finish(2, (1024,))
-        finish(3, (512, 256, 256))
+        quantise(2, SECOND)
+        quantise(1, SECOND)
+        for c in SECOND:
+            for h in range(HALVES):
+                for a in range(1 if c == SECOND[0] else 0, PASSES):
+                    multiply(a, SECOND, c, h)
+            activate(c)
+
+        finish(0, (BANK, BANK))
+        finish(1, (S,))
+        finish(2, (S,))
+        finish(3, (BANK, BANK // 2, BANK // 2))

@@ -16,6 +16,7 @@ FP8X4 = mybir.dt.float8_e4m3fn_x4
 ALU = mybir.AluOpType
 SILU = mybir.ActivationFunctionType.Silu
 COPY = mybir.ActivationFunctionType.Copy
+BYTES_OF = {F32: 4, BF16: 2, I32: 4, U32: 4, U8: 1}
 
 P = 128
 PACK = 4
@@ -35,15 +36,11 @@ WORD_MASK = 0xFFF00000 - (1 << 32)
 SIGN_BIT = -(1 << 31)
 FIRST, SECOND, ALL = (0, 1), (2, 3), (0, 1, 2, 3)
 
-FOLLOWS = {"v_scales": "upper0_2"}
-PIECE_BYTES = len(SECOND) * WIDE * 2
-SHARE_BYTES = PIECE_BYTES // 4
-ON_LAST_MASK = {
-    "turned": 0,
-    "upper2_2": PIECE_BYTES - SHARE_BYTES,
-    "scales2_0": PIECE_BYTES,
-    "parts1_2": PIECE_BYTES + SHARE_BYTES,
-}
+LIES_ON = {"v_words0": ("upper0_2", 0), "scales0_2": ("table0", 0), "v_scales": ("upper1_0", 0), "scales1_0": ("scale_rows", 0),
+    "turned1": ("upper2_2", -1536), "scales2_0": ("upper2_2", 512), "parts1_2": ("upper2_2", 1024)}
+ROOM = {"upper0_2": (0, 2048), "upper2_2": (1536, 3072)}
+BANK_OF = {"bias": "e", ("forth", 1, 0): "t0", ("forth", 1, 1): "t1", ("back", 1): "t0",
+    (0, 0): "a", (0, 1): "b", (1, 0): "c", (1, 1): "d", (2, 0): "e", (2, 1): "f", (3, 0): "a", (3, 1): "b"}
 
 
 def tile_list_tabres_silu_kernel(tc, tab_words, tab_scales, w, rT, b, offs, out):
@@ -51,25 +48,29 @@ def tile_list_tabres_silu_kernel(tc, tab_words, tab_scales, w, rT, b, offs, out)
     with ExitStack() as ctx:
         keep = ctx.enter_context(tc.tile_pool(name="keep", bufs=1))
         psum = ctx.enter_context(tc.psum_pool(name="psum", bufs=1))
-        overlaid = ctx.enter_context(tc.tile_pool(name="overlaid", bufs=1))
+        placed = ctx.enter_context(tc.tile_pool(name="placed", bufs=1))
+        address = {"free": 0}
 
         def new_tile(shape, dtype, name):
-            if name in ON_LAST_MASK:
-                return overlaid.tile(shape, dtype, name=name, align_bytes=ALIGN, offset=ON_LAST_MASK[name])
-            return keep.tile(shape, dtype, name=name, tag=FOLLOWS.get(name, name), align_bytes=ALIGN)
+            size = BYTES_OF[dtype]
+            for n in shape[1:]:
+                size = size * n
+            if name in LIES_ON:
+                older, shift = LIES_ON[name]
+                address[name] = address[older] + shift
+                before, behind = ROOM.get(older, (0, 0))
+                assert -before <= shift and address[name] + size <= address[older, "end"] + behind
+                assert address[name] < address[older, "end"] and address[name] + size > address[older]
+            else:
+                before, behind = ROOM.get(name, (0, 0))
+                address[name] = address["free"] + before
+                address["free"] = address[name] + -(-size // ALIGN) * ALIGN + behind
+            address[name, "end"] = address[name] + size
+            return placed.tile(shape, dtype, name=name, align_bytes=ALIGN, offset=address[name])
 
         offsets = keep.tile([P, S // GROUP], U16, name="offsets")
-
         scale_rows = new_tile([P, T // WORD_BYTES], I32, "scale_rows")
         nc.vector.memset(scale_rows[:], 0)
-
-        identity = new_tile([P, P], F32, "identity")
-        make_identity(nc, identity[:])
-
-        bias_rows = new_tile([P, P], F32, "bias_rows")
-        zeros = new_tile([P, P], F32, "zeros")
-        nc.vector.memset(zeros[:], 0.0)
-        nc.scalar.activation(bias_rows[:], zeros[:], SILU)
 
         table, weight, resid = {}, {}, {}
 
@@ -86,31 +87,30 @@ def tile_list_tabres_silu_kernel(tc, tab_words, tab_scales, w, rT, b, offs, out)
             resid[c] = new_tile([P, T], F32, "resid%d" % c)
             nc.sync.dma_start(resid[c][:], rT[c * P : (c + 1) * P, :])
 
-        def load_scale_rows():
-            for q in range(P // QUADRANT):
-                rows = scale_rows[QUADRANT * q : QUADRANT * q + SCALE_ROWS * PASSES, :]
-                nc.sync.dma_start(rows, tab_scales[:, SCALE_ROWS * q : SCALE_ROWS * (q + 1), :].bitcast(I32))
+        def load_scale_rows(q, queue):
+            rows = scale_rows[QUADRANT * q : QUADRANT * q + SCALE_ROWS * PASSES, :]
+            queue.dma_start(rows, tab_scales[:, SCALE_ROWS * q : SCALE_ROWS * (q + 1), :].bitcast(I32))
 
-        load_weight(0, FIRST)
-        load_weight(0, SECOND)
-        nc.sync.dma_start(offsets[:], offs)
-        load_scale_rows()
-        load_weight(1, ALL)
-        nc.sync.dma_start(bias_rows[:TILES, :], b.rearrange("(c p) -> c p", p=P))
-        load_table(0)
-        load_weight(2, FIRST)
-        load_table(1)
-        load_weight(2, SECOND)
-        load_table(2)
-        for c in range(TILES):
-            load_resid(c)
-
+        identity = new_tile([P, P], F32, "identity")
+        bias_rows = new_tile([P, P], F32, "bias_rows")
+        zeros = new_tile([P, P], F32, "zeros")
         bias = keep.tile([P, TILES], F32, name="bias")
-        turned_bias = psum.tile([P, BANK], F32, name="turned_bias", tag="spare1")
-        nc.tensor.transpose(turned_bias[:, :P], bias_rows[:], identity[:])
-        nc.scalar.copy(bias[:], turned_bias[:, :TILES])
+
+        def prepare():
+            make_identity(nc, identity[:])
+            nc.vector.memset(zeros[:], 0.0)
+            nc.scalar.activation(bias_rows[:], zeros[:], SILU)
+
+        def load_bias():
+            nc.sync.dma_start(bias_rows[:TILES, :], b.rearrange("(c p) -> c p", p=P))
+
+        def turn_bias():
+            turned_bias = psum.tile([P, BANK], F32, name="turned_bias", tag=BANK_OF["bias"])
+            nc.tensor.transpose(turned_bias[:, :P], bias_rows[:], identity[:])
+            nc.scalar.copy(bias[:], turned_bias[:, :TILES])
 
         v_words, v_scales, parts, codes, scales, acc, act = {}, {}, {}, {}, {}, {}, {}
+        masked, transposed, turned, returned = {}, {}, {}, {}
 
         def gather_words(a, cuts):
             v_words[a] = new_tile([P, S], U32, "v_words%d" % a)
@@ -139,87 +139,130 @@ def tile_list_tabres_silu_kernel(tc, tab_words, tab_scales, w, rT, b, offs, out)
             parts[a, tiles[0]] = new_tile([P, 2, len(tiles) * WIDE], BF16, "parts%d_%d" % (a, tiles[0]))
             return parts[a, tiles[0]]
 
-        def split_on_vector(a, tiles):
-            both = new_parts(a, tiles)
-            masked = new_tile([P, PACK, len(tiles) * P], F32, "masked")
-            nc.vector.tensor_scalar(masked[:].bitcast(I32), source(a, tiles).bitcast(I32), WORD_MASK, None, ALU.bitwise_and)
-            nc.vector.tensor_tensor(woven_by_rows(both[:, 1, :]), by_rows(source(a, tiles)), by_rows(masked[:]), ALU.subtract)
-            nc.vector.tensor_copy(woven_by_rows(both[:, 0, :]), by_rows(masked[:]))
+        def mask_words(a, tiles, *flip):
+            masked[a, tiles[0]] = new_tile([P, PACK, len(tiles) * P], F32, "masked%d_%d" % (a, tiles[0]))
+            if flip:
+                nc.vector.tensor_scalar(masked[a, tiles[0]][:].bitcast(I32), source(a, tiles).bitcast(I32), WORD_MASK, SIGN_BIT, ALU.bitwise_and, ALU.bitwise_xor)
+            else:
+                nc.vector.tensor_scalar(masked[a, tiles[0]][:].bitcast(I32), source(a, tiles).bitcast(I32), WORD_MASK, None, ALU.bitwise_and)
 
-        def make_hi(a, tiles):
-            upper = new_tile([P, len(tiles) * WIDE], BF16, "upper%d_%d" % (a, tiles[0]))
+        def hi_from_masked(a, tiles, sign):
             both = new_parts(a, tiles)
-            halves16 = source(a, tiles).bitcast(BF16).rearrange("p t (c i h) -> p c t i h", i=RUN, h=2)
-            nc.scalar.copy(woven_by_rows(upper[:]), halves16[:, :, :, :, 1])
-            nc.vector.tensor_scalar(both[:, 0, :].bitcast(I32), upper[:].bitcast(I32), PAIR_MASK, None, ALU.bitwise_and)
+            nc.scalar.activation(woven_by_rows(both[:, 0, :]), by_rows(masked[a, tiles[0]][:]), COPY, scale=sign)
 
-        def make_lo_on_vector(a, tiles):
+        def lo_from_masked(a, tiles):
             both = parts[a, tiles[0]]
-            nc.vector.tensor_tensor(woven_by_rows(both[:, 1, :]), by_rows(source(a, tiles)), woven_by_rows(both[:, 0, :]), ALU.subtract)
+            nc.gpsimd.tensor_tensor(
+                both[:, 1, :].rearrange("p (n t) -> p n t", t=PACK),
+                source(a, tiles).rearrange("p t n -> p n t"),
+                masked[a, tiles[0]][:].rearrange("p t n -> p n t"),
+                ALU.subtract,
+            )
 
-        def make_lo_on_gpsimd(a, tiles):
+        upper = {}
+
+        def copy_upper(a, tiles):
+            upper[a, tiles[0]] = new_tile([P, len(tiles) * WIDE], BF16, "upper%d_%d" % (a, tiles[0]))
+            halves16 = source(a, tiles).bitcast(BF16).rearrange("p t (c i h) -> p c t i h", i=RUN, h=2)
+            nc.scalar.copy(woven_by_rows(upper[a, tiles[0]][:]), halves16[:, :, :, :, 1])
+
+        def mask_pairs(a, tiles):
+            both = new_parts(a, tiles)
+            nc.vector.tensor_scalar(both[:, 0, :].bitcast(I32), upper[a, tiles[0]][:].bitcast(I32), PAIR_MASK, None, ALU.bitwise_and)
+
+        def lo_woven(a, tiles):
             both = parts[a, tiles[0]]
             woven = new_tile([P, len(tiles) * WIDE], F32, "woven%d_%d" % (a, tiles[0]))
             nc.scalar.copy(woven_by_rows(woven[:]), by_rows(source(a, tiles)))
             nc.gpsimd.tensor_tensor(both[:, 1, :], woven[:], both[:, 0, :], ALU.subtract)
 
-        transposed, minus_hi = {}, {}
+        def lo_strided(a, tiles):
+            both = parts[a, tiles[0]]
+            nc.gpsimd.tensor_tensor(
+                both[:, 1, :].rearrange("p (n t) -> p n t", t=PACK),
+                source(a, tiles).rearrange("p t n -> p n t"),
+                both[:, 0, :].rearrange("p (n t) -> p n t", t=PACK),
+                ALU.subtract,
+            )
 
         def subtract_on_tensor(a, tiles):
             src = source(a, tiles)
-            minus_hi[a] = new_tile([P, PACK, len(tiles) * P], F32, "minus_hi")
-            nc.vector.tensor_scalar(minus_hi[a][:].bitcast(I32), src.bitcast(I32), WORD_MASK, SIGN_BIT, ALU.bitwise_and, ALU.bitwise_xor)
             for m in range(len(tiles)):
                 cols = slice(m * P, (m + 1) * P)
-                transposed[m] = psum.tile([P, BANK], F32, name="transposed%d" % m, tag="spare%d" % m)
+                transposed[a, m] = psum.tile([P, BANK], F32, name="transposed%d_%d" % (a, m), tag=BANK_OF["forth", a, m])
                 for t in range(PACK):
-                    block = transposed[m][:, t * P : (t + 1) * P]
+                    block = transposed[a, m][:, t * P : (t + 1) * P]
                     nc.tensor.matmul(block, src[:, t, cols], identity[:], start=True, stop=False, is_transpose=True)
-                    nc.tensor.matmul(block, minus_hi[a][:, t, cols], identity[:], start=False, stop=True, is_transpose=True)
+                    nc.tensor.matmul(block, masked[a, tiles[0]][:, t, cols], identity[:], start=False, stop=True, is_transpose=True)
 
-        def turn_back(tiles):
-            turned = new_tile([P, len(tiles) * WIDE], BF16, "turned")
+        def round_turned(a, tiles):
+            turned[a] = new_tile([P, len(tiles) * WIDE], BF16, "turned%d" % a)
             for m in range(len(tiles)):
                 nc.scalar.copy(
-                    turned[:, m * WIDE : (m + 1) * WIDE].rearrange("n (u p e) -> n u p e", u=2, e=2),
-                    transposed[m][:].rearrange("n (u e p) -> n u p e", u=2, e=2),
-                )
-            for m in range(len(tiles)):
-                pairs = turned[:, m * WIDE : (m + 1) * WIDE].bitcast(F32)
-                for u in range(2):
-                    nc.tensor.transpose(transposed[m][:, u * P : (u + 1) * P], pairs[:, u * P : (u + 1) * P], identity[:])
-
-        def collect_parts(a, tiles):
-            both = new_parts(a, tiles)
-            nc.scalar.activation(woven_by_rows(both[:, 0, :]), by_rows(minus_hi[a][:]), COPY, scale=-1.0)
-            for m in range(len(tiles)):
-                nc.scalar.copy(
-                    both[:, 1, m * WIDE : (m + 1) * WIDE].bitcast(F32).rearrange("p (n u) -> p n u", u=2),
-                    transposed[m][:, : 2 * P].rearrange("p (u n) -> p n u", u=2),
+                    turned[a][:, m * WIDE : (m + 1) * WIDE].rearrange("n (u p e) -> n u p e", u=2, e=2),
+                    transposed[a, m][:].rearrange("n (u e p) -> n u p e", u=2, e=2),
                 )
 
-        def quantise(a, tiles):
-            span = 2 * P * len(tiles)
-            codes[a, tiles[0]] = new_tile([P, span], U32, "codes%d_%d" % (a, tiles[0]))
-            scales[a, tiles[0]] = new_tile([P, span], U8, "scales%d_%d" % (a, tiles[0]))
-            nc.vector.quantize_mx(
-                out=codes[a, tiles[0]][:].bitcast(FP8X4),
-                scales=scales[a, tiles[0]][:],
-                in_=parts[a, tiles[0]][:].rearrange("p s x -> p (s x)"),
+        def turn_back(a, tiles):
+            returned[a] = psum.tile([P, BANK], F32, name="returned%d" % a, tag=BANK_OF["back", a])
+            pairs = turned[a][:].bitcast(F32)
+            for j in range(2 * len(tiles)):
+                nc.tensor.transpose(returned[a][:, j * P : (j + 1) * P], pairs[:, j * P : (j + 1) * P], identity[:])
+
+        def collect(a, tiles):
+            nc.scalar.copy(
+                parts[a, tiles[0]][:, 1, :].bitcast(F32).rearrange("p (m n u) -> p m n u", m=len(tiles), u=2),
+                returned[a][:].rearrange("p (m u n) -> p m n u", m=len(tiles), u=2),
             )
 
-        def multiply(a, tiles, c, h):
-            if a == 0:
-                acc[c, h] = psum.tile([P, BANK], F32, name="acc%d_%d" % (c, h), tag="bank%d_%d" % (c % (TILES - 1), h))
-            for part in range(2):
-                at = (part * len(tiles) + tiles.index(c)) * P
+        operand, late = {}, {}
+
+        def quantise_values(name, values, places):
+            span = P * len(places)
+            codes[name] = new_tile([P, span], U32, "codes" + name)
+            scales[name] = new_tile([P, span], U8, "scales" + name)
+            nc.vector.quantize_mx(out=codes[name][:].bitcast(FP8X4), scales=scales[name][:], in_=values)
+            for n, place in enumerate(places):
+                operand[place] = (codes[name][:, n * P : (n + 1) * P], scales[name][:, n * P : (n + 1) * P])
+
+        def quantise(a, tiles):
+            places = [(a, c, part) for part in range(2) for c in tiles]
+            quantise_values("%d_%d" % (a, tiles[0]), parts[a, tiles[0]][:].rearrange("p s x -> p (s x)"), places)
+
+        def late_part(part, a):
+            if part not in late:
+                late[part] = new_tile([P, 2, len(SECOND) * WIDE], BF16, "late%d" % part)
+            return late[part][:, a - 1, :]
+
+        def quantise_late(part):
+            places = [(a, c, part) for a in (1, 2) for c in SECOND]
+            quantise_values("late%d" % part, late[part][:].rearrange("p s x -> p (s x)"), places)
+
+        def late_hi(a):
+            nc.scalar.activation(woven_by_rows(late_part(0, a)), by_rows(masked[a, SECOND[0]][:]), COPY, scale=-1.0)
+
+        def late_lo(a):
+            nc.scalar.copy(
+                late_part(1, a).bitcast(F32).rearrange("p (m n u) -> p m n u", m=len(SECOND), u=2),
+                returned[a][:].rearrange("p (m u n) -> p m n u", m=len(SECOND), u=2),
+            )
+
+        begun = set()
+
+        def multiply(a, c, h, which=(0, 1), last=False):
+            for part in which:
+                first = (c, h) not in begun
+                if first:
+                    acc[c, h] = psum.tile([P, BANK], F32, name="acc%d_%d" % (c, h), tag=BANK_OF[c, h])
+                    begun.add((c, h))
+                words, plane = operand[a, c, part]
                 nc.tensor.matmul_mx(
                     out=acc[c, h][:],
-                    lhsT=codes[a, tiles[0]][:, at : at + P].bitcast(FP8X4),
-                    lhsT_scale=scales[a, tiles[0]][:, at : at + P],
+                    lhsT=words.bitcast(FP8X4),
+                    lhsT_scale=plane,
                     rhs=v_words[a][:, h * BANK : (h + 1) * BANK].bitcast(FP8X4),
                     rhs_scale=v_scales[a][:, h * BANK : (h + 1) * BANK],
-                    start=(a == 0 and part == 0),
+                    start=first,
                     stop=(a == PASSES - 1 and part == 1),
                 )
 
@@ -238,52 +281,91 @@ def tile_list_tabres_silu_kernel(tc, tab_words, tab_scales, w, rT, b, offs, out)
                 nc.sync.dma_start(out[c * P : (c + 1) * P, cols], res[:, cols])
                 done += width
 
-        split_on_vector(0, (0,))
-        make_hi(0, (1,))
-        make_lo_on_vector(0, (1,))
-        quantise(0, (0,))
-        quantise(0, (1,))
-        make_hi(0, SECOND)
-        make_lo_on_gpsimd(0, SECOND)
-        gather_scales()
+        def lo_on_vector(a, tiles):
+            both = parts[a, tiles[0]]
+            nc.vector.tensor_tensor(woven_by_rows(both[:, 1, :]), by_rows(source(a, tiles)), by_rows(masked[a, tiles[0]][:]), ALU.subtract)
 
-        subtract_on_tensor(1, SECOND)
+        def gather_scales_cut(cuts):
+            gathered = new_tile([P, S], U8, "v_scales")
+            width = S // cuts
+            for n in range(cuts):
+                picks = offsets[:, n * width // GROUP : (n + 1) * width // GROUP]
+                nc.vector.tensor_copy(gathered[:, n * width : (n + 1) * width], scale_rows[:].bitcast(U8).indirect(picks))
+            for a in range(PASSES):
+                v_scales[a] = gathered[SCALE_ROWS * a : P, :]
+
+        def split_on_vector(a, tiles):
+            mask_words(a, tiles)
+            both = new_parts(a, tiles)
+            nc.vector.tensor_copy(woven_by_rows(both[:, 0, :]), by_rows(masked[a, tiles[0]][:]))
+            nc.vector.tensor_tensor(
+                both[:, 1, :].rearrange("p (c i t) -> p c t i", i=PACK, t=PACK),
+                source(a, tiles).rearrange("p t (c i) -> p c t i", i=PACK),
+                masked[a, tiles[0]][:].rearrange("p t (c i) -> p c t i", i=PACK),
+                ALU.subtract,
+            )
+
+        prepare()
+        load_weight(0, FIRST)
+        load_weight(0, SECOND)
+        nc.sync.dma_start(offsets[:], offs)
+        load_table(0)
+        load_weight(1, ALL)
+        for q in range(P // QUADRANT):
+            load_scale_rows(q, nc.sync)
+        load_bias()
+        load_weight(2, FIRST)
+        load_table(1)
+        load_weight(2, SECOND)
+        load_table(2)
+        for c in range(TILES):
+            load_resid(c)
+        split_on_vector(0, FIRST)
+        copy_upper(0, SECOND)
+        mask_pairs(0, SECOND)
+        quantise(0, FIRST)
+        lo_woven(0, SECOND)
+        gather_words(0, 1)
         quantise(0, SECOND)
-        make_hi(1, FIRST)
-        make_lo_on_gpsimd(1, FIRST)
-        gather_words(0, HALVES)
+        mask_words(1, SECOND, True)
+        copy_upper(1, FIRST)
+        mask_pairs(1, FIRST)
+        lo_woven(1, FIRST)
+        subtract_on_tensor(1, SECOND)
+        turn_bias()
+        gather_scales_cut(HALVES)
         for h in range(HALVES):
-            for c in FIRST:
-                multiply(0, (c,), c, h)
-        for h in range(HALVES):
-            multiply(0, SECOND, SECOND[0], h)
-
-        make_hi(2, FIRST)
-        make_lo_on_gpsimd(2, FIRST)
+            for c in (0, 1, 2):
+                multiply(0, c, h)
+        copy_upper(2, FIRST)
         quantise(1, FIRST)
+        mask_pairs(2, FIRST)
+        lo_woven(2, FIRST)
         gather_words(1, 1)
         for h in range(HALVES):
             for c in FIRST:
-                multiply(1, FIRST, c, h)
-        make_hi(2, SECOND)
-        make_lo_on_gpsimd(2, SECOND)
-        turn_back(SECOND)
-        collect_parts(1, SECOND)
+                multiply(1, c, h)
+        copy_upper(2, SECOND)
+        mask_pairs(2, SECOND)
+        lo_woven(2, SECOND)
+        round_turned(1, SECOND)
+        turn_back(1, SECOND)
+        hi_from_masked(1, SECOND, -1.0)
+        collect(1, SECOND)
         quantise(2, FIRST)
         gather_words(2, HALVES)
         for h in range(HALVES):
             for c in FIRST:
-                multiply(2, FIRST, c, h)
+                multiply(2, c, h)
         for c in FIRST:
             activate(c)
         quantise(2, SECOND)
         quantise(1, SECOND)
         for c in SECOND:
             for h in range(HALVES):
-                for a in range(1 if c == SECOND[0] else 0, PASSES):
-                    multiply(a, SECOND, c, h)
+                for a in range(1 if c == 2 else 0, PASSES):
+                    multiply(a, c, h)
             activate(c)
-
         finish(0, (BANK, BANK))
         finish(1, (S,))
         finish(2, (S,))

@@ -36,9 +36,9 @@ WORD_MASK = 0xFFF00000 - (1 << 32)
 SIGN_BIT = -(1 << 31)
 FIRST, SECOND, ALL = (0, 1), (2, 3), (0, 1, 2, 3)
 
-LIES_ON = {"v_words0": ("upper0_2", 0), "scales0_2": ("table0", 0), "v_scales": ("upper1_0", 0), "scales1_0": ("scale_rows", 0),
+LIES_ON = {"parts2_0": ("scale_rows", 1024), "v_words1": ("upper2_0", 0), "v_words0": ("upper0_2", 0), "scales0_2": ("table0", 0), "v_scales": ("upper1_0", 0), "scales1_0": ("scale_rows", 0),
     "turned1": ("upper2_2", -1536), "scales2_0": ("upper2_2", 512), "parts1_2": ("upper2_2", 1024)}
-ROOM = {"upper0_2": (0, 2048), "upper2_2": (1536, 3072)}
+ROOM = {"upper0_2": (0, 2048), "upper2_2": (1536, 3072), "scale_rows": (0, 3072), "upper2_0": (0, 2048)}
 BANK_OF = {"bias": "e", ("forth", 1, 0): "t0", ("forth", 1, 1): "t1", ("back", 1): "t0",
     (0, 0): "a", (0, 1): "b", (1, 0): "c", (1, 1): "d", (2, 0): "e", (2, 1): "f", (3, 0): "a", (3, 1): "b"}
 
@@ -305,14 +305,14 @@ def tile_list_tabres_silu_kernel(tc, tab_words, tab_scales, w, rT, b, offs, out)
                 ALU.subtract,
             )
 
-        prepare()
         load_weight(0, FIRST)
+        for q in range(P // QUADRANT):
+            load_scale_rows(q, nc.gpsimd)
+        prepare()
         load_weight(0, SECOND)
         nc.sync.dma_start(offsets[:], offs)
         load_table(0)
         load_weight(1, ALL)
-        for q in range(P // QUADRANT):
-            load_scale_rows(q, nc.sync)
         load_bias()
         load_weight(2, FIRST)
         load_table(1)

@@ -36,8 +36,11 @@ WORD_MASK = 0xFFF00000 - (1 << 32)
 SIGN_BIT = -(1 << 31)
 FIRST, SECOND, ALL = (0, 1), (2, 3), (0, 1, 2, 3)
 
-LIES_ON = {"parts2_0": ("scale_rows", 1024), "v_words1": ("upper2_0", 0), "v_words0": ("upper0_2", 0), "scales0_2": ("table0", 0), "v_scales": ("upper1_0", 0), "scales1_0": ("scale_rows", 0),
+LIES_ON = {"weight1_0": ("masked0_0_wide", 0), "weight2_0": ("parts0_0_wide", 0), "weight2_2": ("parts0_0_wide", 4096), "table1": ("parts0_0_wide", 8192), "table2": ("parts0_0_wide", 16384),
+    "resid0": ("parts0_0_wide", 24576), "resid1": ("parts0_0_wide", 32768), "resid2": ("parts0_0_wide", 40960), "resid3": ("parts0_0_wide", 49152),
+    "parts2_0": ("scale_rows", 1024), "v_words1": ("upper2_0", 0), "v_words0": ("upper0_2", 0), "scales0_2": ("table0", 0), "v_scales": ("upper1_0", 0), "scales1_0": ("scale_rows", 0),
     "turned1": ("upper2_2", -1536), "scales2_0": ("upper2_2", 512), "parts1_2": ("upper2_2", 1024)}
+COVERS = {"masked0_0": 8192, "parts0_0": 57344}
 ROOM = {"upper0_2": (0, 2048), "upper2_2": (1536, 3072), "scale_rows": (0, 3072), "upper2_0": (0, 2048)}
 BANK_OF = {"bias": "e", ("forth", 1, 0): "t0", ("forth", 1, 1): "t1", ("back", 1): "t0",
     (0, 0): "a", (0, 1): "b", (1, 0): "c", (1, 1): "d", (2, 0): "e", (2, 1): "f", (3, 0): "a", (3, 1): "b"}
@@ -55,6 +58,10 @@ def tile_list_tabres_silu_kernel(tc, tab_words, tab_scales, w, rT, b, offs, out)
             size = BYTES_OF[dtype]
             for n in shape[1:]:
                 size = size * n
+            if name in COVERS:
+                count = size // BYTES_OF[dtype]
+                whole = new_tile([P, COVERS[name] // BYTES_OF[dtype]], dtype, name + "_wide")
+                return whole[:, :count].rearrange("p (a b) -> p a b", a=shape[1])
             if name in LIES_ON:
                 older, shift = LIES_ON[name]
                 address[name] = address[older] + shift
@@ -298,12 +305,7 @@ def tile_list_tabres_silu_kernel(tc, tab_words, tab_scales, w, rT, b, offs, out)
             mask_words(a, tiles)
             both = new_parts(a, tiles)
             nc.vector.tensor_copy(woven_by_rows(both[:, 0, :]), by_rows(masked[a, tiles[0]][:]))
-            nc.vector.tensor_tensor(
-                both[:, 1, :].rearrange("p (c i t) -> p c t i", i=PACK, t=PACK),
-                source(a, tiles).rearrange("p t (c i) -> p c t i", i=PACK),
-                masked[a, tiles[0]][:].rearrange("p t (c i) -> p c t i", i=PACK),
-                ALU.subtract,
-            )
+            nc.vector.tensor_tensor(woven_by_rows(both[:, 1, :]), by_rows(source(a, tiles)), woven_by_rows(both[:, 0, :]), ALU.subtract)
 
         load_weight(0, FIRST)
         for q in range(P // QUADRANT):
@@ -312,18 +314,18 @@ def tile_list_tabres_silu_kernel(tc, tab_words, tab_scales, w, rT, b, offs, out)
         load_weight(0, SECOND)
         nc.sync.dma_start(offsets[:], offs)
         load_table(0)
-        load_weight(1, ALL)
         load_bias()
+        split_on_vector(0, FIRST)
+        load_weight(1, ALL)
+        copy_upper(0, SECOND)
+        mask_pairs(0, SECOND)
+        quantise(0, FIRST)
         load_weight(2, FIRST)
         load_table(1)
         load_weight(2, SECOND)
         load_table(2)
         for c in range(TILES):
             load_resid(c)
-        split_on_vector(0, FIRST)
-        copy_upper(0, SECOND)
-        mask_pairs(0, SECOND)
-        quantise(0, FIRST)
         lo_woven(0, SECOND)
         gather_words(0, 1)
         quantise(0, SECOND)

@@ -308,12 +308,12 @@ def tile_list_tabres_silu_kernel(tc, tab_words, tab_scales, w, rT, b, offs, out)
             nc.vector.tensor_tensor(woven_by_rows(both[:, 1, :]), by_rows(source(a, tiles)), woven_by_rows(both[:, 0, :]), ALU.subtract)
 
         load_weight(0, FIRST)
-        for q in range(P // QUADRANT):
-            load_scale_rows(q, nc.gpsimd)
         prepare()
         load_weight(0, SECOND)
         nc.sync.dma_start(offsets[:], offs)
         load_table(0)
+        for q in range(P // QUADRANT):
+            load_scale_rows(q, nc.sync)
         load_bias()
         split_on_vector(0, FIRST)
         load_weight(1, ALL)

@@ -36,12 +36,11 @@ WORD_MASK = 0xFFF00000 - (1 << 32)
 SIGN_BIT = -(1 << 31)
 FIRST, SECOND, ALL = (0, 1), (2, 3), (0, 1, 2, 3)
 
-LIES_ON = {"weight1_0": ("masked0_0_wide", 0), "weight2_0": ("parts0_0_wide", 0), "weight2_2": ("parts0_0_wide", 4096), "table1": ("parts0_0_wide", 8192), "table2": ("parts0_0_wide", 16384),
-    "resid0": ("parts0_0_wide", 24576), "resid1": ("parts0_0_wide", 32768), "resid2": ("parts0_0_wide", 40960), "resid3": ("parts0_0_wide", 49152),
-    "parts2_0": ("scale_rows", 1024), "v_words1": ("upper2_0", 0), "v_words0": ("upper0_2", 0), "scales0_2": ("table0", 0), "v_scales": ("upper1_0", 0), "scales1_0": ("scale_rows", 0),
+LIES_ON = {"v_words0": ("upper0_2", 0), "scales0_2": ("table0", 0), "v_scales": ("upper1_0", 0), "scales1_0": ("scale_rows", 0),
     "turned1": ("upper2_2", -1536), "scales2_0": ("upper2_2", 512), "parts1_2": ("upper2_2", 1024)}
-COVERS = {"masked0_0": 8192, "parts0_0": 57344}
-ROOM = {"upper0_2": (0, 2048), "upper2_2": (1536, 3072), "scale_rows": (0, 3072), "upper2_0": (0, 2048)}
+COVERS = {}
+LATE = (1, 2)
+ROOM = {"upper0_2": (0, 2048), "upper2_2": (1536, 3072)}
 BANK_OF = {"bias": "e", ("forth", 1, 0): "t0", ("forth", 1, 1): "t1", ("back", 1): "t0",
     (0, 0): "a", (0, 1): "b", (1, 0): "c", (1, 1): "d", (2, 0): "e", (2, 1): "f", (3, 0): "a", (3, 1): "b"}
 
@@ -239,10 +238,10 @@ def tile_list_tabres_silu_kernel(tc, tab_words, tab_scales, w, rT, b, offs, out)
         def late_part(part, a):
             if part not in late:
                 late[part] = new_tile([P, 2, len(SECOND) * WIDE], BF16, "late%d" % part)
-            return late[part][:, a - 1, :]
+            return late[part][:, LATE.index(a), :]
 
         def quantise_late(part):
-            places = [(a, c, part) for a in (1, 2) for c in SECOND]
+            places = [(a, c, part) for a in LATE for c in SECOND]
             quantise_values("late%d" % part, late[part][:].rearrange("p s x -> p (s x)"), places)
 
         def late_hi(a):
@@ -301,31 +300,39 @@ def tile_list_tabres_silu_kernel(tc, tab_words, tab_scales, w, rT, b, offs, out)
             for a in range(PASSES):
                 v_scales[a] = gathered[SCALE_ROWS * a : P, :]
 
-        def split_on_vector(a, tiles):
+        def split_alone(a, tiles):
             mask_words(a, tiles)
             both = new_parts(a, tiles)
+            nc.vector.tensor_tensor(woven_by_rows(both[:, 1, :]), by_rows(source(a, tiles)), by_rows(masked[a, tiles[0]][:]), ALU.subtract)
             nc.vector.tensor_copy(woven_by_rows(both[:, 0, :]), by_rows(masked[a, tiles[0]][:]))
+
+        def lo_from_hi(a, tiles):
+            both = parts[a, tiles[0]]
             nc.vector.tensor_tensor(woven_by_rows(both[:, 1, :]), by_rows(source(a, tiles)), woven_by_rows(both[:, 0, :]), ALU.subtract)
 
-        load_weight(0, FIRST)
         prepare()
+        load_weight(0, FIRST)
         load_weight(0, SECOND)
         nc.sync.dma_start(offsets[:], offs)
         load_table(0)
         for q in range(P // QUADRANT):
             load_scale_rows(q, nc.sync)
-        load_bias()
-        split_on_vector(0, FIRST)
         load_weight(1, ALL)
-        copy_upper(0, SECOND)
-        mask_pairs(0, SECOND)
-        quantise(0, FIRST)
+        load_bias()
         load_weight(2, FIRST)
         load_table(1)
         load_weight(2, SECOND)
         load_table(2)
         for c in range(TILES):
             load_resid(c)
+        split_alone(0, (0,))
+        copy_upper(0, (1,))
+        mask_pairs(0, (1,))
+        lo_from_hi(0, (1,))
+        quantise(0, (0,))
+        quantise(0, (1,))
+        copy_upper(0, SECOND)
+        mask_pairs(0, SECOND)
         lo_woven(0, SECOND)
         gather_words(0, 1)
         quantise(0, SECOND)

@@ -315,9 +315,9 @@ def tile_list_tabres_silu_kernel(tc, tab_words, tab_scales, w, rT, b, offs, out)
         load_weight(0, SECOND)
         nc.sync.dma_start(offsets[:], offs)
         load_table(0)
+        load_weight(1, ALL)
         for q in range(P // QUADRANT):
             load_scale_rows(q, nc.sync)
-        load_weight(1, ALL)
         load_bias()
         load_weight(2, FIRST)
         load_table(1)

@@ -36,7 +36,7 @@ WORD_MASK = 0xFFF00000 - (1 << 32)
 SIGN_BIT = -(1 << 31)
 FIRST, SECOND, ALL = (0, 1), (2, 3), (0, 1, 2, 3)
 
-LIES_ON = {"v_words0": ("upper0_2", 0), "scales0_2": ("table0", 0), "v_scales": ("upper1_0", 0), "scales1_0": ("scale_rows", 0),
+LIES_ON = {"v_words0": ("upper0_2", 0), "scales0_2": ("table0", 0), "scales1_0": ("scale_rows", 0),
     "turned1": ("upper2_2", -1536), "scales2_0": ("upper2_2", 512), "parts1_2": ("upper2_2", 1024)}
 COVERS = {}
 LATE = (1, 2)
@@ -315,10 +315,11 @@ def tile_list_tabres_silu_kernel(tc, tab_words, tab_scales, w, rT, b, offs, out)
         load_weight(0, SECOND)
         nc.sync.dma_start(offsets[:], offs)
         load_table(0)
+        load_bias()
+        turn_bias()
         load_weight(1, ALL)
         for q in range(P // QUADRANT):
             load_scale_rows(q, nc.sync)
-        load_bias()
         load_weight(2, FIRST)
         load_table(1)
         load_weight(2, SECOND)
@@ -341,7 +342,6 @@ def tile_list_tabres_silu_kernel(tc, tab_words, tab_scales, w, rT, b, offs, out)
         mask_pairs(1, FIRST)
         lo_woven(1, FIRST)
         subtract_on_tensor(1, SECOND)
-        turn_bias()
         gather_scales_cut(HALVES)
         for h in range(HALVES):
             for c in (0, 1, 2):

@@ -36,8 +36,7 @@ WORD_MASK = 0xFFF00000 - (1 << 32)
 SIGN_BIT = -(1 << 31)
 FIRST, SECOND, ALL = (0, 1), (2, 3), (0, 1, 2, 3)
 
-LIES_ON = {"v_words0": ("upper0_2", 0), "scales0_2": ("table0", 0), "scales1_0": ("scale_rows", 0),
-    "turned1": ("upper2_2", -1536), "scales2_0": ("upper2_2", 512), "parts1_2": ("upper2_2", 1024)}
+LIES_ON = {"turned1": ("upper2_2", -1536), "parts1_2": ("upper2_2", 1024)}
 COVERS = {}
 LATE = (1, 2)
 ROOM = {"upper0_2": (0, 2048), "upper2_2": (1536, 3072)}
@@ -300,15 +299,16 @@ def tile_list_tabres_silu_kernel(tc, tab_words, tab_scales, w, rT, b, offs, out)
             for a in range(PASSES):
                 v_scales[a] = gathered[SCALE_ROWS * a : P, :]
 
-        def split_alone(a, tiles):
-            mask_words(a, tiles)
-            both = new_parts(a, tiles)
-            nc.vector.tensor_tensor(woven_by_rows(both[:, 1, :]), by_rows(source(a, tiles)), by_rows(masked[a, tiles[0]][:]), ALU.subtract)
-            nc.vector.tensor_copy(woven_by_rows(both[:, 0, :]), by_rows(masked[a, tiles[0]][:]))
-
-        def lo_from_hi(a, tiles):
-            both = parts[a, tiles[0]]
-            nc.vector.tensor_tensor(woven_by_rows(both[:, 1, :]), by_rows(source(a, tiles)), woven_by_rows(both[:, 0, :]), ALU.subtract)
+        def split_first(a):
+            both = new_parts(a, FIRST)
+            hi = [both[:, 0, n * WIDE : (n + 1) * WIDE] for n in FIRST]
+            lo = [both[:, 1, n * WIDE : (n + 1) * WIDE] for n in FIRST]
+            for c in FIRST:
+                mask_words(a, (c,))
+            nc.scalar.copy(woven_by_rows(hi[0]), by_rows(masked[a, 0][:]))
+            for c in FIRST:
+                nc.vector.tensor_tensor(woven_by_rows(lo[c]), by_rows(source(a, (c,))), by_rows(masked[a, c][:]), ALU.subtract)
+            nc.vector.tensor_copy(woven_by_rows(hi[1]), by_rows(masked[a, 1][:]))
 
         prepare()
         load_weight(0, FIRST)
@@ -326,14 +326,10 @@ def tile_list_tabres_silu_kernel(tc, tab_words, tab_scales, w, rT, b, offs, out)
         load_table(2)
         for c in range(TILES):
             load_resid(c)
-        split_alone(0, (0,))
-        copy_upper(0, (1,))
-        mask_pairs(0, (1,))
-        lo_from_hi(0, (1,))
-        quantise(0, (0,))
-        quantise(0, (1,))
+        split_first(0)
         copy_upper(0, SECOND)
         mask_pairs(0, SECOND)
+        quantise(0, FIRST)
         lo_woven(0, SECOND)
         gather_words(0, 1)
         quantise(0, SECOND)
@@ -355,13 +351,13 @@ def tile_list_tabres_silu_kernel(tc, tab_words, tab_scales, w, rT, b, offs, out)
             for c in FIRST:
                 multiply(1, c, h)
         copy_upper(2, SECOND)
+        quantise(2, FIRST)
         mask_pairs(2, SECOND)
         lo_woven(2, SECOND)
         round_turned(1, SECOND)
         turn_back(1, SECOND)
         hi_from_masked(1, SECOND, -1.0)
         collect(1, SECOND)
-        quantise(2, FIRST)
         gather_words(2, HALVES)
         for h in range(HALVES):
             for c in FIRST:

@@ -306,9 +306,12 @@ def tile_list_tabres_silu_kernel(tc, tab_words, tab_scales, w, rT, b, offs, out)
             for c in FIRST:
                 mask_words(a, (c,))
             nc.scalar.copy(woven_by_rows(hi[0]), by_rows(masked[a, 0][:]))
-            for c in FIRST:
-                nc.vector.tensor_tensor(woven_by_rows(lo[c]), by_rows(source(a, (c,))), by_rows(masked[a, c][:]), ALU.subtract)
+            nc.vector.tensor_tensor(woven_by_rows(lo[0]), by_rows(source(a, (0,))), by_rows(masked[a, 0][:]), ALU.subtract)
             nc.vector.tensor_copy(woven_by_rows(hi[1]), by_rows(masked[a, 1][:]))
+            nc.vector.tensor_tensor(woven_by_rows(lo[1]), by_rows(source(a, (1,))), by_rows(masked[a, 1][:]), ALU.subtract)
+
+        def quantise_part(a, tiles, part):
+            quantise_values("%d_%d_%d" % (a, tiles[0], part), parts[a, tiles[0]][:, part, :], [(a, c, part) for c in tiles])
 
         prepare()
         load_weight(0, FIRST)
@@ -327,9 +330,10 @@ def tile_list_tabres_silu_kernel(tc, tab_words, tab_scales, w, rT, b, offs, out)
         for c in range(TILES):
             load_resid(c)
         split_first(0)
+        quantise_part(0, FIRST, 0)
         copy_upper(0, SECOND)
         mask_pairs(0, SECOND)
-        quantise(0, FIRST)
+        quantise_part(0, FIRST, 1)
         lo_woven(0, SECOND)
         gather_words(0, 1)
         quantise(0, SECOND)

@@ -36,12 +36,12 @@ WORD_MASK = 0xFFF00000 - (1 << 32)
 SIGN_BIT = -(1 << 31)
 FIRST, SECOND, ALL = (0, 1), (2, 3), (0, 1, 2, 3)
 
-LIES_ON = {"turned1": ("upper2_2", -1536), "parts1_2": ("upper2_2", 1024)}
+LIES_ON = {"scales2_0": ("table1", 0), "turned1": ("upper2_2", -1536), "parts1_2": ("upper2_2", 1024)}
 COVERS = {}
 LATE = (1, 2)
 ROOM = {"upper0_2": (0, 2048), "upper2_2": (1536, 3072)}
 BANK_OF = {"bias": "e", ("forth", 1, 0): "t0", ("forth", 1, 1): "t1", ("back", 1): "t0",
-    (0, 0): "a", (0, 1): "b", (1, 0): "c", (1, 1): "d", (2, 0): "e", (2, 1): "f", (3, 0): "a", (3, 1): "b"}
+    (0, 0): "a", (0, 1): "b", (1, 0): "c", (1, 1): "d", (2, 0): "a", (2, 1): "b", (3, 0): "c", (3, 1): "d"}
 
 
 def tile_list_tabres_silu_kernel(tc, tab_words, tab_scales, w, rT, b, offs, out):
@@ -320,10 +320,11 @@ def tile_list_tabres_silu_kernel(tc, tab_words, tab_scales, w, rT, b, offs, out)
         load_table(0)
         load_bias()
         turn_bias()
-        load_weight(1, ALL)
+        load_weight(1, FIRST)
         for q in range(P // QUADRANT):
             load_scale_rows(q, nc.sync)
         load_weight(2, FIRST)
+        load_weight(1, SECOND)
         load_table(1)
         load_weight(2, SECOND)
         load_table(2)
@@ -337,15 +338,15 @@ def tile_list_tabres_silu_kernel(tc, tab_words, tab_scales, w, rT, b, offs, out)
         lo_woven(0, SECOND)
         gather_words(0, 1)
         quantise(0, SECOND)
-        mask_words(1, SECOND, True)
         copy_upper(1, FIRST)
         mask_pairs(1, FIRST)
         lo_woven(1, FIRST)
-        subtract_on_tensor(1, SECOND)
         gather_scales_cut(HALVES)
         for h in range(HALVES):
-            for c in (0, 1, 2):
+            for c in FIRST:
                 multiply(0, c, h)
+        mask_words(1, SECOND, True)
+        subtract_on_tensor(1, SECOND)
         copy_upper(2, FIRST)
         quantise(1, FIRST)
         mask_pairs(2, FIRST)
@@ -372,7 +373,7 @@ def tile_list_tabres_silu_kernel(tc, tab_words, tab_scales, w, rT, b, offs, out)
         quantise(1, SECOND)
         for c in SECOND:
             for h in range(HALVES):
-                for a in range(1 if c == 2 else 0, PASSES):
+                for a in range(PASSES):
                     multiply(a, c, h)
             activate(c)
         finish(0, (BANK, BANK))

@@ -36,7 +36,7 @@ WORD_MASK = 0xFFF00000 - (1 << 32)
 SIGN_BIT = -(1 << 31)
 FIRST, SECOND, ALL = (0, 1), (2, 3), (0, 1, 2, 3)
 
-LIES_ON = {"scales2_0": ("table1", 0), "turned1": ("upper2_2", -1536), "parts1_2": ("upper2_2", 1024)}
+LIES_ON = {"turned1": ("upper2_2", -1536), "parts1_2": ("upper2_2", 1024)}
 COVERS = {}
 LATE = (1, 2)
 ROOM = {"upper0_2": (0, 2048), "upper2_2": (1536, 3072)}
@@ -313,6 +313,18 @@ def tile_list_tabres_silu_kernel(tc, tab_words, tab_scales, w, rT, b, offs, out)
         def quantise_part(a, tiles, part):
             quantise_values("%d_%d_%d" % (a, tiles[0], part), parts[a, tiles[0]][:, part, :], [(a, c, part) for c in tiles])
 
+        def split_woven(a, tiles):
+            both = new_parts(a, tiles)
+            woven = new_tile([P, len(tiles) * WIDE], F32, "woven%d_%d" % (a, tiles[0]))
+            high = new_tile([P, len(tiles) * WIDE], F32, "high%d_%d" % (a, tiles[0]))
+            nc.scalar.copy(woven_by_rows(woven[:]), by_rows(source(a, tiles)))
+            nc.vector.tensor_scalar(high[:].bitcast(I32), woven[:].bitcast(I32), WORD_MASK, None, ALU.bitwise_and)
+            return both, woven, high
+
+        def finish_woven(both, woven, high):
+            nc.gpsimd.tensor_tensor(both[:, 1, :], woven[:], high[:], ALU.subtract)
+            nc.scalar.copy(both[:, 0, :], high[:])
+
         prepare()
         load_weight(0, FIRST)
         load_weight(0, SECOND)
@@ -323,8 +335,8 @@ def tile_list_tabres_silu_kernel(tc, tab_words, tab_scales, w, rT, b, offs, out)
         load_weight(1, FIRST)
         for q in range(P // QUADRANT):
             load_scale_rows(q, nc.sync)
-        load_weight(2, FIRST)
         load_weight(1, SECOND)
+        load_weight(2, FIRST)
         load_table(1)
         load_weight(2, SECOND)
         load_table(2)
@@ -332,10 +344,9 @@ def tile_list_tabres_silu_kernel(tc, tab_words, tab_scales, w, rT, b, offs, out)
             load_resid(c)
         split_first(0)
         quantise_part(0, FIRST, 0)
-        copy_upper(0, SECOND)
-        mask_pairs(0, SECOND)
+        second = split_woven(0, SECOND)
         quantise_part(0, FIRST, 1)
-        lo_woven(0, SECOND)
+        finish_woven(*second)
         gather_words(0, 1)
         quantise(0, SECOND)
         copy_upper(1, FIRST)

@@ -325,6 +325,11 @@ def tile_list_tabres_silu_kernel(tc, tab_words, tab_scales, w, rT, b, offs, out)
             nc.gpsimd.tensor_tensor(both[:, 1, :], woven[:], high[:], ALU.subtract)
             nc.scalar.copy(both[:, 0, :], high[:])
 
+        def load_resid_part(c, first, last):
+            if c not in resid:
+                resid[c] = new_tile([P, T], F32, "resid%d" % c)
+            nc.sync.dma_start(resid[c][:, first:last], rT[c * P : (c + 1) * P, first:last])
+
         prepare()
         load_weight(0, FIRST)
         load_weight(0, SECOND)
@@ -337,10 +342,12 @@ def tile_list_tabres_silu_kernel(tc, tab_words, tab_scales, w, rT, b, offs, out)
             load_scale_rows(q, nc.sync)
         load_weight(1, SECOND)
         load_weight(2, FIRST)
+        load_resid_part(0, 0, T // 4)
         load_table(1)
         load_weight(2, SECOND)
         load_table(2)
-        for c in range(TILES):
+        load_resid_part(0, T // 4, T)
+        for c in range(1, TILES):
             load_resid(c)
         split_first(0)
         quantise_part(0, FIRST, 0)

@@ -41,7 +41,7 @@ COVERS = {}
 LATE = (1, 2)
 ROOM = {"upper0_2": (0, 2048), "upper2_2": (1536, 3072)}
 BANK_OF = {"bias": "e", ("forth", 1, 0): "t0", ("forth", 1, 1): "t1", ("back", 1): "t0",
-    (0, 0): "a", (0, 1): "b", (1, 0): "c", (1, 1): "d", (2, 0): "a", (2, 1): "b", (3, 0): "c", (3, 1): "d"}
+    (0, 0): "a", (0, 1): "b", (1, 0): "c", (1, 1): "d", (2, 0): "e", (2, 1): "f", (3, 0): "a", (3, 1): "b"}
 
 
 def tile_list_tabres_silu_kernel(tc, tab_words, tab_scales, w, rT, b, offs, out):
@@ -361,7 +361,7 @@ def tile_list_tabres_silu_kernel(tc, tab_words, tab_scales, w, rT, b, offs, out)
         lo_woven(1, FIRST)
         gather_scales_cut(HALVES)
         for h in range(HALVES):
-            for c in FIRST:
+            for c in (0, 1, 2):
                 multiply(0, c, h)
         mask_words(1, SECOND, True)
         subtract_on_tensor(1, SECOND)
@@ -391,7 +391,7 @@ def tile_list_tabres_silu_kernel(tc, tab_words, tab_scales, w, rT, b, offs, out)
         quantise(1, SECOND)
         for c in SECOND:
             for h in range(HALVES):
-                for a in range(PASSES):
+                for a in range(1 if c == 2 else 0, PASSES):
                     multiply(a, c, h)
             activate(c)
         finish(0, (BANK, BANK))

@@ -40,7 +40,7 @@ LIES_ON = {"turned1": ("upper2_2", -1536), "parts1_2": ("upper2_2", 1024)}
 COVERS = {}
 LATE = (1, 2)
 ROOM = {"upper0_2": (0, 2048), "upper2_2": (1536, 3072)}
-BANK_OF = {"bias": "e", ("forth", 1, 0): "t0", ("forth", 1, 1): "t1", ("back", 1): "t0",
+BANK_OF = {"warm": "e", "bias": "e", ("forth", 1, 0): "t0", ("forth", 1, 1): "t1", ("back", 1): "t0",
     (0, 0): "a", (0, 1): "b", (1, 0): "c", (1, 1): "d", (2, 0): "e", (2, 1): "f", (3, 0): "a", (3, 1): "b"}
 
 
@@ -330,6 +330,21 @@ def tile_list_tabres_silu_kernel(tc, tab_words, tab_scales, w, rT, b, offs, out)
                 resid[c] = new_tile([P, T], F32, "resid%d" % c)
             nc.sync.dma_start(resid[c][:, first:last], rT[c * P : (c + 1) * P, first:last])
 
+        def warm_up(passes):
+            scratch = psum.tile([P, BANK], F32, name="scratch", tag=BANK_OF["warm"])
+            words, plane = operand[0, 0, 0]
+            for n in range(passes):
+                cols = slice(n % 2 * BANK // 2, (n % 2 + 1) * BANK // 2)
+                nc.tensor.matmul_mx(
+                    out=scratch[:, cols],
+                    lhsT=words.bitcast(FP8X4),
+                    lhsT_scale=plane,
+                    rhs=v_words[0][:, cols].bitcast(FP8X4),
+                    rhs_scale=scales["0_0_0"][:],
+                    start=True,
+                    stop=True,
+                )
+
         prepare()
         load_weight(0, FIRST)
         load_weight(0, SECOND)
@@ -355,6 +370,7 @@ def tile_list_tabres_silu_kernel(tc, tab_words, tab_scales, w, rT, b, offs, out)
         quantise_part(0, FIRST, 1)
         finish_woven(*second)
         gather_words(0, 1)
+        warm_up(8)
         quantise(0, SECOND)
         copy_upper(1, FIRST)
         mask_pairs(1, FIRST)

@@ -345,6 +345,14 @@ def tile_list_tabres_silu_kernel(tc, tab_words, tab_scales, w, rT, b, offs, out)
                     stop=True,
                 )
 
+        def finish_once(c):
+            res = new_tile([P, S], F32, "res%d" % c)
+            for h in range(HALVES):
+                cols = slice(h * BANK, (h + 1) * BANK)
+                picks = offsets[:, h * BANK // GROUP : (h + 1) * BANK // GROUP]
+                nc.vector.tensor_tensor(res[:, cols], resid[c][:].indirect(picks), act[c][:, cols], ALU.add)
+            nc.sync.dma_start(out[c * P : (c + 1) * P, :], res[:])
+
         prepare()
         load_weight(0, FIRST)
         load_weight(0, SECOND)
@@ -356,13 +364,10 @@ def tile_list_tabres_silu_kernel(tc, tab_words, tab_scales, w, rT, b, offs, out)
         for q in range(P // QUADRANT):
             load_scale_rows(q, nc.sync)
         load_weight(1, SECOND)
-        load_weight(2, FIRST)
-        load_resid_part(0, 0, T // 4)
+        load_weight(2, ALL)
         load_table(1)
-        load_weight(2, SECOND)
         load_table(2)
-        load_resid_part(0, T // 4, T)
-        for c in range(1, TILES):
+        for c in range(TILES):
             load_resid(c)
         split_first(0)
         quantise_part(0, FIRST, 0)
@@ -410,7 +415,7 @@ def tile_list_tabres_silu_kernel(tc, tab_words, tab_scales, w, rT, b, offs, out)
                 for a in range(1 if c == 2 else 0, PASSES):
                     multiply(a, c, h)
             activate(c)
-        finish(0, (BANK, BANK))
+        finish_once(0)
         finish(1, (S,))
         finish(2, (S,))
         finish(3, (BANK, BANK // 2, BANK // 2))

@@ -41,7 +41,7 @@ COVERS = {}
 LATE = (1, 2)
 ROOM = {"upper0_2": (0, 2048), "upper2_2": (1536, 3072)}
 BANK_OF = {"warm": "e", "bias": "e", ("forth", 1, 0): "t0", ("forth", 1, 1): "t1", ("back", 1): "t0",
-    (0, 0): "a", (0, 1): "b", (1, 0): "c", (1, 1): "d", (2, 0): "e", (2, 1): "f", (3, 0): "a", (3, 1): "b"}
+    (0, 0): "a", (0, 1): "b", (1, 0): "c", (1, 1): "d", (2, 0): "e", (2, 1): "a", (3, 0): "b", (3, 1): "c"}
 
 
 def tile_list_tabres_silu_kernel(tc, tab_words, tab_scales, w, rT, b, offs, out):
@@ -353,6 +353,15 @@ def tile_list_tabres_silu_kernel(tc, tab_words, tab_scales, w, rT, b, offs, out)
                 nc.vector.tensor_tensor(res[:, cols], resid[c][:].indirect(picks), act[c][:, cols], ALU.add)
             nc.sync.dma_start(out[c * P : (c + 1) * P, :], res[:])
 
+        def subtract_tile(a, tiles, m):
+            src = source(a, tiles)
+            cols = slice(m * P, (m + 1) * P)
+            transposed[a, m] = psum.tile([P, BANK], F32, name="transposed%d_%d" % (a, m), tag=BANK_OF["forth", a, m])
+            for t in range(PACK):
+                block = transposed[a, m][:, t * P : (t + 1) * P]
+                nc.tensor.matmul(block, src[:, t, cols], identity[:], start=True, stop=False, is_transpose=True)
+                nc.tensor.matmul(block, masked[a, tiles[0]][:, t, cols], identity[:], start=False, stop=True, is_transpose=True)
+
         prepare()
         load_weight(0, FIRST)
         load_weight(0, SECOND)
@@ -380,10 +389,11 @@ def tile_list_tabres_silu_kernel(tc, tab_words, tab_scales, w, rT, b, offs, out)
         copy_upper(1, FIRST)
         mask_pairs(1, FIRST)
         lo_woven(1, FIRST)
-        gather_scales_cut(HALVES)
+        gather_scales_cut(1)
         for h in range(HALVES):
-            for c in (0, 1, 2):
+            for c in FIRST:
                 multiply(0, c, h)
+        multiply(0, 2, 0)
         mask_words(1, SECOND, True)
         subtract_on_tensor(1, SECOND)
         copy_upper(2, FIRST)
@@ -412,7 +422,7 @@ def tile_list_tabres_silu_kernel(tc, tab_words, tab_scales, w, rT, b, offs, out)
         quantise(1, SECOND)
         for c in SECOND:
             for h in range(HALVES):
-                for a in range(1 if c == 2 else 0, PASSES):
+                for a in range(1 if (c, h) == (2, 0) else 0, PASSES):
                     multiply(a, c, h)
             activate(c)
         finish_once(0)

@@ -332,7 +332,7 @@ def tile_list_tabres_silu_kernel(tc, tab_words, tab_scales, w, rT, b, offs, out)
 
         def warm_up(passes):
             scratch = psum.tile([P, BANK], F32, name="scratch", tag=BANK_OF["warm"])
-            words, plane = operand[0, 0, 0]
+            words, plane = operand[0, 2, 0]
             for n in range(passes):
                 cols = slice(n % 2 * BANK // 2, (n % 2 + 1) * BANK // 2)
                 nc.tensor.matmul_mx(
@@ -340,7 +340,7 @@ def tile_list_tabres_silu_kernel(tc, tab_words, tab_scales, w, rT, b, offs, out)
                     lhsT=words.bitcast(FP8X4),
                     lhsT_scale=plane,
                     rhs=v_words[0][:, cols].bitcast(FP8X4),
-                    rhs_scale=scales["0_0_0"][:],
+                    rhs_scale=scales["0_2"][:, : BANK // 2],
                     start=True,
                     stop=True,
                 )
@@ -384,8 +384,8 @@ def tile_list_tabres_silu_kernel(tc, tab_words, tab_scales, w, rT, b, offs, out)
         quantise_part(0, FIRST, 1)
         finish_woven(*second)
         gather_words(0, 1)
-        warm_up(8)
         quantise(0, SECOND)
+        warm_up(8)
         copy_upper(1, FIRST)
         mask_pairs(1, FIRST)
         lo_woven(1, FIRST)

@@ -16,7 +16,6 @@ FP8X4 = mybir.dt.float8_e4m3fn_x4
 ALU = mybir.AluOpType
 SILU = mybir.ActivationFunctionType.Silu
 COPY = mybir.ActivationFunctionType.Copy
-BYTES_OF = {F32: 4, BF16: 2, I32: 4, U32: 4, U8: 1}
 
 P = 128
 PACK = 4
@@ -35,13 +34,18 @@ PAIR_MASK = 0xFFF0FFF0 - (1 << 32)
 WORD_MASK = 0xFFF00000 - (1 << 32)
 SIGN_BIT = -(1 << 31)
 FIRST, SECOND, ALL = (0, 1), (2, 3), (0, 1, 2, 3)
+HI, LO = 0, 1
+WARM_WIDTH = BANK // 2
+WARM_PASSES = 8
 
-LIES_ON = {"turned1": ("upper2_2", -1536), "parts1_2": ("upper2_2", 1024)}
-COVERS = {}
-LATE = (1, 2)
-ROOM = {"upper0_2": (0, 2048), "upper2_2": (1536, 3072)}
-BANK_OF = {"warm": "e", "bias": "e", ("forth", 1, 0): "t0", ("forth", 1, 1): "t1", ("back", 1): "t0",
-    (0, 0): "a", (0, 1): "b", (1, 0): "c", (1, 1): "d", (2, 0): "e", (2, 1): "a", (3, 0): "b", (3, 1): "c"}
+PART_BYTES = len(SECOND) * WIDE * 2
+ON_LAST_MASK = {"turned": 0, "upper2_2": PART_BYTES // 2, "parts1_2": PART_BYTES}
+
+SUM_BANK = {
+    (0, 0): "sum0", (0, 1): "sum1", (1, 0): "sum2", (1, 1): "sum3",
+    (2, 0): "early", (2, 1): "sum0", (3, 0): "sum1", (3, 1): "sum2",
+}
+EARLY_SUM = (2, 0)
 
 
 def tile_list_tabres_silu_kernel(tc, tab_words, tab_scales, w, rT, b, offs, out):
@@ -49,33 +53,25 @@ def tile_list_tabres_silu_kernel(tc, tab_words, tab_scales, w, rT, b, offs, out)
     with ExitStack() as ctx:
         keep = ctx.enter_context(tc.tile_pool(name="keep", bufs=1))
         psum = ctx.enter_context(tc.psum_pool(name="psum", bufs=1))
-        placed = ctx.enter_context(tc.tile_pool(name="placed", bufs=1))
-        address = {"free": 0}
+        overlaid = ctx.enter_context(tc.tile_pool(name="overlaid", bufs=1))
 
         def new_tile(shape, dtype, name):
-            size = BYTES_OF[dtype]
-            for n in shape[1:]:
-                size = size * n
-            if name in COVERS:
-                count = size // BYTES_OF[dtype]
-                whole = new_tile([P, COVERS[name] // BYTES_OF[dtype]], dtype, name + "_wide")
-                return whole[:, :count].rearrange("p (a b) -> p a b", a=shape[1])
-            if name in LIES_ON:
-                older, shift = LIES_ON[name]
-                address[name] = address[older] + shift
-                before, behind = ROOM.get(older, (0, 0))
-                assert -before <= shift and address[name] + size <= address[older, "end"] + behind
-                assert address[name] < address[older, "end"] and address[name] + size > address[older]
-            else:
-                before, behind = ROOM.get(name, (0, 0))
-                address[name] = address["free"] + before
-                address["free"] = address[name] + -(-size // ALIGN) * ALIGN + behind
-            address[name, "end"] = address[name] + size
-            return placed.tile(shape, dtype, name=name, align_bytes=ALIGN, offset=address[name])
+            if name in ON_LAST_MASK:
+                return overlaid.tile(shape, dtype, name=name, align_bytes=ALIGN, offset=ON_LAST_MASK[name])
+            return keep.tile(shape, dtype, name=name, align_bytes=ALIGN)
 
         offsets = keep.tile([P, S // GROUP], U16, name="offsets")
+
         scale_rows = new_tile([P, T // WORD_BYTES], I32, "scale_rows")
         nc.vector.memset(scale_rows[:], 0)
+
+        identity = new_tile([P, P], F32, "identity")
+        make_identity(nc, identity[:])
+
+        bias_rows = new_tile([P, P], F32, "bias_rows")
+        zeros = new_tile([P, P], F32, "zeros")
+        nc.vector.memset(zeros[:], 0.0)
+        nc.scalar.activation(bias_rows[:], zeros[:], SILU)
 
         table, weight, resid = {}, {}, {}
 
@@ -84,45 +80,56 @@ def tile_list_tabres_silu_kernel(tc, tab_words, tab_scales, w, rT, b, offs, out)
             nc.sync.dma_start(table[a][:], tab_words[a].rearrange("p t i -> p (t i)").bitcast(I32))
 
         def load_weight(a, tiles):
-            weight[a, tiles[0]] = new_tile([P, PACK, len(tiles) * P], F32, "weight%d_%d" % (a, tiles[0]))
+            whole = new_tile([P, PACK, len(tiles) * P], F32, "weight%d_%d" % (a, tiles[0]))
             rows = w[a * P * PACK : (a + 1) * P * PACK, tiles[0] * P : (tiles[-1] + 1) * P]
-            nc.sync.dma_start(weight[a, tiles[0]][:], rows.rearrange("(p t) n -> p t n", t=PACK))
+            nc.sync.dma_start(whole[:], rows.rearrange("(p t) n -> p t n", t=PACK))
+            for piece in (FIRST, SECOND):
+                if piece[0] in tiles:
+                    start = (piece[0] - tiles[0]) * P
+                    weight[a, piece] = whole[:, :, start : start + len(piece) * P]
 
         def load_resid(c):
             resid[c] = new_tile([P, T], F32, "resid%d" % c)
             nc.sync.dma_start(resid[c][:], rT[c * P : (c + 1) * P, :])
 
-        def load_scale_rows(q, queue):
-            rows = scale_rows[QUADRANT * q : QUADRANT * q + SCALE_ROWS * PASSES, :]
-            queue.dma_start(rows, tab_scales[:, SCALE_ROWS * q : SCALE_ROWS * (q + 1), :].bitcast(I32))
+        def load_scale_rows():
+            for q in range(P // QUADRANT):
+                rows = scale_rows[QUADRANT * q : QUADRANT * q + SCALE_ROWS * PASSES, :]
+                nc.sync.dma_start(rows, tab_scales[:, SCALE_ROWS * q : SCALE_ROWS * (q + 1), :].bitcast(I32))
 
-        identity = new_tile([P, P], F32, "identity")
-        bias_rows = new_tile([P, P], F32, "bias_rows")
-        zeros = new_tile([P, P], F32, "zeros")
         bias = keep.tile([P, TILES], F32, name="bias")
-
-        def prepare():
-            make_identity(nc, identity[:])
-            nc.vector.memset(zeros[:], 0.0)
-            nc.scalar.activation(bias_rows[:], zeros[:], SILU)
 
         def load_bias():
             nc.sync.dma_start(bias_rows[:TILES, :], b.rearrange("(c p) -> c p", p=P))
-
-        def turn_bias():
-            turned_bias = psum.tile([P, BANK], F32, name="turned_bias", tag=BANK_OF["bias"])
+            turned_bias = psum.tile([P, BANK], F32, name="turned_bias", tag=SUM_BANK[EARLY_SUM])
             nc.tensor.transpose(turned_bias[:, :P], bias_rows[:], identity[:])
             nc.scalar.copy(bias[:], turned_bias[:, :TILES])
 
-        v_words, v_scales, parts, codes, scales, acc, act = {}, {}, {}, {}, {}, {}, {}
-        masked, transposed, turned, returned = {}, {}, {}, {}
+        load_weight(0, FIRST)
+        load_weight(0, SECOND)
+        nc.sync.dma_start(offsets[:], offs)
+        load_table(0)
+        load_bias()
+        load_weight(1, FIRST)
+        load_scale_rows()
+        load_weight(1, SECOND)
+        load_weight(2, ALL)
+        load_table(1)
+        load_table(2)
+        for c in range(TILES):
+            load_resid(c)
+
+        v_words, v_scales, parts, operand, acc, act = {}, {}, {}, {}, {}, {}
+
+        def listed(first, width):
+            return offsets[:, first // GROUP : (first + width) // GROUP]
 
         def gather_words(a, cuts):
             v_words[a] = new_tile([P, S], U32, "v_words%d" % a)
             width = S // cuts
             for n in range(cuts):
-                picks = offsets[:, n * width // GROUP : (n + 1) * width // GROUP]
-                nc.vector.tensor_copy(v_words[a][:, n * width : (n + 1) * width], table[a][:].bitcast(U32).indirect(picks))
+                window = table[a][:].bitcast(U32)
+                nc.vector.tensor_copy(v_words[a][:, n * width : (n + 1) * width], window.indirect(listed(n * width, width)))
 
         def gather_scales():
             gathered = new_tile([P, S], U8, "v_scales")
@@ -130,136 +137,110 @@ def tile_list_tabres_silu_kernel(tc, tab_words, tab_scales, w, rT, b, offs, out)
             for a in range(PASSES):
                 v_scales[a] = gathered[SCALE_ROWS * a : P, :]
 
-        def source(a, tiles):
-            first = max(f for (n, f) in weight if n == a and f <= tiles[0])
-            return weight[a, first][:, :, (tiles[0] - first) * P : (tiles[-1] + 1 - first) * P]
-
         def by_rows(rows):
             return rows.rearrange("p t (c i) -> p c t i", i=RUN)
 
         def woven_by_rows(values):
             return values.rearrange("p (c i t) -> p c t i", i=RUN, t=PACK)
 
-        def new_parts(a, tiles):
-            parts[a, tiles[0]] = new_tile([P, 2, len(tiles) * WIDE], BF16, "parts%d_%d" % (a, tiles[0]))
-            return parts[a, tiles[0]]
+        def new_parts(a, piece):
+            parts[a, piece] = new_tile([P, 2, len(piece) * WIDE], BF16, "parts%d_%d" % (a, piece[0]))
+            return parts[a, piece]
 
-        def mask_words(a, tiles, *flip):
-            masked[a, tiles[0]] = new_tile([P, PACK, len(tiles) * P], F32, "masked%d_%d" % (a, tiles[0]))
-            if flip:
-                nc.vector.tensor_scalar(masked[a, tiles[0]][:].bitcast(I32), source(a, tiles).bitcast(I32), WORD_MASK, SIGN_BIT, ALU.bitwise_and, ALU.bitwise_xor)
-            else:
-                nc.vector.tensor_scalar(masked[a, tiles[0]][:].bitcast(I32), source(a, tiles).bitcast(I32), WORD_MASK, None, ALU.bitwise_and)
+        def mask_bits(target, values, mask):
+            nc.vector.tensor_scalar(target.bitcast(I32), values.bitcast(I32), mask, None, ALU.bitwise_and)
 
-        def hi_from_masked(a, tiles, sign):
-            both = new_parts(a, tiles)
-            nc.scalar.activation(woven_by_rows(both[:, 0, :]), by_rows(masked[a, tiles[0]][:]), COPY, scale=sign)
+        def weave(a, piece):
+            woven = new_tile([P, len(piece) * WIDE], F32, "woven%d_%d" % (a, piece[0]))
+            nc.scalar.copy(woven_by_rows(woven[:]), by_rows(weight[a, piece]))
+            return woven
 
-        def lo_from_masked(a, tiles):
-            both = parts[a, tiles[0]]
-            nc.gpsimd.tensor_tensor(
-                both[:, 1, :].rearrange("p (n t) -> p n t", t=PACK),
-                source(a, tiles).rearrange("p t n -> p n t"),
-                masked[a, tiles[0]][:].rearrange("p t n -> p n t"),
-                ALU.subtract,
+        def quantise(a, piece, which=(HI, LO)):
+            places = [(a, c, part) for part in which for c in piece]
+            name = "%d_%d_%d" % (a, piece[0], which[-1])
+            words = new_tile([P, P * len(places)], U32, "words" + name)
+            scales = new_tile([P, P * len(places)], U8, "scales" + name)
+            values = parts[a, piece][:, which[0] : which[-1] + 1, :].rearrange("p s x -> p (s x)")
+            nc.vector.quantize_mx(out=words[:].bitcast(FP8X4), scales=scales[:], in_=values)
+            for n, place in enumerate(places):
+                operand[place] = (words[:, n * P : (n + 1) * P], scales[:, n * P : (n + 1) * P])
+            return scales
+
+        def split_on_vector(a, piece):
+            both = new_parts(a, piece)
+            rows = [weight[a, piece][:, :, n * P : (n + 1) * P] for n in range(len(piece))]
+            high = [new_tile([P, PACK, P], F32, "high%d_%d" % (a, c)) for c in piece]
+            hi, lo = ([both[:, part, n * WIDE : (n + 1) * WIDE] for n in range(len(piece))] for part in (HI, LO))
+            for n in range(len(piece)):
+                mask_bits(high[n][:], rows[n], WORD_MASK)
+            nc.scalar.copy(woven_by_rows(hi[0]), by_rows(high[0][:]))
+            nc.vector.tensor_tensor(woven_by_rows(lo[0]), by_rows(rows[0]), by_rows(high[0][:]), ALU.subtract)
+            nc.vector.tensor_copy(woven_by_rows(hi[1]), by_rows(high[1][:]))
+            nc.vector.tensor_tensor(woven_by_rows(lo[1]), by_rows(rows[1]), by_rows(high[1][:]), ALU.subtract)
+
+        def copy_upper(a, piece):
+            upper = new_tile([P, len(piece) * WIDE], BF16, "upper%d_%d" % (a, piece[0]))
+            halves = weight[a, piece].bitcast(BF16).rearrange("p t (c i h) -> p c t i h", i=RUN, h=2)
+            nc.scalar.copy(woven_by_rows(upper[:]), halves[:, :, :, :, 1])
+            return upper
+
+        def split_beside_gather(a, piece, upper):
+            both = new_parts(a, piece)
+            mask_bits(both[:, HI, :], upper[:], PAIR_MASK)
+            nc.gpsimd.tensor_tensor(both[:, LO, :], weave(a, piece)[:], both[:, HI, :], ALU.subtract)
+
+        def subtract_on_tensor(a, piece):
+            negated = new_tile([P, PACK, len(piece) * P], F32, "negated")
+            nc.vector.tensor_scalar(
+                negated[:].bitcast(I32), weight[a, piece].bitcast(I32), WORD_MASK, SIGN_BIT, ALU.bitwise_and, ALU.bitwise_xor
             )
-
-        upper = {}
-
-        def copy_upper(a, tiles):
-            upper[a, tiles[0]] = new_tile([P, len(tiles) * WIDE], BF16, "upper%d_%d" % (a, tiles[0]))
-            halves16 = source(a, tiles).bitcast(BF16).rearrange("p t (c i h) -> p c t i h", i=RUN, h=2)
-            nc.scalar.copy(woven_by_rows(upper[a, tiles[0]][:]), halves16[:, :, :, :, 1])
-
-        def mask_pairs(a, tiles):
-            both = new_parts(a, tiles)
-            nc.vector.tensor_scalar(both[:, 0, :].bitcast(I32), upper[a, tiles[0]][:].bitcast(I32), PAIR_MASK, None, ALU.bitwise_and)
-
-        def lo_woven(a, tiles):
-            both = parts[a, tiles[0]]
-            woven = new_tile([P, len(tiles) * WIDE], F32, "woven%d_%d" % (a, tiles[0]))
-            nc.scalar.copy(woven_by_rows(woven[:]), by_rows(source(a, tiles)))
-            nc.gpsimd.tensor_tensor(both[:, 1, :], woven[:], both[:, 0, :], ALU.subtract)
-
-        def lo_strided(a, tiles):
-            both = parts[a, tiles[0]]
-            nc.gpsimd.tensor_tensor(
-                both[:, 1, :].rearrange("p (n t) -> p n t", t=PACK),
-                source(a, tiles).rearrange("p t n -> p n t"),
-                both[:, 0, :].rearrange("p (n t) -> p n t", t=PACK),
-                ALU.subtract,
-            )
-
-        def subtract_on_tensor(a, tiles):
-            src = source(a, tiles)
-            for m in range(len(tiles)):
+            banks = []
+            for m in range(len(piece)):
                 cols = slice(m * P, (m + 1) * P)
-                transposed[a, m] = psum.tile([P, BANK], F32, name="transposed%d_%d" % (a, m), tag=BANK_OF["forth", a, m])
+                banks.append(psum.tile([P, BANK], F32, name="transposed%d" % m, tag="turn%d" % m))
                 for t in range(PACK):
-                    block = transposed[a, m][:, t * P : (t + 1) * P]
-                    nc.tensor.matmul(block, src[:, t, cols], identity[:], start=True, stop=False, is_transpose=True)
-                    nc.tensor.matmul(block, masked[a, tiles[0]][:, t, cols], identity[:], start=False, stop=True, is_transpose=True)
+                    block = banks[m][:, t * P : (t + 1) * P]
+                    nc.tensor.matmul(block, weight[a, piece][:, t, cols], identity[:], start=True, stop=False, is_transpose=True)
+                    nc.tensor.matmul(block, negated[:, t, cols], identity[:], start=False, stop=True, is_transpose=True)
+            return negated, banks
 
-        def round_turned(a, tiles):
-            turned[a] = new_tile([P, len(tiles) * WIDE], BF16, "turned%d" % a)
-            for m in range(len(tiles)):
+        def collect_from_tensor(a, piece, negated, banks):
+            turned = new_tile([P, len(piece) * WIDE], BF16, "turned")
+            for m in range(len(piece)):
                 nc.scalar.copy(
-                    turned[a][:, m * WIDE : (m + 1) * WIDE].rearrange("n (u p e) -> n u p e", u=2, e=2),
-                    transposed[a, m][:].rearrange("n (u e p) -> n u p e", u=2, e=2),
+                    turned[:, m * WIDE : (m + 1) * WIDE].rearrange("n (u p e) -> n u p e", u=2, e=2),
+                    banks[m][:].rearrange("n (u e p) -> n u p e", u=2, e=2),
+                )
+            returned = psum.tile([P, BANK], F32, name="returned", tag="turn0")
+            pairs = turned[:].bitcast(F32)
+            for j in range(2 * len(piece)):
+                nc.tensor.transpose(returned[:, j * P : (j + 1) * P], pairs[:, j * P : (j + 1) * P], identity[:])
+            both = new_parts(a, piece)
+            nc.scalar.activation(woven_by_rows(both[:, HI, :]), by_rows(negated[:]), COPY, scale=-1.0)
+            nc.scalar.copy(
+                both[:, LO, :].bitcast(F32).rearrange("p (m n u) -> p m n u", m=len(piece), u=2),
+                returned[:].rearrange("p (m u n) -> p m n u", m=len(piece), u=2),
+            )
+
+        def warm_up(scales):
+            scratch = psum.tile([P, BANK], F32, name="scratch", tag=SUM_BANK[EARLY_SUM])
+            words, plane = operand[0, SECOND[0], HI]
+            for n in range(WARM_PASSES):
+                cols = slice(n % 2 * WARM_WIDTH, (n % 2 + 1) * WARM_WIDTH)
+                nc.tensor.matmul_mx(
+                    out=scratch[:, cols],
+                    lhsT=words.bitcast(FP8X4),
+                    lhsT_scale=plane,
+                    rhs=v_words[0][:, cols].bitcast(FP8X4),
+                    rhs_scale=scales[:, :WARM_WIDTH],
+                    start=True,
+                    stop=True,
                 )
 
-        def turn_back(a, tiles):
-            returned[a] = psum.tile([P, BANK], F32, name="returned%d" % a, tag=BANK_OF["back", a])
-            pairs = turned[a][:].bitcast(F32)
-            for j in range(2 * len(tiles)):
-                nc.tensor.transpose(returned[a][:, j * P : (j + 1) * P], pairs[:, j * P : (j + 1) * P], identity[:])
-
-        def collect(a, tiles):
-            nc.scalar.copy(
-                parts[a, tiles[0]][:, 1, :].bitcast(F32).rearrange("p (m n u) -> p m n u", m=len(tiles), u=2),
-                returned[a][:].rearrange("p (m u n) -> p m n u", m=len(tiles), u=2),
-            )
-
-        operand, late = {}, {}
-
-        def quantise_values(name, values, places):
-            span = P * len(places)
-            codes[name] = new_tile([P, span], U32, "codes" + name)
-            scales[name] = new_tile([P, span], U8, "scales" + name)
-            nc.vector.quantize_mx(out=codes[name][:].bitcast(FP8X4), scales=scales[name][:], in_=values)
-            for n, place in enumerate(places):
-                operand[place] = (codes[name][:, n * P : (n + 1) * P], scales[name][:, n * P : (n + 1) * P])
-
-        def quantise(a, tiles):
-            places = [(a, c, part) for part in range(2) for c in tiles]
-            quantise_values("%d_%d" % (a, tiles[0]), parts[a, tiles[0]][:].rearrange("p s x -> p (s x)"), places)
-
-        def late_part(part, a):
-            if part not in late:
-                late[part] = new_tile([P, 2, len(SECOND) * WIDE], BF16, "late%d" % part)
-            return late[part][:, LATE.index(a), :]
-
-        def quantise_late(part):
-            places = [(a, c, part) for a in LATE for c in SECOND]
-            quantise_values("late%d" % part, late[part][:].rearrange("p s x -> p (s x)"), places)
-
-        def late_hi(a):
-            nc.scalar.activation(woven_by_rows(late_part(0, a)), by_rows(masked[a, SECOND[0]][:]), COPY, scale=-1.0)
-
-        def late_lo(a):
-            nc.scalar.copy(
-                late_part(1, a).bitcast(F32).rearrange("p (m n u) -> p m n u", m=len(SECOND), u=2),
-                returned[a][:].rearrange("p (m u n) -> p m n u", m=len(SECOND), u=2),
-            )
-
-        begun = set()
-
-        def multiply(a, c, h, which=(0, 1), last=False):
-            for part in which:
-                first = (c, h) not in begun
-                if first:
-                    acc[c, h] = psum.tile([P, BANK], F32, name="acc%d_%d" % (c, h), tag=BANK_OF[c, h])
-                    begun.add((c, h))
+        def multiply(a, c, h):
+            if a == 0:
+                acc[c, h] = psum.tile([P, BANK], F32, name="acc%d_%d" % (c, h), tag=SUM_BANK[c, h])
+            for part in (HI, LO):
                 words, plane = operand[a, c, part]
                 nc.tensor.matmul_mx(
                     out=acc[c, h][:],
@@ -267,165 +248,72 @@ def tile_list_tabres_silu_kernel(tc, tab_words, tab_scales, w, rT, b, offs, out)
                     lhsT_scale=plane,
                     rhs=v_words[a][:, h * BANK : (h + 1) * BANK].bitcast(FP8X4),
                     rhs_scale=v_scales[a][:, h * BANK : (h + 1) * BANK],
-                    start=first,
-                    stop=(a == PASSES - 1 and part == 1),
+                    start=(a == 0 and part == HI),
+                    stop=(a == PASSES - 1 and part == LO),
                 )
+
+        def multiply_first_tiles(a):
+            for h in range(HALVES):
+                for c in FIRST:
+                    multiply(a, c, h)
 
         def activate(c):
             act[c] = new_tile([P, S], F32, "act%d" % c)
             for h in range(HALVES):
                 nc.scalar.activation(act[c][:, h * BANK : (h + 1) * BANK], acc[c, h][:], SILU, bias=bias[:, c : c + 1])
 
-        def finish(c, widths):
+        def finish(c, stores):
             res = new_tile([P, S], F32, "res%d" % c)
             done = 0
-            for width in widths:
-                cols = slice(done, done + width)
-                picks = offsets[:, done // GROUP : (done + width) // GROUP]
-                nc.vector.tensor_tensor(res[:, cols], resid[c][:].indirect(picks), act[c][:, cols], ALU.add)
-                nc.sync.dma_start(out[c * P : (c + 1) * P, cols], res[:, cols])
-                done += width
+            for widths in stores:
+                first = done
+                for width in widths:
+                    cols = slice(done, done + width)
+                    nc.vector.tensor_tensor(res[:, cols], resid[c][:].indirect(listed(done, width)), act[c][:, cols], ALU.add)
+                    done += width
+                nc.sync.dma_start(out[c * P : (c + 1) * P, first:done], res[:, first:done])
 
-        def lo_on_vector(a, tiles):
-            both = parts[a, tiles[0]]
-            nc.vector.tensor_tensor(woven_by_rows(both[:, 1, :]), by_rows(source(a, tiles)), by_rows(masked[a, tiles[0]][:]), ALU.subtract)
-
-        def gather_scales_cut(cuts):
-            gathered = new_tile([P, S], U8, "v_scales")
-            width = S // cuts
-            for n in range(cuts):
-                picks = offsets[:, n * width // GROUP : (n + 1) * width // GROUP]
-                nc.vector.tensor_copy(gathered[:, n * width : (n + 1) * width], scale_rows[:].bitcast(U8).indirect(picks))
-            for a in range(PASSES):
-                v_scales[a] = gathered[SCALE_ROWS * a : P, :]
-
-        def split_first(a):
-            both = new_parts(a, FIRST)
-            hi = [both[:, 0, n * WIDE : (n + 1) * WIDE] for n in FIRST]
-            lo = [both[:, 1, n * WIDE : (n + 1) * WIDE] for n in FIRST]
-            for c in FIRST:
-                mask_words(a, (c,))
-            nc.scalar.copy(woven_by_rows(hi[0]), by_rows(masked[a, 0][:]))
-            nc.vector.tensor_tensor(woven_by_rows(lo[0]), by_rows(source(a, (0,))), by_rows(masked[a, 0][:]), ALU.subtract)
-            nc.vector.tensor_copy(woven_by_rows(hi[1]), by_rows(masked[a, 1][:]))
-            nc.vector.tensor_tensor(woven_by_rows(lo[1]), by_rows(source(a, (1,))), by_rows(masked[a, 1][:]), ALU.subtract)
-
-        def quantise_part(a, tiles, part):
-            quantise_values("%d_%d_%d" % (a, tiles[0], part), parts[a, tiles[0]][:, part, :], [(a, c, part) for c in tiles])
-
-        def split_woven(a, tiles):
-            both = new_parts(a, tiles)
-            woven = new_tile([P, len(tiles) * WIDE], F32, "woven%d_%d" % (a, tiles[0]))
-            high = new_tile([P, len(tiles) * WIDE], F32, "high%d_%d" % (a, tiles[0]))
-            nc.scalar.copy(woven_by_rows(woven[:]), by_rows(source(a, tiles)))
-            nc.vector.tensor_scalar(high[:].bitcast(I32), woven[:].bitcast(I32), WORD_MASK, None, ALU.bitwise_and)
-            return both, woven, high
-
-        def finish_woven(both, woven, high):
-            nc.gpsimd.tensor_tensor(both[:, 1, :], woven[:], high[:], ALU.subtract)
-            nc.scalar.copy(both[:, 0, :], high[:])
-
-        def load_resid_part(c, first, last):
-            if c not in resid:
-                resid[c] = new_tile([P, T], F32, "resid%d" % c)
-            nc.sync.dma_start(resid[c][:, first:last], rT[c * P : (c + 1) * P, first:last])
-
-        def warm_up(passes):
-            scratch = psum.tile([P, BANK], F32, name="scratch", tag=BANK_OF["warm"])
-            words, plane = operand[0, 2, 0]
-            for n in range(passes):
-                cols = slice(n % 2 * BANK // 2, (n % 2 + 1) * BANK // 2)
-                nc.tensor.matmul_mx(
-                    out=scratch[:, cols],
-                    lhsT=words.bitcast(FP8X4),
-                    lhsT_scale=plane,
-                    rhs=v_words[0][:, cols].bitcast(FP8X4),
-                    rhs_scale=scales["0_2"][:, : BANK // 2],
-                    start=True,
-                    stop=True,
-                )
-
-        def finish_once(c):
-            res = new_tile([P, S], F32, "res%d" % c)
-            for h in range(HALVES):
-                cols = slice(h * BANK, (h + 1) * BANK)
-                picks = offsets[:, h * BANK // GROUP : (h + 1) * BANK // GROUP]
-                nc.vector.tensor_tensor(res[:, cols], resid[c][:].indirect(picks), act[c][:, cols], ALU.add)
-            nc.sync.dma_start(out[c * P : (c + 1) * P, :], res[:])
-
-        def subtract_tile(a, tiles, m):
-            src = source(a, tiles)
-            cols = slice(m * P, (m + 1) * P)
-            transposed[a, m] = psum.tile([P, BANK], F32, name="transposed%d_%d" % (a, m), tag=BANK_OF["forth", a, m])
-            for t in range(PACK):
-                block = transposed[a, m][:, t * P : (t + 1) * P]
-                nc.tensor.matmul(block, src[:, t, cols], identity[:], start=True, stop=False, is_transpose=True)
-                nc.tensor.matmul(block, masked[a, tiles[0]][:, t, cols], identity[:], start=False, stop=True, is_transpose=True)
-
-        prepare()
-        load_weight(0, FIRST)
-        load_weight(0, SECOND)
-        nc.sync.dma_start(offsets[:], offs)
-        load_table(0)
-        load_bias()
-        turn_bias()
-        load_weight(1, FIRST)
-        for q in range(P // QUADRANT):
-            load_scale_rows(q, nc.sync)
-        load_weight(1, SECOND)
-        load_weight(2, ALL)
-        load_table(1)
-        load_table(2)
-        for c in range(TILES):
-            load_resid(c)
-        split_first(0)
-        quantise_part(0, FIRST, 0)
-        second = split_woven(0, SECOND)
-        quantise_part(0, FIRST, 1)
-        finish_woven(*second)
+        split_on_vector(0, FIRST)
+        quantise(0, FIRST, (HI,))
+        both = new_parts(0, SECOND)
+        woven = weave(0, SECOND)
+        high = new_tile([P, len(SECOND) * WIDE], F32, "high0_2")
+        mask_bits(high[:], woven[:], WORD_MASK)
+        quantise(0, FIRST, (LO,))
+        nc.gpsimd.tensor_tensor(both[:, LO, :], woven[:], high[:], ALU.subtract)
+        nc.scalar.copy(both[:, HI, :], high[:])
         gather_words(0, 1)
-        quantise(0, SECOND)
-        warm_up(8)
-        copy_upper(1, FIRST)
-        mask_pairs(1, FIRST)
-        lo_woven(1, FIRST)
-        gather_scales_cut(1)
-        for h in range(HALVES):
-            for c in FIRST:
-                multiply(0, c, h)
-        multiply(0, 2, 0)
-        mask_words(1, SECOND, True)
-        subtract_on_tensor(1, SECOND)
-        copy_upper(2, FIRST)
+        warm_up(quantise(0, SECOND))
+
+        split_beside_gather(1, FIRST, copy_upper(1, FIRST))
+        gather_scales()
+        multiply_first_tiles(0)
+        multiply(0, *EARLY_SUM)
+        on_tensor = subtract_on_tensor(1, SECOND)
+
+        upper = copy_upper(2, FIRST)
         quantise(1, FIRST)
-        mask_pairs(2, FIRST)
-        lo_woven(2, FIRST)
+        split_beside_gather(2, FIRST, upper)
         gather_words(1, 1)
-        for h in range(HALVES):
-            for c in FIRST:
-                multiply(1, c, h)
-        copy_upper(2, SECOND)
+        multiply_first_tiles(1)
+        upper = copy_upper(2, SECOND)
         quantise(2, FIRST)
-        mask_pairs(2, SECOND)
-        lo_woven(2, SECOND)
-        round_turned(1, SECOND)
-        turn_back(1, SECOND)
-        hi_from_masked(1, SECOND, -1.0)
-        collect(1, SECOND)
+        split_beside_gather(2, SECOND, upper)
+        collect_from_tensor(1, SECOND, *on_tensor)
+
         gather_words(2, HALVES)
-        for h in range(HALVES):
-            for c in FIRST:
-                multiply(2, c, h)
+        multiply_first_tiles(2)
         for c in FIRST:
             activate(c)
         quantise(2, SECOND)
         quantise(1, SECOND)
         for c in SECOND:
             for h in range(HALVES):
-                for a in range(1 if (c, h) == (2, 0) else 0, PASSES):
+                for a in range(1 if (c, h) == EARLY_SUM else 0, PASSES):
                     multiply(a, c, h)
             activate(c)
-        finish_once(0)
-        finish(1, (S,))
-        finish(2, (S,))
-        finish(3, (BANK, BANK // 2, BANK // 2))
+
+        finish(0, [(BANK, BANK)])
+        finish(1, [(S,)])
+        finish(2, [(S,)])
+        finish(3, [(BANK,), (BANK // 2,), (BANK // 2,)])

@@ -43,7 +43,7 @@ ON_LAST_MASK = {"turned": 0, "upper2_2": PART_BYTES // 2, "parts1_2": PART_BYTES
 
 SUM_BANK = {
     (0, 0): "sum0", (0, 1): "sum1", (1, 0): "sum2", (1, 1): "sum3",
-    (2, 0): "early", (2, 1): "sum0", (3, 0): "sum1", (3, 1): "sum2",
+    (2, 0): "early", (2, 1): "early1", (3, 0): "sum0", (3, 1): "sum1",
 }
 EARLY_SUM = (2, 0)
 
@@ -133,7 +133,8 @@ def tile_list_tabres_silu_kernel(tc, tab_words, tab_scales, w, rT, b, offs, out)
 
         def gather_scales():
             gathered = new_tile([P, S], U8, "v_scales")
-            nc.vector.tensor_copy(gathered[:], scale_rows[:].bitcast(U8).indirect(offsets[:]))
+            for h in range(HALVES):
+                nc.vector.tensor_copy(gathered[:, h * BANK : (h + 1) * BANK], scale_rows[:].bitcast(U8).indirect(listed(h * BANK, BANK)))
             for a in range(PASSES):
                 v_scales[a] = gathered[SCALE_ROWS * a : P, :]
 
@@ -288,7 +289,8 @@ def tile_list_tabres_silu_kernel(tc, tab_words, tab_scales, w, rT, b, offs, out)
         split_beside_gather(1, FIRST, copy_upper(1, FIRST))
         gather_scales()
         multiply_first_tiles(0)
-        multiply(0, *EARLY_SUM)
+        for h in range(HALVES):
+            multiply(0, 2, h)
         on_tensor = subtract_on_tensor(1, SECOND)
 
         upper = copy_upper(2, FIRST)
@@ -309,7 +311,7 @@ def tile_list_tabres_silu_kernel(tc, tab_words, tab_scales, w, rT, b, offs, out)
         quantise(1, SECOND)
         for c in SECOND:
             for h in range(HALVES):
-                for a in range(1 if (c, h) == EARLY_SUM else 0, PASSES):
+                for a in range(1 if c == 2 else 0, PASSES):
                     multiply(a, c, h)
             activate(c)
 

@@ -46,6 +46,7 @@ SUM_BANK = {
     (2, 0): "early", (2, 1): "early1", (3, 0): "sum0", (3, 1): "sum1",
 }
 EARLY_SUM = (2, 0)
+LATE_SUM = (1, 1)
 
 
 def tile_list_tabres_silu_kernel(tc, tab_words, tab_scales, w, rT, b, offs, out):
@@ -250,13 +251,14 @@ def tile_list_tabres_silu_kernel(tc, tab_words, tab_scales, w, rT, b, offs, out)
                     rhs=v_words[a][:, h * BANK : (h + 1) * BANK].bitcast(FP8X4),
                     rhs_scale=v_scales[a][:, h * BANK : (h + 1) * BANK],
                     start=(a == 0 and part == HI),
-                    stop=(a == PASSES - 1 and part == LO),
+                    stop=(a == (1 if (c, h) == LATE_SUM else PASSES - 1) and part == LO),
                 )
 
         def multiply_first_tiles(a):
             for h in range(HALVES):
                 for c in FIRST:
-                    multiply(a, c, h)
+                    if (a, (c, h)) != (1, LATE_SUM):
+                        multiply(a, c, h)
 
         def activate(c):
             act[c] = new_tile([P, S], F32, "act%d" % c)
@@ -305,6 +307,7 @@ def tile_list_tabres_silu_kernel(tc, tab_words, tab_scales, w, rT, b, offs, out)
 
         gather_words(2, HALVES)
         multiply_first_tiles(2)
+        multiply(1, *LATE_SUM)
         for c in FIRST:
             activate(c)
         quantise(2, SECOND)

@@ -36,7 +36,7 @@ SIGN_BIT = -(1 << 31)
 FIRST, SECOND, ALL = (0, 1), (2, 3), (0, 1, 2, 3)
 HI, LO = 0, 1
 WARM_WIDTH = BANK // 2
-WARM_PASSES = 8
+WARM_PASSES = 6
 
 PART_BYTES = len(SECOND) * WIDE * 2
 ON_LAST_MASK = {"turned": 0, "upper2_2": PART_BYTES // 2, "parts1_2": PART_BYTES}

@@ -36,7 +36,7 @@ SIGN_BIT = -(1 << 31)
 FIRST, SECOND, ALL = (0, 1), (2, 3), (0, 1, 2, 3)
 HI, LO = 0, 1
 WARM_WIDTH = BANK // 2
-WARM_PASSES = 6
+WARM_PASSES = 4
 
 PART_BYTES = len(SECOND) * WIDE * 2
 ON_LAST_MASK = {"turned": 0, "upper2_2": PART_BYTES // 2, "parts1_2": PART_BYTES}

@@ -35,8 +35,6 @@ WORD_MASK = 0xFFF00000 - (1 << 32)
 SIGN_BIT = -(1 << 31)
 FIRST, SECOND, ALL = (0, 1), (2, 3), (0, 1, 2, 3)
 HI, LO = 0, 1
-WARM_WIDTH = BANK // 2
-WARM_PASSES = 4
 
 PART_BYTES = len(SECOND) * WIDE * 2
 ON_LAST_MASK = {"turned": 0, "upper2_2": PART_BYTES // 2, "parts1_2": PART_BYTES}
@@ -166,7 +164,6 @@ def tile_list_tabres_silu_kernel(tc, tab_words, tab_scales, w, rT, b, offs, out)
             nc.vector.quantize_mx(out=words[:].bitcast(FP8X4), scales=scales[:], in_=values)
             for n, place in enumerate(places):
                 operand[place] = (words[:, n * P : (n + 1) * P], scales[:, n * P : (n + 1) * P])
-            return scales
 
         def split_on_vector(a, piece):
             both = new_parts(a, piece)
@@ -224,21 +221,6 @@ def tile_list_tabres_silu_kernel(tc, tab_words, tab_scales, w, rT, b, offs, out)
                 returned[:].rearrange("p (m u n) -> p m n u", m=len(piece), u=2),
             )
 
-        def warm_up(scales):
-            scratch = psum.tile([P, BANK], F32, name="scratch", tag=SUM_BANK[EARLY_SUM])
-            words, plane = operand[0, SECOND[0], HI]
-            for n in range(WARM_PASSES):
-                cols = slice(n % 2 * WARM_WIDTH, (n % 2 + 1) * WARM_WIDTH)
-                nc.tensor.matmul_mx(
-                    out=scratch[:, cols],
-                    lhsT=words.bitcast(FP8X4),
-                    lhsT_scale=plane,
-                    rhs=v_words[0][:, cols].bitcast(FP8X4),
-                    rhs_scale=scales[:, :WARM_WIDTH],
-                    start=True,
-                    stop=True,
-                )
-
         def multiply(a, c, h):
             if a == 0:
                 acc[c, h] = psum.tile([P, BANK], F32, name="acc%d_%d" % (c, h), tag=SUM_BANK[c, h])
@@ -286,7 +268,7 @@ def tile_list_tabres_silu_kernel(tc, tab_words, tab_scales, w, rT, b, offs, out)
         nc.gpsimd.tensor_tensor(both[:, LO, :], woven[:], high[:], ALU.subtract)
         nc.scalar.copy(both[:, HI, :], high[:])
         gather_words(0, 1)
-        warm_up(quantise(0, SECOND))
+        quantise(0, SECOND)
 
         split_beside_gather(1, FIRST, copy_upper(1, FIRST))
         gather_scales()

@@ -44,7 +44,7 @@ SUM_BANK = {
     (2, 0): "early", (2, 1): "early1", (3, 0): "sum0", (3, 1): "sum1",
 }
 EARLY_SUM = (2, 0)
-LATE_SUM = (1, 1)
+LATE_TILE = 1
 
 
 def tile_list_tabres_silu_kernel(tc, tab_words, tab_scales, w, rT, b, offs, out):
@@ -233,14 +233,13 @@ def tile_list_tabres_silu_kernel(tc, tab_words, tab_scales, w, rT, b, offs, out)
                     rhs=v_words[a][:, h * BANK : (h + 1) * BANK].bitcast(FP8X4),
                     rhs_scale=v_scales[a][:, h * BANK : (h + 1) * BANK],
                     start=(a == 0 and part == HI),
-                    stop=(a == (1 if (c, h) == LATE_SUM else PASSES - 1) and part == LO),
+                    stop=(a == (1 if c == LATE_TILE else PASSES - 1) and part == LO),
                 )
 
         def multiply_first_tiles(a):
             for h in range(HALVES):
                 for c in FIRST:
-                    if (a, (c, h)) != (1, LATE_SUM):
-                        multiply(a, c, h)
+                    multiply(a, c, h)
 
         def activate(c):
             act[c] = new_tile([P, S], F32, "act%d" % c)
@@ -281,7 +280,8 @@ def tile_list_tabres_silu_kernel(tc, tab_words, tab_scales, w, rT, b, offs, out)
         quantise(1, FIRST)
         split_beside_gather(2, FIRST, upper)
         gather_words(1, 1)
-        multiply_first_tiles(1)
+        for h in range(HALVES):
+            multiply(1, 0, h)
         upper = copy_upper(2, SECOND)
         quantise(2, FIRST)
         split_beside_gather(2, SECOND, upper)
@@ -289,7 +289,8 @@ def tile_list_tabres_silu_kernel(tc, tab_words, tab_scales, w, rT, b, offs, out)
 
         gather_words(2, HALVES)
         multiply_first_tiles(2)
-        multiply(1, *LATE_SUM)
+        for h in range(HALVES):
+            multiply(1, LATE_TILE, h)
         for c in FIRST:
             activate(c)
         quantise(2, SECOND)

@@ -186,6 +186,11 @@ def tile_list_tabres_silu_kernel(tc, tab_words, tab_scales, w, rT, b, offs, out)
         def split_beside_gather(a, piece, upper):
             both = new_parts(a, piece)
             mask_bits(both[:, HI, :], upper[:], PAIR_MASK)
+            if (a, piece) == (1, FIRST):
+                nc.gpsimd.tensor_tensor(
+                    woven_by_rows(both[:, LO, :]), by_rows(weight[a, piece]), woven_by_rows(both[:, HI, :]), ALU.subtract
+                )
+                return
             nc.gpsimd.tensor_tensor(both[:, LO, :], weave(a, piece)[:], both[:, HI, :], ALU.subtract)
 
         def subtract_on_tensor(a, piece):

@@ -37,7 +37,7 @@ FIRST, SECOND, ALL = (0, 1), (2, 3), (0, 1, 2, 3)
 HI, LO = 0, 1
 
 PART_BYTES = len(SECOND) * WIDE * 2
-ON_LAST_MASK = {"turned": 0, "upper2_2": PART_BYTES // 2, "parts1_2": PART_BYTES}
+ON_LAST_MASK = {"turned": 0, "upper2_2": PART_BYTES // 2, "parts1_2": PART_BYTES, "parts0_0": 4 * PART_BYTES, "second_lo": 4 * PART_BYTES}
 
 SUM_BANK = {
     (0, 0): "sum0", (0, 1): "sum1", (1, 0): "sum2", (1, 1): "sum3",
@@ -118,6 +118,7 @@ def tile_list_tabres_silu_kernel(tc, tab_words, tab_scales, w, rT, b, offs, out)
         for c in range(TILES):
             load_resid(c)
 
+        planes = {}
         v_words, v_scales, parts, operand, acc, act = {}, {}, {}, {}, {}, {}
 
         def listed(first, width):
@@ -183,13 +184,22 @@ def tile_list_tabres_silu_kernel(tc, tab_words, tab_scales, w, rT, b, offs, out)
             nc.scalar.copy(woven_by_rows(upper[:]), halves[:, :, :, :, 1])
             return upper
 
+        def subtract_by_pairs(a, piece, hi, lo):
+            nc.gpsimd.tensor_tensor(woven_by_rows(lo), by_rows(weight[a, piece]), woven_by_rows(hi), ALU.subtract)
+
+        def quantise_units(values, places, name):
+            words = new_tile([P, P * len(places)], U32, "words_" + name)
+            scales = new_tile([P, P * len(places)], U8, "scales_" + name)
+            planes[name] = scales
+            nc.vector.quantize_mx(out=words[:].bitcast(FP8X4), scales=scales[:], in_=values)
+            for n, place in enumerate(places):
+                operand[place] = (words[:, n * P : (n + 1) * P], scales[:, n * P : (n + 1) * P])
+
         def split_beside_gather(a, piece, upper):
             both = new_parts(a, piece)
             mask_bits(both[:, HI, :], upper[:], PAIR_MASK)
             if (a, piece) == (1, FIRST):
-                nc.gpsimd.tensor_tensor(
-                    woven_by_rows(both[:, LO, :]), by_rows(weight[a, piece]), woven_by_rows(both[:, HI, :]), ALU.subtract
-                )
+                subtract_by_pairs(a, piece, both[:, HI, :], both[:, LO, :])
                 return
             nc.gpsimd.tensor_tensor(both[:, LO, :], weave(a, piece)[:], both[:, HI, :], ALU.subtract)
 
@@ -262,19 +272,43 @@ def tile_list_tabres_silu_kernel(tc, tab_words, tab_scales, w, rT, b, offs, out)
                     done += width
                 nc.sync.dma_start(out[c * P : (c + 1) * P, first:done], res[:, first:done])
 
-        split_on_vector(0, FIRST)
+        both = new_parts(0, FIRST)
+        rows = [weight[0, FIRST][:, :, n * P : (n + 1) * P] for n in FIRST]
+        high = [new_tile([P, PACK, P], F32, "high0_%d" % c) for c in FIRST]
+        hi, lo = ([both[:, part, n * WIDE : (n + 1) * WIDE] for n in FIRST] for part in (HI, LO))
+        for n in FIRST:
+            mask_bits(high[n][:], rows[n], WORD_MASK)
+            nc.scalar.copy(woven_by_rows(hi[n]), by_rows(high[n][:]))
+        nc.vector.tensor_tensor(woven_by_rows(lo[0]), by_rows(rows[0]), by_rows(high[0][:]), ALU.subtract)
+        both_high = new_tile([P, len(SECOND), PACK, P], F32, "second_high")
+        second_high = [both_high[:, n] for n in range(len(SECOND))]
+        for n in range(len(SECOND)):
+            mask_bits(second_high[n][:], weight[0, SECOND][:, :, n * P : (n + 1) * P], WORD_MASK)
+        nc.vector.tensor_tensor(woven_by_rows(lo[1]), by_rows(rows[1]), woven_by_rows(hi[1]), ALU.subtract)
+        second_hi = new_tile([P, len(SECOND) * WIDE], BF16, "second_hi")
+        for n in range(len(SECOND)):
+            nc.scalar.copy(woven_by_rows(second_hi[:, n * WIDE : (n + 1) * WIDE]), by_rows(second_high[n][:]))
         quantise(0, FIRST, (HI,))
-        both = new_parts(0, SECOND)
-        woven = weave(0, SECOND)
-        high = new_tile([P, len(SECOND) * WIDE], F32, "high0_2")
-        mask_bits(high[:], woven[:], WORD_MASK)
         quantise(0, FIRST, (LO,))
-        nc.gpsimd.tensor_tensor(both[:, LO, :], woven[:], high[:], ALU.subtract)
-        nc.scalar.copy(both[:, HI, :], high[:])
+        quantise_units(second_hi[:], [(0, c, HI) for c in SECOND], "second_hi")
+        second_lo = new_tile([P, len(SECOND) * WIDE], BF16, "second_lo")
+        subtract_by_pairs(0, SECOND, second_hi[:], second_lo[:])
         gather_words(0, 1)
-        quantise(0, SECOND)
+        quantise_units(second_lo[:], [(0, c, LO) for c in SECOND], "second_lo")
 
         split_beside_gather(1, FIRST, copy_upper(1, FIRST))
+        idle = psum.tile([P, BANK], F32, name="idle", tag=SUM_BANK[EARLY_SUM])
+        words, plane = operand[0, 2, HI]
+        for n in range(8):
+            nc.tensor.matmul_mx(
+                out=idle[:, : BANK // 2],
+                lhsT=words.bitcast(FP8X4),
+                lhsT_scale=plane,
+                rhs=v_words[0][:, : BANK // 2].bitcast(FP8X4),
+                rhs_scale=planes["second_hi"][:, : BANK // 2],
+                start=True,
+                stop=True,
+            )
         gather_scales()
         multiply_first_tiles(0)
         for h in range(HALVES):

@@ -37,7 +37,11 @@ FIRST, SECOND, ALL = (0, 1), (2, 3), (0, 1, 2, 3)
 HI, LO = 0, 1
 
 PART_BYTES = len(SECOND) * WIDE * 2
-ON_LAST_MASK = {"turned": 0, "upper2_2": PART_BYTES // 2, "parts1_2": PART_BYTES, "parts0_0": 4 * PART_BYTES, "second_lo": 4 * PART_BYTES}
+ON_LAST_MASK = {
+    "woven2_2": 0, "upper2_0": 3840, "upper2_2": 5632, "turned": 4096, "parts1_2": 6144,
+    "parts0_0": 12288, "second_lo": 12288,
+    "table1": 16384, "words2_0_1": 16384,
+}
 
 SUM_BANK = {
     (0, 0): "sum0", (0, 1): "sum1", (1, 0): "sum2", (1, 1): "sum3",
@@ -198,7 +202,7 @@ def tile_list_tabres_silu_kernel(tc, tab_words, tab_scales, w, rT, b, offs, out)
         def split_beside_gather(a, piece, upper):
             both = new_parts(a, piece)
             mask_bits(both[:, HI, :], upper[:], PAIR_MASK)
-            if (a, piece) == (1, FIRST):
+            if piece == FIRST:
                 subtract_by_pairs(a, piece, both[:, HI, :], both[:, LO, :])
                 return
             nc.gpsimd.tensor_tensor(both[:, LO, :], weave(a, piece)[:], both[:, HI, :], ALU.subtract)
@@ -322,8 +326,8 @@ def tile_list_tabres_silu_kernel(tc, tab_words, tab_scales, w, rT, b, offs, out)
         for h in range(HALVES):
             multiply(1, 0, h)
         upper = copy_upper(2, SECOND)
-        quantise(2, FIRST)
         split_beside_gather(2, SECOND, upper)
+        quantise(2, FIRST)
         collect_from_tensor(1, SECOND, *on_tensor)
 
         gather_words(2, HALVES)

@@ -207,13 +207,15 @@ def tile_list_tabres_silu_kernel(tc, tab_words, tab_scales, w, rT, b, offs, out)
                 return
             nc.gpsimd.tensor_tensor(both[:, LO, :], weave(a, piece)[:], both[:, HI, :], ALU.subtract)
 
-        def subtract_on_tensor(a, piece):
+        def subtract_on_tensor(a, piece, between):
             negated = new_tile([P, PACK, len(piece) * P], F32, "negated")
             nc.vector.tensor_scalar(
                 negated[:].bitcast(I32), weight[a, piece].bitcast(I32), WORD_MASK, SIGN_BIT, ALU.bitwise_and, ALU.bitwise_xor
             )
             banks = []
             for m in range(len(piece)):
+                if m:
+                    between()
                 cols = slice(m * P, (m + 1) * P)
                 banks.append(psum.tile([P, BANK], F32, name="transposed%d" % m, tag="turn%d" % m))
                 for t in range(PACK):
@@ -315,9 +317,7 @@ def tile_list_tabres_silu_kernel(tc, tab_words, tab_scales, w, rT, b, offs, out)
             )
         gather_scales()
         multiply_first_tiles(0)
-        for h in range(HALVES):
-            multiply(0, 2, h)
-        on_tensor = subtract_on_tensor(1, SECOND)
+        on_tensor = subtract_on_tensor(1, SECOND, lambda: [multiply(0, 2, h) for h in range(HALVES)])
 
         upper = copy_upper(2, FIRST)
         quantise(1, FIRST)

@@ -35,19 +35,26 @@ WORD_MASK = 0xFFF00000 - (1 << 32)
 SIGN_BIT = -(1 << 31)
 FIRST, SECOND, ALL = (0, 1), (2, 3), (0, 1, 2, 3)
 HI, LO = 0, 1
+WARM_UP = 4
 
-PART_BYTES = len(SECOND) * WIDE * 2
-ON_LAST_MASK = {
-    "woven2_2": 0, "upper2_0": 3840, "upper2_2": 5632, "turned": 4096, "parts1_2": 6144,
-    "parts0_0": 12288, "second_lo": 12288,
-    "table1": 16384, "words2_0_1": 16384,
+PART = len(FIRST) * WIDE * 2
+SHARED = {
+    "woven2_2": 0,
+    "upper2_0": 2 * PART - ALIGN,
+    "upper2_2": 3 * PART - 2 * ALIGN,
+    "turned": 2 * PART,
+    "parts1_2": 3 * PART,
+    "parts0_0": 6 * PART,
+    "second_lo": 6 * PART,
+    "table1": 8 * PART,
+    "words2_0_1": 8 * PART,
 }
 
 SUM_BANK = {
     (0, 0): "sum0", (0, 1): "sum1", (1, 0): "sum2", (1, 1): "sum3",
     (2, 0): "early", (2, 1): "early1", (3, 0): "sum0", (3, 1): "sum1",
 }
-EARLY_SUM = (2, 0)
+EARLY_TILE = 2
 LATE_TILE = 1
 
 
@@ -59,8 +66,8 @@ def tile_list_tabres_silu_kernel(tc, tab_words, tab_scales, w, rT, b, offs, out)
         overlaid = ctx.enter_context(tc.tile_pool(name="overlaid", bufs=1))
 
         def new_tile(shape, dtype, name):
-            if name in ON_LAST_MASK:
-                return overlaid.tile(shape, dtype, name=name, align_bytes=ALIGN, offset=ON_LAST_MASK[name])
+            if name in SHARED:
+                return overlaid.tile(shape, dtype, name=name, align_bytes=ALIGN, offset=SHARED[name])
             return keep.tile(shape, dtype, name=name, align_bytes=ALIGN)
 
         offsets = keep.tile([P, S // GROUP], U16, name="offsets")
@@ -104,7 +111,7 @@ def tile_list_tabres_silu_kernel(tc, tab_words, tab_scales, w, rT, b, offs, out)
 
         def load_bias():
             nc.sync.dma_start(bias_rows[:TILES, :], b.rearrange("(c p) -> c p", p=P))
-            turned_bias = psum.tile([P, BANK], F32, name="turned_bias", tag=SUM_BANK[EARLY_SUM])
+            turned_bias = psum.tile([P, BANK], F32, name="turned_bias", tag=SUM_BANK[EARLY_TILE, 0])
             nc.tensor.transpose(turned_bias[:, :P], bias_rows[:], identity[:])
             nc.scalar.copy(bias[:], turned_bias[:, :TILES])
 
@@ -122,7 +129,6 @@ def tile_list_tabres_silu_kernel(tc, tab_words, tab_scales, w, rT, b, offs, out)
         for c in range(TILES):
             load_resid(c)
 
-        planes = {}
         v_words, v_scales, parts, operand, acc, act = {}, {}, {}, {}, {}, {}
 
         def listed(first, width):
@@ -137,8 +143,9 @@ def tile_list_tabres_silu_kernel(tc, tab_words, tab_scales, w, rT, b, offs, out)
 
         def gather_scales():
             gathered = new_tile([P, S], U8, "v_scales")
+            window = scale_rows[:].bitcast(U8)
             for h in range(HALVES):
-                nc.vector.tensor_copy(gathered[:, h * BANK : (h + 1) * BANK], scale_rows[:].bitcast(U8).indirect(listed(h * BANK, BANK)))
+                nc.vector.tensor_copy(gathered[:, h * BANK : (h + 1) * BANK], window.indirect(listed(h * BANK, BANK)))
             for a in range(PASSES):
                 v_scales[a] = gathered[SCALE_ROWS * a : P, :]
 
@@ -148,6 +155,9 @@ def tile_list_tabres_silu_kernel(tc, tab_words, tab_scales, w, rT, b, offs, out)
         def woven_by_rows(values):
             return values.rearrange("p (c i t) -> p c t i", i=RUN, t=PACK)
 
+        def columns(rows, n):
+            return rows[:, :, n * P : (n + 1) * P]
+
         def new_parts(a, piece):
             parts[a, piece] = new_tile([P, 2, len(piece) * WIDE], BF16, "parts%d_%d" % (a, piece[0]))
             return parts[a, piece]
@@ -155,32 +165,18 @@ def tile_list_tabres_silu_kernel(tc, tab_words, tab_scales, w, rT, b, offs, out)
         def mask_bits(target, values, mask):
             nc.vector.tensor_scalar(target.bitcast(I32), values.bitcast(I32), mask, None, ALU.bitwise_and)
 
-        def weave(a, piece):
-            woven = new_tile([P, len(piece) * WIDE], F32, "woven%d_%d" % (a, piece[0]))
-            nc.scalar.copy(woven_by_rows(woven[:]), by_rows(weight[a, piece]))
-            return woven
-
-        def quantise(a, piece, which=(HI, LO)):
-            places = [(a, c, part) for part in which for c in piece]
-            name = "%d_%d_%d" % (a, piece[0], which[-1])
+        def quantise_values(values, places, name):
             words = new_tile([P, P * len(places)], U32, "words" + name)
             scales = new_tile([P, P * len(places)], U8, "scales" + name)
-            values = parts[a, piece][:, which[0] : which[-1] + 1, :].rearrange("p s x -> p (s x)")
             nc.vector.quantize_mx(out=words[:].bitcast(FP8X4), scales=scales[:], in_=values)
             for n, place in enumerate(places):
                 operand[place] = (words[:, n * P : (n + 1) * P], scales[:, n * P : (n + 1) * P])
+            return scales
 
-        def split_on_vector(a, piece):
-            both = new_parts(a, piece)
-            rows = [weight[a, piece][:, :, n * P : (n + 1) * P] for n in range(len(piece))]
-            high = [new_tile([P, PACK, P], F32, "high%d_%d" % (a, c)) for c in piece]
-            hi, lo = ([both[:, part, n * WIDE : (n + 1) * WIDE] for n in range(len(piece))] for part in (HI, LO))
-            for n in range(len(piece)):
-                mask_bits(high[n][:], rows[n], WORD_MASK)
-            nc.scalar.copy(woven_by_rows(hi[0]), by_rows(high[0][:]))
-            nc.vector.tensor_tensor(woven_by_rows(lo[0]), by_rows(rows[0]), by_rows(high[0][:]), ALU.subtract)
-            nc.vector.tensor_copy(woven_by_rows(hi[1]), by_rows(high[1][:]))
-            nc.vector.tensor_tensor(woven_by_rows(lo[1]), by_rows(rows[1]), by_rows(high[1][:]), ALU.subtract)
+        def quantise(a, piece, which=(HI, LO)):
+            values = parts[a, piece][:, which[0] : which[-1] + 1, :].rearrange("p s x -> p (s x)")
+            places = [(a, c, part) for part in which for c in piece]
+            quantise_values(values, places, "%d_%d_%d" % (a, piece[0], which[-1]))
 
         def copy_upper(a, piece):
             upper = new_tile([P, len(piece) * WIDE], BF16, "upper%d_%d" % (a, piece[0]))
@@ -188,41 +184,35 @@ def tile_list_tabres_silu_kernel(tc, tab_words, tab_scales, w, rT, b, offs, out)
             nc.scalar.copy(woven_by_rows(upper[:]), halves[:, :, :, :, 1])
             return upper
 
-        def subtract_by_pairs(a, piece, hi, lo):
+        def subtract_from_rows(a, piece, hi, lo):
             nc.gpsimd.tensor_tensor(woven_by_rows(lo), by_rows(weight[a, piece]), woven_by_rows(hi), ALU.subtract)
 
-        def quantise_units(values, places, name):
-            words = new_tile([P, P * len(places)], U32, "words_" + name)
-            scales = new_tile([P, P * len(places)], U8, "scales_" + name)
-            planes[name] = scales
-            nc.vector.quantize_mx(out=words[:].bitcast(FP8X4), scales=scales[:], in_=values)
-            for n, place in enumerate(places):
-                operand[place] = (words[:, n * P : (n + 1) * P], scales[:, n * P : (n + 1) * P])
-
-        def split_beside_gather(a, piece, upper):
+        def split_from_rows(a, piece, upper):
             both = new_parts(a, piece)
             mask_bits(both[:, HI, :], upper[:], PAIR_MASK)
-            if piece == FIRST:
-                subtract_by_pairs(a, piece, both[:, HI, :], both[:, LO, :])
-                return
-            nc.gpsimd.tensor_tensor(both[:, LO, :], weave(a, piece)[:], both[:, HI, :], ALU.subtract)
+            subtract_from_rows(a, piece, both[:, HI, :], both[:, LO, :])
 
-        def subtract_on_tensor(a, piece, between):
+        def split_woven(a, piece, upper):
+            both = new_parts(a, piece)
+            mask_bits(both[:, HI, :], upper[:], PAIR_MASK)
+            woven = new_tile([P, len(piece) * WIDE], F32, "woven%d_%d" % (a, piece[0]))
+            nc.scalar.copy(woven_by_rows(woven[:]), by_rows(weight[a, piece]))
+            nc.gpsimd.tensor_tensor(both[:, LO, :], woven[:], both[:, HI, :], ALU.subtract)
+
+        def negate_high(a, piece):
             negated = new_tile([P, PACK, len(piece) * P], F32, "negated")
             nc.vector.tensor_scalar(
                 negated[:].bitcast(I32), weight[a, piece].bitcast(I32), WORD_MASK, SIGN_BIT, ALU.bitwise_and, ALU.bitwise_xor
             )
-            banks = []
-            for m in range(len(piece)):
-                if m:
-                    between()
-                cols = slice(m * P, (m + 1) * P)
-                banks.append(psum.tile([P, BANK], F32, name="transposed%d" % m, tag="turn%d" % m))
-                for t in range(PACK):
-                    block = banks[m][:, t * P : (t + 1) * P]
-                    nc.tensor.matmul(block, weight[a, piece][:, t, cols], identity[:], start=True, stop=False, is_transpose=True)
-                    nc.tensor.matmul(block, negated[:, t, cols], identity[:], start=False, stop=True, is_transpose=True)
-            return negated, banks
+            return negated
+
+        def subtract_on_tensor(a, piece, negated, m):
+            bank = psum.tile([P, BANK], F32, name="transposed%d" % m, tag="turn%d" % m)
+            for t in range(PACK):
+                block = bank[:, t * P : (t + 1) * P]
+                nc.tensor.matmul(block, columns(weight[a, piece], m)[:, t, :], identity[:], start=True, stop=False, is_transpose=True)
+                nc.tensor.matmul(block, columns(negated[:], m)[:, t, :], identity[:], start=False, stop=True, is_transpose=True)
+            return bank
 
         def collect_from_tensor(a, piece, negated, banks):
             turned = new_tile([P, len(piece) * WIDE], BF16, "turned")
@@ -257,6 +247,10 @@ def tile_list_tabres_silu_kernel(tc, tab_words, tab_scales, w, rT, b, offs, out)
                     stop=(a == (1 if c == LATE_TILE else PASSES - 1) and part == LO),
                 )
 
+        def multiply_tile(a, c):
+            for h in range(HALVES):
+                multiply(a, c, h)
+
         def multiply_first_tiles(a):
             for h in range(HALVES):
                 for c in FIRST:
@@ -279,68 +273,69 @@ def tile_list_tabres_silu_kernel(tc, tab_words, tab_scales, w, rT, b, offs, out)
                 nc.sync.dma_start(out[c * P : (c + 1) * P, first:done], res[:, first:done])
 
         both = new_parts(0, FIRST)
-        rows = [weight[0, FIRST][:, :, n * P : (n + 1) * P] for n in FIRST]
+        rows = [columns(weight[0, FIRST], n) for n in FIRST]
         high = [new_tile([P, PACK, P], F32, "high0_%d" % c) for c in FIRST]
         hi, lo = ([both[:, part, n * WIDE : (n + 1) * WIDE] for n in FIRST] for part in (HI, LO))
         for n in FIRST:
             mask_bits(high[n][:], rows[n], WORD_MASK)
             nc.scalar.copy(woven_by_rows(hi[n]), by_rows(high[n][:]))
         nc.vector.tensor_tensor(woven_by_rows(lo[0]), by_rows(rows[0]), by_rows(high[0][:]), ALU.subtract)
-        both_high = new_tile([P, len(SECOND), PACK, P], F32, "second_high")
-        second_high = [both_high[:, n] for n in range(len(SECOND))]
+        second_high = new_tile([P, len(SECOND), PACK, P], F32, "second_high")
         for n in range(len(SECOND)):
-            mask_bits(second_high[n][:], weight[0, SECOND][:, :, n * P : (n + 1) * P], WORD_MASK)
+            mask_bits(second_high[:, n], columns(weight[0, SECOND], n), WORD_MASK)
         nc.vector.tensor_tensor(woven_by_rows(lo[1]), by_rows(rows[1]), woven_by_rows(hi[1]), ALU.subtract)
         second_hi = new_tile([P, len(SECOND) * WIDE], BF16, "second_hi")
         for n in range(len(SECOND)):
-            nc.scalar.copy(woven_by_rows(second_hi[:, n * WIDE : (n + 1) * WIDE]), by_rows(second_high[n][:]))
+            nc.scalar.copy(woven_by_rows(second_hi[:, n * WIDE : (n + 1) * WIDE]), by_rows(second_high[:, n]))
         quantise(0, FIRST, (HI,))
         quantise(0, FIRST, (LO,))
-        quantise_units(second_hi[:], [(0, c, HI) for c in SECOND], "second_hi")
+        second_plane = quantise_values(second_hi[:], [(0, c, HI) for c in SECOND], "_second_hi")
         second_lo = new_tile([P, len(SECOND) * WIDE], BF16, "second_lo")
-        subtract_by_pairs(0, SECOND, second_hi[:], second_lo[:])
+        subtract_from_rows(0, SECOND, second_hi[:], second_lo[:])
         gather_words(0, 1)
-        quantise_units(second_lo[:], [(0, c, LO) for c in SECOND], "second_lo")
+        quantise_values(second_lo[:], [(0, c, LO) for c in SECOND], "_second_lo")
 
-        split_beside_gather(1, FIRST, copy_upper(1, FIRST))
-        idle = psum.tile([P, BANK], F32, name="idle", tag=SUM_BANK[EARLY_SUM])
-        words, plane = operand[0, 2, HI]
-        for n in range(8):
+        split_from_rows(1, FIRST, copy_upper(1, FIRST))
+
+        idle = psum.tile([P, BANK], F32, name="idle", tag=SUM_BANK[EARLY_TILE, 0])
+        words, plane = operand[0, SECOND[0], HI]
+        for n in range(WARM_UP):
             nc.tensor.matmul_mx(
                 out=idle[:, : BANK // 2],
                 lhsT=words.bitcast(FP8X4),
                 lhsT_scale=plane,
                 rhs=v_words[0][:, : BANK // 2].bitcast(FP8X4),
-                rhs_scale=planes["second_hi"][:, : BANK // 2],
+                rhs_scale=second_plane[:, : BANK // 2],
                 start=True,
                 stop=True,
             )
         gather_scales()
         multiply_first_tiles(0)
-        on_tensor = subtract_on_tensor(1, SECOND, lambda: [multiply(0, 2, h) for h in range(HALVES)])
+
+        negated = negate_high(1, SECOND)
+        banks = [subtract_on_tensor(1, SECOND, negated, 0)]
+        multiply_tile(0, EARLY_TILE)
+        banks.append(subtract_on_tensor(1, SECOND, negated, 1))
 
         upper = copy_upper(2, FIRST)
         quantise(1, FIRST)
-        split_beside_gather(2, FIRST, upper)
+        split_from_rows(2, FIRST, upper)
         gather_words(1, 1)
-        for h in range(HALVES):
-            multiply(1, 0, h)
-        upper = copy_upper(2, SECOND)
-        split_beside_gather(2, SECOND, upper)
+        multiply_tile(1, 0)
+        split_woven(2, SECOND, copy_upper(2, SECOND))
         quantise(2, FIRST)
-        collect_from_tensor(1, SECOND, *on_tensor)
+        collect_from_tensor(1, SECOND, negated, banks)
 
         gather_words(2, HALVES)
         multiply_first_tiles(2)
-        for h in range(HALVES):
-            multiply(1, LATE_TILE, h)
+        multiply_tile(1, LATE_TILE)
         for c in FIRST:
             activate(c)
         quantise(2, SECOND)
         quantise(1, SECOND)
         for c in SECOND:
             for h in range(HALVES):
-                for a in range(1 if c == 2 else 0, PASSES):
+                for a in range(1 if c == EARLY_TILE else 0, PASSES):
                     multiply(a, c, h)
             activate(c)
 

from contextlib import ExitStack

import concourse.mybir as mybir
from concourse.masks import make_identity

K, M, T, S = 1536, 512, 2048, 1024
FLOPS = 2 * 2 * K * M * S

F32 = mybir.dt.float32
BF16 = mybir.dt.bfloat16
I32 = mybir.dt.int32
U32 = mybir.dt.uint32
U16 = mybir.dt.uint16
U8 = mybir.dt.uint8
FP8X4 = mybir.dt.float8_e4m3fn_x4
ALU = mybir.AluOpType
SILU = mybir.ActivationFunctionType.Silu
COPY = mybir.ActivationFunctionType.Copy

P = 128
PACK = 4
PASSES = K // (P * PACK)
TILES = M // P
BANK = 512
HALVES = S // BANK
GROUP = 16
QUADRANT = 32
SCALE_ROWS = 4
WORD_BYTES = 4
WIDE = PACK * P
RUN = 2
ALIGN = 256
PAIR_MASK = 0xFFF0FFF0 - (1 << 32)
WORD_MASK = 0xFFF00000 - (1 << 32)
SIGN_BIT = -(1 << 31)
FIRST, SECOND, ALL = (0, 1), (2, 3), (0, 1, 2, 3)
HI, LO = 0, 1
WARM_UP = 4

PART = len(FIRST) * WIDE * 2
SHARED = {
    "woven2_2": 0,
    "upper2_0": 2 * PART - ALIGN,
    "upper2_2": 3 * PART - 2 * ALIGN,
    "turned": 2 * PART,
    "parts1_2": 3 * PART,
    "parts0_0": 6 * PART,
    "second_lo": 6 * PART,
    "table1": 8 * PART,
    "words2_0_1": 8 * PART,
}

SUM_BANK = {
    (0, 0): "sum0", (0, 1): "sum1", (1, 0): "sum2", (1, 1): "sum3",
    (2, 0): "early", (2, 1): "early1", (3, 0): "sum0", (3, 1): "sum1",
}
EARLY_TILE = 2
LATE_TILE = 1


def tile_list_tabres_silu_kernel(tc, tab_words, tab_scales, w, rT, b, offs, out):
    nc = tc.nc
    with ExitStack() as ctx:
        keep = ctx.enter_context(tc.tile_pool(name="keep", bufs=1))
        psum = ctx.enter_context(tc.psum_pool(name="psum", bufs=1))
        overlaid = ctx.enter_context(tc.tile_pool(name="overlaid", bufs=1))

        def new_tile(shape, dtype, name):
            if name in SHARED:
                return overlaid.tile(shape, dtype, name=name, align_bytes=ALIGN, offset=SHARED[name])
            return keep.tile(shape, dtype, name=name, align_bytes=ALIGN)

        offsets = keep.tile([P, S // GROUP], U16, name="offsets")

        scale_rows = new_tile([P, T // WORD_BYTES], I32, "scale_rows")
        nc.vector.memset(scale_rows[:], 0)

        identity = new_tile([P, P], F32, "identity")
        make_identity(nc, identity[:])

        bias_rows = new_tile([P, P], F32, "bias_rows")
        zeros = new_tile([P, P], F32, "zeros")
        nc.vector.memset(zeros[:], 0.0)
        nc.scalar.activation(bias_rows[:], zeros[:], SILU)

        table, weight, resid = {}, {}, {}

        def load_table(a):
            table[a] = new_tile([P, T], I32, "table%d" % a)
            nc.sync.dma_start(table[a][:], tab_words[a].rearrange("p t i -> p (t i)").bitcast(I32))

        def load_weight(a, tiles):
            whole = new_tile([P, PACK, len(tiles) * P], F32, "weight%d_%d" % (a, tiles[0]))
            rows = w[a * P * PACK : (a + 1) * P * PACK, tiles[0] * P : (tiles[-1] + 1) * P]
            nc.sync.dma_start(whole[:], rows.rearrange("(p t) n -> p t n", t=PACK))
            for piece in (FIRST, SECOND):
                if piece[0] in tiles:
                    start = (piece[0] - tiles[0]) * P
                    weight[a, piece] = whole[:, :, start : start + len(piece) * P]

        def load_resid(c):
            resid[c] = new_tile([P, T], F32, "resid%d" % c)
            nc.sync.dma_start(resid[c][:], rT[c * P : (c + 1) * P, :])

        def load_scale_rows():
            for q in range(P // QUADRANT):
                rows = scale_rows[QUADRANT * q : QUADRANT * q + SCALE_ROWS * PASSES, :]
                nc.sync.dma_start(rows, tab_scales[:, SCALE_ROWS * q : SCALE_ROWS * (q + 1), :].bitcast(I32))

        bias = keep.tile([P, TILES], F32, name="bias")

        def load_bias():
            nc.sync.dma_start(bias_rows[:TILES, :], b.rearrange("(c p) -> c p", p=P))
            turned_bias = psum.tile([P, BANK], F32, name="turned_bias", tag=SUM_BANK[EARLY_TILE, 0])
            nc.tensor.transpose(turned_bias[:, :P], bias_rows[:], identity[:])
            nc.scalar.copy(bias[:], turned_bias[:, :TILES])

        load_weight(0, FIRST)
        load_weight(0, SECOND)
        nc.sync.dma_start(offsets[:], offs)
        load_table(0)
        load_bias()
        load_weight(1, FIRST)
        load_scale_rows()
        load_weight(1, SECOND)
        load_weight(2, ALL)
        load_table(1)
        load_table(2)
        for c in range(TILES):
            load_resid(c)

        v_words, v_scales, parts, operand, acc, act = {}, {}, {}, {}, {}, {}

        def listed(first, width):
            return offsets[:, first // GROUP : (first + width) // GROUP]

        def gather_words(a, cuts):
            v_words[a] = new_tile([P, S], U32, "v_words%d" % a)
            width = S // cuts
            for n in range(cuts):
                window = table[a][:].bitcast(U32)
                nc.vector.tensor_copy(v_words[a][:, n * width : (n + 1) * width], window.indirect(listed(n * width, width)))

        def gather_scales():
            gathered = new_tile([P, S], U8, "v_scales")
            window = scale_rows[:].bitcast(U8)
            for h in range(HALVES):
                nc.vector.tensor_copy(gathered[:, h * BANK : (h + 1) * BANK], window.indirect(listed(h * BANK, BANK)))
            for a in range(PASSES):
                v_scales[a] = gathered[SCALE_ROWS * a : P, :]

        def by_rows(rows):
            return rows.rearrange("p t (c i) -> p c t i", i=RUN)

        def woven_by_rows(values):
            return values.rearrange("p (c i t) -> p c t i", i=RUN, t=PACK)

        def columns(rows, n):
            return rows[:, :, n * P : (n + 1) * P]

        def new_parts(a, piece):
            parts[a, piece] = new_tile([P, 2, len(piece) * WIDE], BF16, "parts%d_%d" % (a, piece[0]))
            return parts[a, piece]

        def mask_bits(target, values, mask):
            nc.vector.tensor_scalar(target.bitcast(I32), values.bitcast(I32), mask, None, ALU.bitwise_and)

        def quantise_values(values, places, name):
            words = new_tile([P, P * len(places)], U32, "words" + name)
            scales = new_tile([P, P * len(places)], U8, "scales" + name)
            nc.vector.quantize_mx(out=words[:].bitcast(FP8X4), scales=scales[:], in_=values)
            for n, place in enumerate(places):
                operand[place] = (words[:, n * P : (n + 1) * P], scales[:, n * P : (n + 1) * P])
            return scales

        def quantise(a, piece, which=(HI, LO)):
            values = parts[a, piece][:, which[0] : which[-1] + 1, :].rearrange("p s x -> p (s x)")
            places = [(a, c, part) for part in which for c in piece]
            quantise_values(values, places, "%d_%d_%d" % (a, piece[0], which[-1]))

        def copy_upper(a, piece):
            upper = new_tile([P, len(piece) * WIDE], BF16, "upper%d_%d" % (a, piece[0]))
            halves = weight[a, piece].bitcast(BF16).rearrange("p t (c i h) -> p c t i h", i=RUN, h=2)
            nc.scalar.copy(woven_by_rows(upper[:]), halves[:, :, :, :, 1])
            return upper

        def subtract_from_rows(a, piece, hi, lo):
            nc.gpsimd.tensor_tensor(woven_by_rows(lo), by_rows(weight[a, piece]), woven_by_rows(hi), ALU.subtract)

        def split_from_rows(a, piece, upper):
            both = new_parts(a, piece)
            mask_bits(both[:, HI, :], upper[:], PAIR_MASK)
            subtract_from_rows(a, piece, both[:, HI, :], both[:, LO, :])

        def split_woven(a, piece, upper):
            both = new_parts(a, piece)
            mask_bits(both[:, HI, :], upper[:], PAIR_MASK)
            woven = new_tile([P, len(piece) * WIDE], F32, "woven%d_%d" % (a, piece[0]))
            nc.scalar.copy(woven_by_rows(woven[:]), by_rows(weight[a, piece]))
            nc.gpsimd.tensor_tensor(both[:, LO, :], woven[:], both[:, HI, :], ALU.subtract)

        def negate_high(a, piece):
            negated = new_tile([P, PACK, len(piece) * P], F32, "negated")
            nc.vector.tensor_scalar(
                negated[:].bitcast(I32), weight[a, piece].bitcast(I32), WORD_MASK, SIGN_BIT, ALU.bitwise_and, ALU.bitwise_xor
            )
            return negated

        def subtract_on_tensor(a, piece, negated, m):
            bank = psum.tile([P, BANK], F32, name="transposed%d" % m, tag="turn%d" % m)
            for t in range(PACK):
                block = bank[:, t * P : (t + 1) * P]
                nc.tensor.matmul(block, columns(weight[a, piece], m)[:, t, :], identity[:], start=True, stop=False, is_transpose=True)
                nc.tensor.matmul(block, columns(negated[:], m)[:, t, :], identity[:], start=False, stop=True, is_transpose=True)
            return bank

        def collect_from_tensor(a, piece, negated, banks):
            turned = new_tile([P, len(piece) * WIDE], BF16, "turned")
            for m in range(len(piece)):
                nc.scalar.copy(
                    turned[:, m * WIDE : (m + 1) * WIDE].rearrange("n (u p e) -> n u p e", u=2, e=2),
                    banks[m][:].rearrange("n (u e p) -> n u p e", u=2, e=2),
                )
            returned = psum.tile([P, BANK], F32, name="returned", tag="turn0")
            pairs = turned[:].bitcast(F32)
            for j in range(2 * len(piece)):
                nc.tensor.transpose(returned[:, j * P : (j + 1) * P], pairs[:, j * P : (j + 1) * P], identity[:])
            both = new_parts(a, piece)
            nc.scalar.activation(woven_by_rows(both[:, HI, :]), by_rows(negated[:]), COPY, scale=-1.0)
            nc.scalar.copy(
                both[:, LO, :].bitcast(F32).rearrange("p (m n u) -> p m n u", m=len(piece), u=2),
                returned[:].rearrange("p (m u n) -> p m n u", m=len(piece), u=2),
            )

        def multiply(a, c, h):
            if a == 0:
                acc[c, h] = psum.tile([P, BANK], F32, name="acc%d_%d" % (c, h), tag=SUM_BANK[c, h])
            for part in (HI, LO):
                words, plane = operand[a, c, part]
                nc.tensor.matmul_mx(
                    out=acc[c, h][:],
                    lhsT=words.bitcast(FP8X4),
                    lhsT_scale=plane,
                    rhs=v_words[a][:, h * BANK : (h + 1) * BANK].bitcast(FP8X4),
                    rhs_scale=v_scales[a][:, h * BANK : (h + 1) * BANK],
                    start=(a == 0 and part == HI),
                    stop=(a == (1 if c == LATE_TILE else PASSES - 1) and part == LO),
                )

        def multiply_tile(a, c):
            for h in range(HALVES):
                multiply(a, c, h)

        def multiply_first_tiles(a):
            for h in range(HALVES):
                for c in FIRST:
                    multiply(a, c, h)

        def activate(c):
            act[c] = new_tile([P, S], F32, "act%d" % c)
            for h in range(HALVES):
                nc.scalar.activation(act[c][:, h * BANK : (h + 1) * BANK], acc[c, h][:], SILU, bias=bias[:, c : c + 1])

        def finish(c, stores):
            res = new_tile([P, S], F32, "res%d" % c)
            done = 0
            for widths in stores:
                first = done
                for width in widths:
                    cols = slice(done, done + width)
                    nc.vector.tensor_tensor(res[:, cols], resid[c][:].indirect(listed(done, width)), act[c][:, cols], ALU.add)
                    done += width
                nc.sync.dma_start(out[c * P : (c + 1) * P, first:done], res[:, first:done])

        both = new_parts(0, FIRST)
        rows = [columns(weight[0, FIRST], n) for n in FIRST]
        high = [new_tile([P, PACK, P], F32, "high0_%d" % c) for c in FIRST]
        hi, lo = ([both[:, part, n * WIDE : (n + 1) * WIDE] for n in FIRST] for part in (HI, LO))
        for n in FIRST:
            mask_bits(high[n][:], rows[n], WORD_MASK)
            nc.scalar.copy(woven_by_rows(hi[n]), by_rows(high[n][:]))
        nc.vector.tensor_tensor(woven_by_rows(lo[0]), by_rows(rows[0]), by_rows(high[0][:]), ALU.subtract)
        second_high = new_tile([P, len(SECOND), PACK, P], F32, "second_high")
        for n in range(len(SECOND)):
            mask_bits(second_high[:, n], columns(weight[0, SECOND], n), WORD_MASK)
        nc.vector.tensor_tensor(woven_by_rows(lo[1]), by_rows(rows[1]), woven_by_rows(hi[1]), ALU.subtract)
        second_hi = new_tile([P, len(SECOND) * WIDE], BF16, "second_hi")
        for n in range(len(SECOND)):
            nc.scalar.copy(woven_by_rows(second_hi[:, n * WIDE : (n + 1) * WIDE]), by_rows(second_high[:, n]))
        quantise(0, FIRST, (HI,))
        quantise(0, FIRST, (LO,))
        second_plane = quantise_values(second_hi[:], [(0, c, HI) for c in SECOND], "_second_hi")
        second_lo = new_tile([P, len(SECOND) * WIDE], BF16, "second_lo")
        subtract_from_rows(0, SECOND, second_hi[:], second_lo[:])
        gather_words(0, 1)
        quantise_values(second_lo[:], [(0, c, LO) for c in SECOND], "_second_lo")

        split_from_rows(1, FIRST, copy_upper(1, FIRST))

        idle = psum.tile([P, BANK], F32, name="idle", tag=SUM_BANK[EARLY_TILE, 0])
        words, plane = operand[0, SECOND[0], HI]
        for n in range(WARM_UP):
            nc.tensor.matmul_mx(
                out=idle[:, : BANK // 2],
                lhsT=words.bitcast(FP8X4),
                lhsT_scale=plane,
                rhs=v_words[0][:, : BANK // 2].bitcast(FP8X4),
                rhs_scale=second_plane[:, : BANK // 2],
                start=True,
                stop=True,
            )
        gather_scales()
        multiply_first_tiles(0)

        negated = negate_high(1, SECOND)
        banks = [subtract_on_tensor(1, SECOND, negated, 0)]
        multiply_tile(0, EARLY_TILE)
        banks.append(subtract_on_tensor(1, SECOND, negated, 1))

        upper = copy_upper(2, FIRST)
        quantise(1, FIRST)
        split_from_rows(2, FIRST, upper)
        gather_words(1, 1)
        multiply_tile(1, 0)
        split_woven(2, SECOND, copy_upper(2, SECOND))
        quantise(2, FIRST)
        collect_from_tensor(1, SECOND, negated, banks)

        gather_words(2, HALVES)
        multiply_first_tiles(2)
        multiply_tile(1, LATE_TILE)
        for c in FIRST:
            activate(c)
        quantise(2, SECOND)
        quantise(1, SECOND)
        for c in SECOND:
            for h in range(HALVES):
                for a in range(1 if c == EARLY_TILE else 0, PASSES):
                    multiply(a, c, h)
            activate(c)

        finish(0, [(BANK, BANK)])
        finish(1, [(S,)])
        finish(2, [(S,)])
        finish(3, [(BANK,), (BANK // 2,), (BANK // 2,)])
